import numpy as np, ml_dtypes
CORES = [16,18,20,22]
N = 4
BF = ml_dtypes.bfloat16
def gentries(a):
    return np.ascontiguousarray(a.reshape(8, 16, -1).transpose(0, 2, 1)).reshape(8, -1)
def gtable(e):
    e = np.asarray(e); return np.ascontiguousarray(e.reshape(8, -1, 16).transpose(0, 2, 1)).reshape(128, -1).astype(np.int32)
B0, S, RO, DA = 2048, 256, 4, 1024
TS, TE, TC = 12, 9, 12
JUMPS = [1, 2, 3, 1]
W = B0 + RO * S
QC = 0.35
def parts(rng):
    x = rng.integers(0, 256, (N, 8, 16, B0)); x = np.where(rng.random((N, 8, 1, B0)) < 0.02, x >> 4, x)
    par = (np.arange(B0) - 1 - rng.integers(0, B0 >> 4, (N, 8, B0))) % B0
    p = np.zeros((N, 8, 16, B0), np.int64); p[:, :, 0] = np.arange(B0)
    for k in range(1, 16): p[:, :, k] = np.take_along_axis(par, p[:, :, k - 1], 2)
    v = rng.integers(0, B0, (N, 8, S))
    near = np.take_along_axis(v, rng.integers(0, S, (N, 8, B0)), 2)
    c = np.where(rng.random((N, 8, B0)) < 0.5, near, rng.integers(0, B0, (N, 8, B0)))
    c = np.where(rng.random((N, 8, B0)) < QC, c, -1)
    return x, p, c, rng.integers(0, 256, (N, 8, 16, DA)), rng.integers(0, 4096, (N, 8, 16, 16)), v
def pack(x, p, c, d, w, v):
    return {"lab": np.ascontiguousarray(x.reshape(N, 128, B0)).astype(np.float32).astype(BF), "pth": np.ascontiguousarray(p.reshape(N, 128, B0)).astype(np.int32),
            "cov": np.ascontiguousarray(c).astype(np.int32), "act": np.ascontiguousarray(d.reshape(N, 128, DA)).astype(np.float32).astype(BF),
            "wts": np.ascontiguousarray(w.reshape(N, 128, 16)).astype(np.int32), "leaf": np.stack([gtable(a) for a in v])}
def setup_inputs(rng):
    return pack(*parts(rng))
def setup_inputs_spread(rng):
    x, p, c, d, w, v = parts(rng)
    x = np.where(rng.random((N, 8, 1, B0)) < 0.03, (256 * np.exp2(-7 * rng.random((N, 8, 1, B0))) * rng.random(x.shape)).astype(np.int64), x)
    d = (256 * np.exp2(-7 * rng.random((N, 8, 1, DA))) * rng.random(d.shape)).astype(np.int64)
    w = np.exp2(12 * rng.random(w.shape)).astype(np.int64) - 1
    p = np.where(rng.random((N, 8, 1, B0)) < 0.5, rng.integers(0, B0, p.shape), p)
    c = np.where(rng.random(c.shape) < 0.5, c, -1)
    v = (B0 * rng.random(v.shape) ** 3).astype(np.int64)
    return pack(x, p, c, d, w, v)
def setup_inputs_ends(rng):
    x = 255 * (rng.random((N, 8, 16, B0)) < 0.75).astype(np.int64); k = rng.random((N, 8, 1, B0))
    x = np.where(k < 0.01, 0, np.where(k > 0.95, 255, x))
    x[:, 1::2, :, B0 - 1] = 255; x[:, ::2, :, B0 - 1] = 0; x[:, :, :, 2:4] = 255
    d = 255 * (rng.random((N, 8, 16, DA)) < 0.85).astype(np.int64); d[..., 16] = 0; d[..., 0] = 255; d[..., DA - 1] = 255
    w = 4095 * rng.integers(0, 2, (N, 8, 16, 16)); w[..., 15] = 4095; w[..., 2] = 0; w[:, 1::2, :, 0] = 4095
    p = (B0 - 1) * rng.integers(0, 2, (N, 8, 16, B0)); p = np.where(rng.random(p.shape) < 0.28, rng.integers(0, B0, p.shape), p)
    c = np.where(rng.random((N, 8, B0)) < 0.06, B0 - 1, -1); c[:, :, 0] = -1; c[:, :, B0 - 1] = -1; c[:, 5, B0 - 1] = B0 - 1
    v = (B0 - 1) * rng.integers(0, 2, (N, 8, S)); v = np.where(rng.random(v.shape) < 0.3, rng.integers(0, B0, v.shape), v)
    return pack(x, p, c, d, w, v)
def setup_inputs_corners(rng):
    x, p, c, d, w, v = parts(rng); a = np.arange(B0); h = B0 >> 1
    for r in range(N):
        for g in range(8):
            k = (g + r) % 8
            if k == 0: p[r, g] = a
            elif k == 1:
                p[r, g] = np.where(((np.arange(16)[:, None] + a) & 1) == 0, 0, B0 - 1); c[r, g, 0] = -1; c[r, g, B0 - 1] = -1
                v[r, g] = np.where(rng.random(S) < 0.5, v[r, g], (B0 - 1) * rng.integers(0, 2, S))
            elif k == 2: w[r, g] = 0
            elif k == 3:
                c[r, g] = np.where(a >= h, a, -1); p[r, g, :, :h] = p[r, g, :, :h] % h
            elif k == 4:
                x[r, g] = np.where(rng.random((1, B0)) < 0.9, 100, x[r, g]); d[r, g] = np.where(rng.random((1, DA)) < 0.5, 0, d[r, g])
                c[r, g] = np.where(rng.random(B0) < 0.02, rng.integers(0, B0, B0), -1)
            elif k == 5:
                w[r, g] = 4095 * np.eye(16, dtype=np.int64)
                x[r, g] = rng.choice(np.array([0, 1, 2, 255]), (16, B0)); d[r, g] = rng.choice(np.array([0, 1, 255]), (16, DA))
                c[r, g] = np.where(rng.random(B0) < 0.03, c[r, g], -1)
            elif k == 6:
                o = int(rng.integers(0, B0)); v[r, g] = o; c[r, g, p[r, g, :, o]] = -1
            else:
                z = 16 - TS + rng.integers(0, 2, (1, B0)); z[:, B0 - 16:] = 0
                x[r, g] = 100 - (np.argsort(rng.random((16, B0)), axis=0) < z)
                c[r, g] = np.where(rng.random(B0) < 0.05, B0 - 1 - rng.integers(0, 16, B0), -1); c[r, g, B0 - 16:] = -1
    return pack(x, p, c, d, w, v)
def setup_inputs_crowd(rng):
    x, p, c, d, w, v = parts(rng); c[:] = -1
    for r in range(N):
        for g in range(8):
            k = (g + r) % 4; o = rng.permutation(B0)[:S + 4]; y, z, q, b = [int(e) for e in o[:4]]; v[r, g] = o[4:]
            p[r, g] = np.where((p[r, g] == y) | (p[r, g] == z) | (p[r, g] == b), q, p[r, g])
            x[r, g, :, z] = 0; x[r, g, :, b] = 0; c[r, g, y] = z; hit = np.zeros(S, bool)
            if k < 2: hit[:] = True
            if k == 0:
                i = int(rng.integers(0, S)); hit[i] = False
                h = 128 * int(np.sum(w[r, g, :, 0])) & 4095; n = TC + (rng.random(B0) < 0.25).astype(np.int64); n[(h * B0) >> 12] = TC
                low = np.argsort(rng.random((16, B0)), axis=0) < n
                x[r, g] = np.where(low, rng.integers(0, 129, (16, B0)), rng.integers(129, 256, (16, B0)))
                x[r, g, :, z] = 0; x[r, g, :, b] = 0; x[r, g, :, int(v[r, g, i])] = 128; d[r, g, :, h & (DA - 1)] = 0
            if k == 3: hit[0] = True
            if k >= 2:
                t = p[r, g, ::2]; t[:, v[r, g]] = b
            p[r, g, 15, v[r, g][hit]] = y
    return pack(x, p, c, d, w, v)
def setup_inputs_brims(rng):
    x, p, c, d, w, v = parts(rng); turn = int(rng.integers(0, 4))
    for r in range(N):
        for g in range(8):
            k = (g + turn) % 4; t = x[r, g]; u = p[r, g]
            if k == 0:
                b = np.where(rng.random((16, B0)) < 0.85, 192, 64 * rng.integers(0, 4, (16, B0))); b[15] = 1
                t[:] = np.where(rng.random((1, B0)) < 0.75, b, t); t[:, [0, B0 - 1]] = 0
                w[r, g] = 64 * rng.integers(56, 64, (16, 16)); w[r, g, 15] = 4095 * ((np.arange(16) + int(rng.integers(0, 2))) & 1)
                e = np.where(rng.random((16, DA)) < 0.9, 0, 64 * rng.integers(0, 4, (16, DA))); e[15] = rng.integers(0, 2, DA); e[:, [0, DA - 1]] = 0
                d[r, g] = e; c[r, g] = -1
            elif k == 1:
                t[:] = np.where(rng.random((1, B0)) < 0.5, 255 - (rng.random((16, B0)) < 0.2).astype(np.int64), t)
                w[r, g] = 4095 - rng.integers(0, 6, (16, 16)); d[r, g] = d[r, g] * (rng.random((1, DA)) < 0.5); c[r, g] = -1
            elif k == 2:
                o = 1 + rng.permutation(B0 - 1)[:S + 10]; y, z = int(o[0]), int(o[1]); few = o[2:10]; v[r, g] = o[10:]
                m = rng.random(S) < 0.75; m[int(rng.integers(0, S))] = False; wait = v[r, g][m]; go = v[r, g][~m]; n = len(wait)
                u[:] = np.where((u == y) | (u == z), 0, u); u[0, wait] = rng.choice(few, n); u[15, wait] = y; u[:, go] = z
                c[r, g] = -1; c[r, g, y] = z
                t[:, 0] = 255; t[:, y] = 100; t[:, z] = 50; t[:, few] = rng.integers(0, 32, (16, 8))
                t[:, wait] = np.where(rng.random((1, n)) < 0.5, 255, t[:, wait])
                t[0, wait] = np.where(rng.random(n) < 0.5, rng.integers(240, 256, n), rng.integers(0, 240, n)); t[0, go] = 0
                w[r, g, :, :2] = 0; w[r, g, 0, :2] = 16
                d[r, g] = d[r, g] * (rng.random((1, DA)) < 0.3)
    return pack(x, p, c, d, w, v)
def check_inputs(d):
    bad = []
    for k, lo, hi in (("lab", 0, 255), ("pth", 0, B0 - 1), ("cov", -1, B0 - 1), ("act", 0, 255), ("wts", 0, 4095), ("leaf", 0, B0 - 1)):
        a = np.asarray(d[k]).astype(np.float64)
        if not (np.min(a) >= lo and np.max(a) <= hi and np.all(a == np.floor(a))): bad.append("range of " + k)
    return bad
def pick(t, ix):
    return np.take_along_axis(t, ix[:, :, None, :], 3)
def reference(lab, pth, cov, act, wts, leaf):
    x = np.full((N, 8, 16, W), 256, np.int32); x[..., :B0] = lab.astype(np.float32).astype(np.int32).reshape(N, 8, 16, B0)
    p = np.zeros((N, 8, 16, W), np.int64); p[..., :B0] = pth.reshape(N, 8, 16, B0)
    c = np.full((N, 8, W), -1, np.int64); c[..., :B0] = cov
    d = act.astype(np.float32).astype(np.int32).reshape(N, 8, 16, DA)
    w = wts.astype(np.int32).reshape(N, 8, 16, 16).transpose(0, 1, 3, 2)
    v = np.stack([gentries(a) for a in leaf]).astype(np.int64)
    for t in range(RO):
        B = B0 + t * S
        xv = pick(x, v); pv = pick(p, v)
        flat = pv.reshape(N, 8, 16 * S); xp = pick(x, flat).reshape(N, 8, 16, 16, S)
        cp = np.take_along_axis(c, flat, 2); xc = pick(x, np.maximum(cp, 0)).reshape(N, 8, 16, 16, S)
        holds = (cp.reshape(N, 8, 16, S) >= 0) & (np.sum(xp >= xc, axis=2) >= TS)
        susp = np.any(holds, axis=2); live = ~susp; cnt = np.sum(susp, axis=2)
        h = np.matmul(w, xv) & 4095
        xn = np.abs(xv - pick(d, h[:, :, 0] & (DA - 1)))
        q = (h[:, :, 1] * B) >> 12
        e = np.stack([np.take_along_axis(x[(r + JUMPS[t]) % N], q[r][:, None, :], 2) for r in range(N)])
        low = np.sum(xp >= e[:, :, :, None, :], axis=2) < TE
        want = np.any(low, axis=2) & live & (e[:, :, 0] < 256)
        tg = np.where(want, np.take_along_axis(pv, np.argmax(low, axis=2)[:, :, None, :], 2)[:, :, 0], -1)
        cand = ((np.matmul(w, xn) & 4095) * B) >> 12
        xk = pick(x, cand.reshape(N, 8, 16 * S)).reshape(N, 8, 16, 16, S)
        fit = np.sum(xn[:, :, :, None, :] >= xk, axis=2) >= (TC + (cnt & 1))[:, :, None, None]
        cn = np.where(np.any(fit, axis=2), np.take_along_axis(cand, np.argmax(fit, axis=2)[:, :, None, :], 2)[:, :, 0], -1)
        new = np.broadcast_to(B + np.arange(S), (N, 8, S))
        for r in range(N):
            for g in range(8):
                s = np.nonzero(tg[r, g] >= 0)[0]
                u, first = np.unique(tg[r, g][s], return_index=True); s = s[first]
                x[r, g][:, u] = np.maximum(x[r, g][:, u], e[r, g][:, s])
        x[..., B:B + S] = np.where(live[:, :, None, :], xn, 256)
        p[..., B:B + S] = np.where(live[:, :, None, :], np.concatenate([new[:, :, None, :], pv[:, :, :15]], axis=2), 0)
        c[..., B:B + S] = np.where(live, cn, -1)
        v = np.where(live, new, v)
    return {"yx": x.reshape(N, 128, W).astype(np.float32).astype(BF), "yp": np.ascontiguousarray(p[..., B0:]).reshape(N, 128, RO * S).astype(np.float32),
            "yc": np.ascontiguousarray(c[..., B0:]).astype(np.float32), "yv": np.stack([gtable(a) for a in v]).astype(np.float32)}

@@ -1,0 +1,614 @@
+from concourse.mybir import AluOpType, ActivationFunctionType
+
+A = AluOpType
+F = ActivationFunctionType
+B0, S, RO, W = 2048, 256, 4, 3072
+JUMPS = [1, 2, 3, 1]
+X0 = 64
+C0 = 98560.5
+bf, f32, i32, u16, f16 = "bfloat16", "float32", "int32", "uint16", "float16"
+SB = {
+    "X": ([X0 + W], bf), "X2": ([X0 + W - S], bf), "xr0": ([2048], bf), "xr1": ([2304], bf), "xr2": ([2560], bf), "xr3": ([2816], bf),
+    "TT": ([2816], f32), "pt": ([2048], i32), "ac": ([1024], bf), "cv": ([128], i32), "wt": ([16], i32), "lf": ([16], i32),
+    "O": ([4096], bf), "XK": ([4096], bf), "SG": ([4096], bf), "C": ([2816], bf), "YP": ([1024], f32), "YC": ([1024], f32),
+    "COV": ([192], u16), "PL": ([256], u16), "LU": ([16], u16), "LV": ([16], f32), "PV": ([256], f16),
+    "xv": ([256], bf), "av": ([256], bf), "z0": ([256], bf), "z1": ([256], bf), "E": ([512], bf), "EM": ([256], bf),
+    "tx": ([8, 32], f32), "hi": ([16, 2], i32), "ha": ([16], i32), "hq": ([16], i32), "LA": ([16], u16), "LQ": ([16], u16),
+    "ci": ([256], i32), "cj": ([256], i32), "CL": ([256], u16), "cs0": ([256], f16), "cs1": ([256], f16),
+    "F1": ([256], bf), "F2": ([256], bf), "OH": ([8, 32], bf), "lv0": ([8, 32], bf), "lv1": ([8, 32], bf), "M": ([8, 32], f16),
+    "LR": ([8, 32], f32), "NE": ([384], bf), "KP": ([384], bf), "RS": ([384], bf), "vt": ([16], f32), "vo": ([8], f32), "GL": ([16], u16),
+    "TL": ([16], u16), "NV": ([256], bf), "la": ([16], f32), "Y": ([256], bf), "yq": ([256], f32), "tp": ([256], f32),
+    "cn": ([4], f32), "pi": ([4], i32), "pj": ([4], i32), "pb": ([4], f32), "FS": ([256], bf), "O2": ([256], bf), "M2": ([256], f16),
+    "GQ": ([160], bf), "MQ": ([160], bf), "QQ": ([160], bf), "KEY": ([160], bf), "k1": ([160], bf), "k2": ([160], bf), "k3": ([160], bf),
+    "pc": ([4], i32), "pd": ([8], i32), "col": ([44], f32), "XC": ([512], bf), "SB2": ([128], bf), "IL": ([64], f32), "io16": ([16], f32), "IOT": ([256], bf), "SM": ([256], bf),
+    "I": ([160], bf), "NI": ([128], bf), "I128": ([128], bf), "NI64": ([128], bf), "BD": ([160], bf), "SBD": ([128], bf),
+    "BK": ([160], bf), "PK": ([160], bf), "U0": ([128], bf), "U1": ([128], bf), "U2": ([128], bf), "HB": ([128], bf),
+    "SH": ([128], bf), "TOP": ([128], bf), "LW": ([512], bf), "BS": ([320], bf), "IS": ([320], bf), "WS": ([640], bf),
+    "WB": ([320], bf), "G8": ([8], bf), "ZR": ([128], bf), "CM": ([16, 32], bf), "wh": ([32], i32), "wf": ([32], f32),
+    "wl": ([10], u16), "p1": ([16], u16), "p2": ([8], u16), "c16": ([128], f16), "tc": ([128], f32),
+}
+PS = ["A0", "A1", "CB", "P1", "P2", "M0", "M1", "M2b"]
+SCRATCH = {k: ("sbuf", [128] + v[0], v[1]) for k, v in SB.items()}
+SCRATCH.update({k: ("psum", [128, 16, 32], f32) for k in PS})
+NDMA = 20
+SEMAPHORES = ["v", "s", "p", "g"] + ["d%d" % i for i in range(NDMA)] + ["arr%d" % t for t in range(RO)] + ["snt%d" % t for t in range(RO)]
+CY, PCY, HOP, GA, SCA = 1.04, 0.52, 120.0, 1.55, 3.8
+RATE, LAT, PASSES = 200.0, 2000.0, 4500
+COPY = ["ssss", "vvsss", "vvsss", "vvssss"]
+MV = [8, 8, 8, 8]
+HS = [0, 0, 0, 0]
+HC = 1024
+ORDER = []
+CG = 512
+
+
+def build(g, T, rank, core, topo):
+    ops = []
+
+    def ref(name, lo=None, hi=None, step=1, parts=None):
+        sh = SB[name][0]
+        n = sh[0]
+        lo = 0 if lo is None else lo
+        hi = n if hi is None else hi
+        p = slice(0, 128) if parts is None else slice(parts[0], parts[1])
+        return {"ap": T[name][p, lo:hi:step] if step != 1 else T[name][p, lo:hi], "rg": [(name, lo, hi)],
+                "n": len(range(lo, hi, step)), "two": SB[name][1] in (bf, u16, f16), "ps": False, "ind": False}
+
+    def r3(name, a0=None, a1=None, b0=None, b1=None, step=1, parts=None):
+        ps = name in PS
+        sh = [16, 32] if ps else SB[name][0]
+        a0 = 0 if a0 is None else a0
+        a1 = sh[0] if a1 is None else a1
+        b0 = 0 if b0 is None else b0
+        b1 = sh[1] if b1 is None else b1
+        p = slice(0, 128) if parts is None else slice(parts[0], parts[1])
+        ap = T[name][p, a0:a1, b0:b1:step] if step != 1 else T[name][p, a0:a1, b0:b1]
+        return {"ap": ap, "rg": [(name, a0 * sh[1] + b0, (a1 - 1) * sh[1] + b1)], "n": (a1 - a0) * len(range(b0, b1, step)),
+                "two": (not ps) and SB[name][1] in (bf, u16, f16), "ps": ps, "ind": False}
+
+    def pq(name, lo, hi, parts=None):
+        return r3(name, lo // 32, hi // 32, parts=parts)
+
+    def ind(win, off):
+        return {"ap": win["ap"].indirect(off["ap"]), "rg": win["rg"], "off": off["rg"], "n": 16 * off["n"], "two": False, "ps": False, "ind": True}
+
+    def col(k):
+        return ref("col", k, k + 1)
+
+    def add(eng, fn, outs, ins, cost, **kw):
+        R, Wr = [], []
+        for x in ins:
+            if isinstance(x, dict):
+                R += x["rg"] + x.get("off", [])
+        for x in outs:
+            Wr += x["rg"]
+            R += x.get("off", [])
+        o = {"e": eng, "fn": fn, "R": R, "W": Wr, "c": cost, "id": len(ops)}
+        o.update(kw)
+        ops.append(o)
+
+    def ap(x):
+        return x["ap"] if isinstance(x, dict) else x
+
+    def vc(out, ins, per):
+        if out["ind"]:
+            return 55 + SCA * CY * out["n"]
+        if ins[0]["ind"]:
+            return 55 + GA * CY * out["n"]
+        return max(64, per * ins[0]["n"]) * CY
+
+    def cp(out, a):
+        add("v", lambda: g.vector.tensor_copy(out["ap"], a["ap"]), [out], [a], vc(out, [a], 0.5 if out["two"] and a["two"] else 1))
+
+    def tt(out, a, b, op):
+        add("v", lambda: g.vector.tensor_tensor(out["ap"], a["ap"], b["ap"], op), [out], [a, b], vc(out, [a], 1 if a["ps"] or b["ps"] else 2))
+
+    early = [True]
+
+    def ts(out, a, s1, op0, s2=None, op1=None):
+        if early[0] and not a["ind"] and all(SB[x["rg"][0][0]][1] in (bf, f32) for x in (out, a)):
+            if op0 == A.mult and op1 in (None, A.add):
+                return act(out, a, F.Identity, bias=0.0 if op1 is None else s2, scale=s1)
+            if op0 == A.add and op1 is None:
+                return act(out, a, F.Identity, bias=s1)
+        if op1 is None:
+            fn = lambda: g.vector.tensor_scalar(out["ap"], a["ap"], ap(s1), None, op0)
+        else:
+            fn = lambda: g.vector.tensor_scalar(out["ap"], a["ap"], ap(s1), ap(s2), op0, op1)
+        add("v", fn, [out], [a, s1, s2], vc(out, [a], 0.5 if out["two"] and a["two"] else 1))
+
+    def ms(out, v):
+        add("v", lambda: g.vector.memset(out["ap"], v), [out], [], max(64, out["n"] * 0.5) * CY)
+
+    def tr(out, a):
+        add("v", lambda: g.vector.transpose(out["ap"], a["ap"]), [out], [a], a["n"] * CY)
+
+    def act(out, a, fn, bias=0.0, scale=1.0, acc=None):
+        kw = {}
+        if fn != F.Copy:
+            kw["bias"] = ap(bias)
+        if scale != 1.0:
+            kw["scale"] = ap(scale)
+        if acc is not None:
+            kw["accum_out"] = acc["ap"]
+        c = 70 + GA * CY * out["n"] if a["ind"] else max(64, out["n"]) * CY + 40
+        add("s", lambda: g.scalar.activation(out["ap"], a["ap"], fn, **kw), [out] + ([acc] if acc else []), [a, bias, scale], c)
+
+    def mm(out, l, r, start, stop):
+        add("p", lambda: g.tensor.matmul(out["ap"], l["ap"], r["ap"], start, stop), [out], [l, r], max(64, r["n"]) * PCY)
+
+    def group(out, pairs):
+        for i, (l, r) in enumerate(pairs):
+            mm(out, l, r, i == 0, i == len(pairs) - 1)
+
+    def iota(out, pat, base, cm):
+        small = SB[out["rg"][0][0]][1] != i32
+        if small:
+            fn = lambda: g.iota(out["ap"], pat, base, cm, allow_small_or_imprecise_dtypes=True)
+        else:
+            fn = lambda: g.iota(out["ap"], pat, base, cm)
+        add("g", fn, [out], [], 130 + 2 * CY * out["n"])
+
+    nd = [0]
+
+    def dma(out, a, nbytes, load):
+        sem = "d%d" % nd[0]
+        nd[0] += 1
+        oa, ia = (out["ap"], a) if load else (out, a["ap"])
+        add("y", lambda: g.sync.dma_start(oa, ia), [out] if load else [], [] if load else [a], 60, sem=sem, nb=nbytes)
+
+    def push(t):
+        B = B0 + S * t
+        dst = T.cores[(rank - JUMPS[t]) % len(T.cores)]
+        rid, pid, se = topo.addr(dst)
+        src = ref("X", X0, X0 + B)
+        o = ref("xr%d" % t)
+        add("g", lambda: g.remote_dma(o["ap"], src["ap"], T.sem["arr%d" % t], T.sem["snt%d" % t], pid, rid, topo.mask(core, dst)),
+            [], [src], 600, sem="snt%d" % t, nb=B * 256, cnt=len(topo.engines(core, dst)), remote=True)
+        frm = T.cores[(rank + JUMPS[t]) % len(T.cores)]
+        add("x", None, [o], [], 0, sem="arr%d" % t, cnt=len(topo.engines(frm, core)), after=len(ops) - 1)
+
+    def swapped(bank, mats, srcs, rows, first=None):
+        lst = []
+        for (mat, base), src in zip(mats, srcs):
+            for c in range(2):
+                for h in range(2):
+                    o = base + 160 * c + 16 + 16 * (c - h)
+                    lst.append((c, ref(mat, o, o + 128), src(h)))
+        if first is not None:
+            mm(pq(bank, 0, 32 * rows), first[0], first[1], True, False)
+            for i, (c, l, r) in enumerate(lst):
+                mm(r3(bank, 0, rows, 16 * c, 16 * c + 16), l, r, False, i == len(lst) - 1)
+        else:
+            for c in range(2):
+                group(r3(bank, 0, rows, 16 * c, 16 * c + 16), [(l, r) for cc, l, r in lst if cc == c])
+
+    dma(ref("lf"), T.leaf[:], 8192, True)
+    dma(ref("wt"), T.wts[:], 8192, True)
+    dma(ref("cv"), T.cov[:], 65536, True)
+    dma(ref("X", X0, X0 + B0), T.lab[:], 524288, True)
+    dma(ref("ac"), T.act[:], 262144, True)
+    dma(ref("pt"), T.pth[:], 1048576, True)
+    iota(ref("pc", 0, 1), [[0, 1]], 0, 1)
+    iota(ref("GQ"), [[1, 10], [0, 16]], -1, 0)
+    iota(ref("MQ"), [[0, 10], [1, 16]], 0, 0)
+    iota(ref("QQ"), [[1, 160]], 0, 0)
+    iota(ref("io16"), [[1, 16]], 0, 0)
+    iota(ref("IL"), [[16, 64]], B0, 0)
+    iota(ref("SM"), [[0, 16], [1, 16]], 0, 0)
+    iota(ref("IOT"), [[1, 256]], 0, 0)
+    ms(ref("X", 0, X0), 300.0)
+    ms(ref("ZR"), 0.0)
+    p = ref("pc", 0, 1)
+    ts(ref("pd", 0, 1), p, 4, A.arith_shift_right)
+    ts(ref("pd", 1, 2), p, 15, A.bitwise_and)
+    ts(ref("pd", 2, 3), p, 4, A.arith_shift_right, 1, A.bitwise_and)
+    ts(ref("pd", 3, 4), p, 3, A.arith_shift_right, 1, A.bitwise_and)
+    ts(ref("pd", 4, 5), p, 7, A.bitwise_and)
+    cp(ref("col", 0, 5), ref("pd", 0, 5))
+    cg, pm, hf, up, lo8 = col(0), col(1), col(2), col(3), col(4)
+    ts(ref("BD"), ref("GQ"), cg, A.is_equal)
+    ts(ref("k1"), ref("BD"), 100.0, A.mult)
+    tt(ref("KEY"), ref("k1"), ref("MQ"), A.add)
+    K = ref("KEY", 16, 144)
+    ts(col(5), pm, 100.0, A.add)
+    ts(ref("I"), ref("KEY"), col(5), A.is_equal)
+    I_, NI = ref("I", 16, 144), ref("NI")
+    ts(NI, I_, -1.0, A.mult)
+    ts(col(6), hf, -1.0, A.mult, 1.0, A.add)
+    half = [col(6), hf]
+    for c in range(2):
+        ts(ref("IS", 160 * c, 160 * c + 160), ref("I"), half[c], A.mult)
+        ts(ref("BS", 160 * c, 160 * c + 160), ref("BD"), half[c], A.mult)
+    ts(ref("wh", 0, 16), ref("wt"), 4032, A.bitwise_and)
+    ts(ref("wh", 16, 32), ref("wt"), 63, A.bitwise_and)
+    cp(ref("wf"), ref("wh"))
+    ts(ref("wl"), ref("io16", 0, 10), 0.0, A.mult, pm, A.add)
+    for h in range(2):
+        wn = ref("wf", 16 * h, 16 * h + 16)
+        tt(ref("WB", 160 * h, 160 * h + 160), ind(wn, ref("wl")), ref("BD"), A.mult)
+        for c in range(2):
+            ts(ref("WS", 320 * h + 160 * c, 320 * h + 160 * c + 160), ref("WB", 160 * h, 160 * h + 160), half[c], A.mult)
+    cp(ref("LU"), ref("lf"))
+    cp(ref("LV"), ref("lf"))
+    ts(ref("c16"), ref("cv"), -960.0, A.add)
+    swapped("M1", [("IS", 0)], [lambda h: ref("c16", 64 * h, 64 * h + 64)], 4)
+    tr(ref("tc"), pq("M1", 0, 128))
+    ts(ref("pd", 5, 6), p, 3, A.bitwise_and)
+    ts(ref("pd", 6, 7), p, 2, A.arith_shift_right, 1, A.bitwise_and)
+    cp(ref("col", 12, 14), ref("pd", 5, 7))
+    ts(col(14), col(12), 32.0, A.mult, up, A.add)
+    ts(col(15), col(13), 16.0, A.mult, col(14), A.add)
+    ts(ref("p2"), ref("io16", 0, 8), 2.0, A.mult, col(15), A.add)
+    ts(ref("COV", 0, 128), ind(ref("tc"), ref("p2")), 1024.0, A.add)
+    ts(ref("k1", 0, 128), ref("MQ", 16, 144), -7.5, A.add, 4096.0, A.mult)
+    ts(ref("k2", 0, 128), ref("k1", 0, 128), 1024.0, A.min, -1024.0, A.max)
+    tt(ref("SBD"), ref("k2", 0, 128), ref("BD", 16, 144), A.mult)
+    ts(col(16), cg, 16.0, A.mult, 16.0, A.add)
+    ts(col(17), cg, 16.0, A.mult, 24.0, A.add)
+    ts(col(18), up, 2.0, A.mult, -1.0, A.add)
+    if any(HS):
+        ts(col(8), col(18), 8192.0, A.mult, C0, A.add)
+        ts(ref("SB2"), ref("SBD"), 0.5, A.mult)
+    for j, mv in enumerate(sorted(set(MV))):
+        ts(col(9), pm, mv - 0.5, A.is_ge)
+        ts(col(36 + 2 * j), col(9), 1.0, A.mult, -2.0, A.add)
+        ts(col(37 + 2 * j), col(9), -4.5, A.mult, -7.0, A.add)
+    ts(ref("BK"), ref("QQ"), col(16), A.is_equal)
+    ts(ref("k3"), ref("QQ"), col(17), A.is_equal, col(18), A.mult)
+    tt(ref("PK"), ref("k3"), ref("BK"), A.subtract)
+    ts(col(19), lo8, 32.0, A.mult)
+    ts(col(20), up, 16.0, A.mult, col(19), A.add)
+    ts(ref("p1"), ref("io16"), col(20), A.add)
+    ts(col(21), up, -188416.0 - 1577216.0, A.mult, 1577216.0, A.add)
+    ts(col(22), pm, -512.0, A.mult, -7680.0, A.add)
+    ts(col(23), pm, -512.0, A.mult, -512.0, A.add)
+    ts(col(24), pm, 16.0, A.add)
+    for nm, base in (("U1", 0.0), ("U2", 8.0)):
+        ts(col(25), up, 200.0, A.mult, col(5), A.add)
+        ts(col(26), col(25), base, A.add)
+        ts(col(27), col(26), 200.0, A.is_lt, col(26), A.mult)
+        ts(col(28), col(27), 99.0, A.max)
+        ts(ref("k1", 0, 128), K, col(26), A.is_equal)
+        ts(ref("k2", 0, 128), K, col(28), A.is_gt)
+        tt(ref(nm), ref("k1", 0, 128), ref("k2", 0, 128), A.subtract)
+    ts(ref("k3", 0, 128), K, col(5), A.is_gt)
+    tt(ref("U0"), I_, ref("k3", 0, 128), A.subtract)
+    ts(ref("HB"), ref("BD", 16, 144), up, A.mult)
+    ts(col(30), pm, 101.0, A.add)
+    ts(ref("SH"), K, col(30), A.is_equal, 1024.0, A.mult)
+    ts(col(31), pm, 0.0, A.is_equal)
+    ts(ref("TOP"), I_, col(31), A.mult)
+    for t in range(RO):
+        ts(col(32 + t), col(31), 4.25 + t, A.mult, 16.0, A.add)
+        ts(ref("LW", 128 * t, 128 * t + 128), I_, col(32 + t), A.mult)
+    ts(ref("I128"), I_, 1.0 / 128, A.mult)
+    ts(ref("NI64"), I_, -1.0 / 64, A.mult)
+    ts(ref("G8"), ref("QQ", 0, 8), cg, A.is_equal)
+    ts(r3("CM", 0, 8), ref("SM"), pm, A.is_lt, 8192.0, A.mult)
+    ts(r3("CM", 0, 8), r3("CM", 0, 8), -4096.0, A.add)
+    ms(r3("CM", 8, 16), 4096.0)
+    ts(ref("RS", 0, 256), ref("SM"), 0.0, A.is_equal)
+    ts(ref("RS", 256, 384), ref("SM", 0, 128), 0.0, A.is_equal)
+    ts(ref("IL"), ref("IL"), pm, A.add)
+    early[0] = False
+
+    def path_list():
+        swapped("M1", [("IS", 0)], [lambda h: ref("PV", 128 * h, 128 * h + 128)], 8)
+        tr(ref("tp"), pq("M1", 0, 256))
+        ts(ref("PL"), ind(ref("tp"), ref("p1")), 1024.0, A.mult, 960.0, A.add)
+
+    def hold(t, lo, hi, banks):
+        B = B0 + S * t
+        tt(ref("C", lo, hi), ind(ref("X", 0, X0 + B), ref("COV", lo // 16, hi // 16)), ref("X2", X0 + lo, X0 + hi), A.is_le)
+        for i, a in enumerate(range(lo, hi, 512)):
+            b = min(hi, a + 512)
+            bank = pq(banks[i % len(banks)], 0, b - a)
+            group(bank, [(I_, ref("X", X0 + a, X0 + b)), (ref("SBD"), ref("C", a, b))])
+            act(ref("TT", a, b), bank, F.Identity, bias=C0)
+
+    def hold_s(t, a, b, bank):
+        bank = pq(bank, 0, b - a)
+        xs = ref("X", X0 + a, X0 + b)
+        act(ref("XC", 0, b - a), ind(ref("X", 0, X0 + B0 + S * t), ref("COV", a // 16, b // 16)), F.Copy)
+        group(bank, [(I_, xs), (NI, ref("XC", 0, b - a))])
+        act(ref("C", a, b), bank, F.Sign, bias=0.5)
+        group(bank, [(I_, xs), (ref("SB2"), ref("C", a, b))])
+        act(ref("TT", a, b), bank, F.Identity, bias=col(8))
+
+    for t in range(RO):
+        B = B0 + S * t
+        last = t == RO - 1
+        z, cs, lvn = ref("z%d" % (t & 1)), ref("cs%d" % (t & 1)), "lv%d" % (t & 1)
+        lv = r3(lvn)
+        Xw = ref("X", X0, X0 + B)
+        fr = (8 + t) / 16.0
+        push(t)
+        for i, a in enumerate(range(X0, X0 + B, 512)):
+            b = min(a + 512, X0 + B)
+            if COPY[t][i] == "s":
+                act(ref("X2", a, b), ref("X", a, b), F.Copy)
+            else:
+                cp(ref("X2", a, b), ref("X", a, b))
+        act(ref("xv"), ind(Xw, ref("LU")), F.Copy)
+        xh = lambda h: ref("xv", 128 * h, 128 * h + 128)
+        swapped("M0", [("WS", 0), ("WS", 320)], [xh, xh], 8)
+        tr(r3("tx"), pq("M0", 0, 256))
+        for h in range(2):
+            cp(r3("hi", 8 * h, 8 * h + 8), r3("tx", 0, 8, 16 * h, 16 * h + 2))
+        ts(ref("ha"), r3("hi", 0, 16, 0, 1), 1023, A.bitwise_and)
+        cp(ref("LA"), ref("ha"))
+        ts(ref("hq"), r3("hi", 0, 16, 1, 2), 4095, A.bitwise_and)
+        ts(ref("LQ"), ref("hq"), fr, A.mult, -15.0 / 32, A.add)
+        act(ref("av"), ind(ref("ac"), ref("LA")), F.Copy)
+        group(pq("M1", 0, 256), [(I_, ref("xv")), (NI, ref("av"))])
+        act(z, pq("M1", 0, 256), F.Abs)
+        group(pq("M2b", 0, 256), [(ref("WB", 16, 144), z), (ref("WB", 176, 304), z)])
+        cp(ref("ci"), pq("M2b", 0, 256))
+        ts(ref("cj"), ref("ci"), 4095, A.bitwise_and)
+        ts(ref("CL"), ref("cj"), fr, A.mult, -15.0 / 32, A.add)
+        ts(cs, ref("CL"), -1023.0, A.add, 1.0 / 1024, A.mult)
+        for a in range(0, 4096, CG):
+            act(ref("XK", a, a + CG), ind(ref("X2", X0, X0 + B), ref("CL", a // 16, (a + CG) // 16)), F.Copy)
+        act(ref("E", 0, 256), ind(ref("xr%d" % t), ref("LQ")), F.Copy)
+        act(ref("E", 256, 512), ref("E", 0, 256), F.Copy)
+        act(ref("EM"), ref("E", 0, 256), F.Relu, bias=-510.0, scale=2.0)
+        if t == 0:
+            ts(ref("PV"), ind(ref("pt"), ref("LU")), -960.0, A.add, 1.0 / 1024, A.mult)
+            path_list()
+        old = B if t == 0 else B - S
+        if HS[t]:
+            hold_s(t, 0, HS[t], "M2b")
+        for a in range(HS[t], old, HC):
+            hold(t, a, min(old, a + HC), ["P1", "P2"] if HC > 512 or ((a - HS[t]) // HC) % 2 else ["P2"])
+        for k in range(15, -1, -1):
+            if k % 2:
+                if k == 1 and t:
+                    hold(t, old, B, ["M1"])
+                tt(ref("O", 256 * k - 256, 256 * k + 256), ind(ref("TT", 0, old if k > 1 else B), ref("PL", 16 * k - 16, 16 * k + 16)), ref("E"), A.subtract)
+            j = k % 8
+            mm(pq("P2" if k >= 8 else "P1", 0, 256), ref("PK", 16 - j, 144 - j), ref("O", 256 * k, 256 * k + 256), j == 7, j == 0)
+            if j == 0:
+                act(ref("F2" if k else "F1"), pq("P2" if k else "P1", 0, 256), F.Sign, bias=col(21))
+        group(pq("M0", 0, 256), [(NI, ref("EM")), (ref("U2"), ref("F2")), (ref("U1"), ref("F1"))])
+        group(pq("M1", 0, 256), [(ref("HB"), ref("F2")), (ref("HB"), ref("F1"))])
+        act(r3("OH"), pq("M0", 0, 256), F.Relu, bias=col(22), scale=512.0)
+        ts(lv, pq("M1", 0, 256), -15.0, A.is_lt, 256.0, A.mult)
+        act(ref("Y"), lv, F.Identity, acc=ref("cn", t, t + 1))
+        tt(r3("M"), r3("OH"), ref("PV"), A.mult)
+        hv = lambda nm: (lambda h: r3(nm, 0, 8, 16 * h, 16 * h + 16))
+        swapped("M2b", [("BS", 0)] * 3, [hv(lvn), hv("OH"), hv("M")], 8, first=(ref("ZR"), ref("IOT")))
+        BDm = ref("BD", 16, 144)
+        mm(pq("M0", 0, 512), I_, r3("CM"), True, False)
+        mm(pq("M0", 0, 256), BDm, r3("OH"), False, False)
+        mm(r3("M0", 8, 16, 0, 16), BDm, r3("OH", 0, 8, 0, 16), False, False)
+        mm(pq("M0", 0, 256), BDm, r3("M"), False, False)
+        mm(r3("M0", 8, 16, 0, 16), BDm, r3("M", 0, 8, 0, 16), False, True)
+        tr(r3("LR"), pq("M2b", 0, 256))
+        L = r3("LR", 0, 8, 0, 32, 16)
+        ts(ref("GL"), L, -4096.0, A.add, 0.0, A.max)
+        tt(ref("NE", 0, 256), r3("LR"), pq("M0", 0, 256), A.not_equal)
+        tt(ref("NE", 256, 384), r3("LR", 0, 8, 16, 32), r3("M0", 8, 16, 0, 16), A.not_equal)
+        kp, rs, ne = ref("KP"), ref("RS"), ref("NE")
+        add("v", lambda kp=kp, rs=rs, ne=ne: g.vector.tensor_tensor_scan(kp["ap"], rs["ap"], ne["ap"], 0.0, A.max, A.mult), [kp], [rs, ne], 200 * CY)
+        tt(ref("vt"), ref("KP", 15, 256, 16), L, A.mult)
+        tt(ref("vo"), ref("vt", 1, 16, 2), ref("KP", 271, 384, 16), A.mult)
+        ts(ref("TL", 0, 16, 2), ref("vt", 0, 16, 2), -4096.0, A.add, pm, A.max)
+        ts(ref("TL", 1, 16, 2), ref("vo"), -4096.0, A.add, col(24), A.max)
+        Xa = ref("X", 0, X0 + B)
+        tt(ref("NV"), ind(Xa, ref("GL")), ref("E", 0, 256), A.max)
+        for b in range(7, -1, -1):
+            cp(ind(Xa, ref("TL", 2 * b, 2 * b + 2)), ref("NV", 32 * b, 32 * b + 32))
+        tt(ref("la"), L, ref("IL", 16 * t, 16 * t + 16), A.min)
+        tt(ref("LV"), ref("LV"), ref("la"), A.max)
+        if not last:
+            cp(ref("LU"), ref("LV"))
+        group(pq("M1", 0, 256), [(I_, z), (NI, lv)])
+        act(ref("Y"), pq("M1", 0, 256), F.Relu, scale=-1.0)
+        act(ref("X", X0 + B, X0 + B + S), ref("Y"), F.Identity, bias=256.0, scale=-1.0)
+        group(pq("P2", 0, 256), [(ref("SH"), ref("PV")), (ref("TOP"), ref("IOT")), (ref("LW", 128 * t, 128 * t + 128), lv)])
+        yp = ref("YP", S * t, S * t + S)
+        act(yp, pq("P2", 0, 256), F.Relu, bias=-3136.0)
+        dma(T.yp[:, S * t:S * t + S], yp, 131072, False)
+        if not last:
+            act(ref("yq"), yp, F.Identity, bias=-0.9375, scale=1.0 / 1024)
+            group(pq("P1", 0, 256), [(I_, ref("PV")), (ref("NI64"), lv)])
+            tt(ref("PV"), pq("P1", 0, 256), ref("yq"), A.max)
+            path_list()
+        n = 0
+        mv = MV[t]
+        if mv < 16:
+            group(pq("A1", 0, 256), [(I_, z)])
+        for q in range(2):
+            for m0 in range(0, mv, 4):
+                bank = "A%d" % (n & 1) if mv == 16 else "A0"
+                n += 1
+                m1 = min(mv, m0 + 4)
+                for m in range(m0, m1):
+                    o = pq(bank, 128 * (m - m0), 128 * (m - m0) + 128)
+                    group(o, [(I_, ref("z%d" % (t & 1), 128 * q, 128 * q + 128)), (NI, ref("XK", 2048 * q + m, 2048 * q + 2048, 16))])
+                a = 2048 * q + 128 * m0
+                act(ref("SG", a, a + 128 * (m1 - m0)), pq(bank, 0, 128 * (m1 - m0)), F.Sign, bias=0.5)
+            for m in range(mv, 16):
+                a = 2048 * q + 128 * m
+                tt(ref("SG", a, a + 128), ref("XK", 2048 * q + m, 2048 * q + 2048, 16), pq("A1", 128 * q, 128 * q + 128), A.is_le)
+            for m in range(16):
+                a = 2048 * q + 128 * m
+                mm(pq("CB", 128 * q, 128 * q + 128), ref("BK", 16 - m, 144 - m), ref("SG", a, a + 128), m == 0, m == 15)
+        ts(ref("pi", t, t + 1), ref("cn", t, t + 1), 1.0 / 256, A.mult)
+        ts(ref("pj", t, t + 1), ref("pi", t, t + 1), 1, A.bitwise_and)
+        j = 36 + 2 * sorted(set(MV)).index(mv)
+        ts(ref("pb", t, t + 1), ref("pj", t, t + 1), col(j), A.mult, col(j + 1), A.add)
+        act(ref("FS"), pq("CB", 0, 256), F.Sign, bias=ref("pb", t, t + 1))
+        group(pq("A0", 0, 256), [(ref("I128"), lv), (ref("U0"), ref("FS"))])
+        act(ref("O2"), pq("A0", 0, 256), F.Relu, bias=col(23), scale=512.0)
+        act(pq("CB", 0, 256), pq("A0", 0, 256), F.Relu, bias=col(23), scale=512.0)
+        tt(ref("M2"), pq("CB", 0, 256), cs, A.mult)
+        if not last:
+            group(r3("CB", 0, 1, 0, 16), [(ref("BK", 16 - i, 144 - i), ref(nm, i, 256, 16)) for nm in ("O2", "M2") for i in range(16)])
+            ts(ref("COV", B // 16, B // 16 + 16), r3("CB", 0, 1, 0, 16), 63.0, A.add)
+        group(pq("A0", 0, 256, (0, 8)), [(ref("G8"), ref("O2")), (ref("G8"), ref("M2"))])
+        act(ref("YC", S * t, S * t + S, parts=(0, 8)), pq("A0", 0, 256, (0, 8)), F.Identity, bias=-1.0)
+    dma(T.yx[:, 0:W - S], ref("X", X0, X0 + W - S), 720896, False)
+    dma(T.yx[:, W - S:W], ref("X", X0 + W - S, X0 + W), 65536, False)
+    dma(T.yv[:], ref("LV"), 8192, False)
+    dma(T.yc[:], ref("YC", parts=(0, 8)), 32768, False)
+    return ops
+
+
+def depend(ops):
+    seen = {}
+    for o in ops:
+        d = {}
+        if "after" in o:
+            d[o["after"]] = False
+        for kind in ("R", "W"):
+            for (nm, lo, hi) in o[kind]:
+                ps = nm in PS
+                for (j, k2, l2, h2) in seen.get(nm, []):
+                    if j == o["id"]:
+                        continue
+                    same = ops[j]["e"] == o["e"]
+                    if ps:
+                        d[j] = d.get(j, False) or not same
+                    elif (kind == "W" or k2 == "W") and lo < h2 and l2 < hi:
+                        d[j] = True
+        o["d"] = d
+        for kind in ("R", "W"):
+            for (nm, lo, hi) in o[kind]:
+                lst = seen.setdefault(nm, [])
+                if nm in PS:
+                    lst[:] = [x for x in lst if ops[x[0]]["e"] != o["e"]][-3:]
+                elif kind == "W":
+                    lst[:] = [x for x in lst if not (lo <= x[2] and x[3] <= hi)]
+                lst.append((o["id"], kind, lo, hi))
+
+
+def schedule(ops):
+    n = len(ops)
+    succ = [[] for _ in ops]
+    for o in ops:
+        for j in o["d"]:
+            succ[j].append(o["id"])
+
+    res = ["dma" if "nb" in o else o["e"] for o in ops]
+    dur = [o["nb"] / RATE + 60 if "nb" in o else o["c"] for o in ops]
+    tail = [LAT if "nb" in o else 0 for o in ops]
+    pred = [[(j, tail[j] + (HOP if w else 0)) for j, w in o["d"].items()] for o in ops]
+    post = [[(j, tail[i] + (HOP if ops[j]["d"][i] else 0)) for j in succ[i]] for i in range(n)]
+
+    def place(seq, before):
+        st = [0.0] * n
+        busy = {}
+        for i in seq:
+            t = max([st[j] + dur[j] + lag for j, lag in before[i]] + [0.0])
+            b = busy.setdefault(res[i], [])
+            lo, hi = 0, len(b)
+            while lo < hi:
+                mid = (lo + hi) // 2
+                if b[mid][1] <= t:
+                    lo = mid + 1
+                else:
+                    hi = mid
+            while lo < len(b) and b[lo][0] < t + dur[i]:
+                t = max(t, b[lo][1])
+                lo += 1
+            b.insert(lo, (t, t + dur[i]))
+            st[i] = t
+        return st
+
+    seed = [12345]
+
+    def rnd():
+        seed[0] = (seed[0] * 1103515245 + 12345) % 2147483648
+        return seed[0] / 2147483648.0
+
+    def topo_by(key, before, after):
+        left = [len(before[i]) for i in range(n)]
+        rank = sorted(range(n), key=lambda i: key[i])
+        pos = [0] * n
+        for k, i in enumerate(rank):
+            pos[i] = k
+        pool = sorted(pos[i] for i in range(n) if not left[i])
+        out = []
+        while pool:
+            i = rank[pool.pop(0)]
+            out.append(i)
+            new = []
+            for j, lag in after[i]:
+                left[j] -= 1
+                if not left[j]:
+                    new.append(pos[j])
+            if new:
+                pool = sorted(pool + new)
+        return out
+
+    def both(key):
+        back = place(topo_by(key, post, pred), post)
+        st = place(topo_by([-(back[i] + dur[i]) for i in range(n)], pred, post), pred)
+        return max(st[i] + dur[i] + tail[i] for i in range(n)), st
+
+    best = both([-float(i) for i in range(n)])
+    cur = best
+    for it in range(PASSES):
+        st = cur[1]
+        a = best[0] * rnd()
+        b = a + 1000.0 + 5000.0 * rnd()
+        amp = 2500.0 * rnd() ** 2
+        eng = "vsp*"[int(4 * rnd())]
+        new = both([-(st[i] + dur[i]) + (amp * (rnd() - 0.5) if a <= st[i] <= b and eng in ("*", res[i]) else 0.0) for i in range(n)])
+        if new[0] <= cur[0] + 150.0 * (1.0 - it / PASSES):
+            cur = new
+        if new[0] < best[0]:
+            best = new
+    st = best[1]
+    for i, o in enumerate(ops):
+        o["t"], o["f"] = st[i], st[i] + dur[i] + tail[i]
+    return [ops[i] for i in topo_by(st, pred, post)]
+
+
+def rank_program(g, core, T, topo):
+    rank = T.rank_of(core)
+    if rank is None:
+        return
+    ops = build(g, T, rank, core, topo)
+    depend(ops)
+    if not ORDER:
+        ORDER.extend(o["id"] for o in schedule(ops))
+    order = [ops[i] for i in ORDER]
+    Q = {"v": g.vector, "s": g.scalar, "p": g.tensor, "g": g, "y": g.sync}
+    cnt = {"v": 0, "s": 0, "p": 0, "g": 0}
+    need = set(j for o in ops for j, w in o["d"].items() if w)
+    had = {e: {} for e in Q}
+    top = {}
+    for o in order:
+        e = o["e"]
+        if e == "x":
+            o["sig"] = (o["sem"], o["cnt"])
+            top[o["sem"]] = o["cnt"]
+            continue
+        want = {}
+        for j, w in o["d"].items():
+            if w:
+                s, c = ops[j]["sig"]
+                want[s] = max(want.get(s, 0), c)
+        for s, c in want.items():
+            if had[e].get(s, 0) < c:
+                Q[e].wait_ge(T.sem[s], c)
+                had[e][s] = c
+        ins = o["fn"]()
+        if o.get("remote"):
+            o["sig"] = (o["sem"], o["cnt"])
+        elif "sem" in o:
+            ins.then_inc(T.sem[o["sem"]], 16)
+            o["sig"] = (o["sem"], 16)
+        elif o["id"] in need:
+            cnt[e] += 1
+            ins.then_inc(T.sem[e], 1)
+            o["sig"] = (e, cnt[e])
+        else:
+            continue
+        top[o["sig"][0]] = o["sig"][1]
+    for s, c in top.items():
+        if had["y"].get(s, 0) < c:
+            g.sync.wait_ge(T.sem[s], c)

@@ -6,38 +6,46 @@ B0, S, RO, W = 2048, 256, 4, 3072
 JUMPS = [1, 2, 3, 1]
 X0 = 64
 C0 = 98560.5
+K2 = 2048.0
+LIVE = 4096.0
+OFF = 16 * LIVE - 16 * 1088
 bf, f32, i32, u16, f16 = "bfloat16", "float32", "int32", "uint16", "float16"
 SB = {
-    "X": ([X0 + W], bf), "X2": ([X0 + W - S], bf), "xr0": ([2048], bf), "xr1": ([2304], bf), "xr2": ([2560], bf), "xr3": ([2816], bf),
+    "X": ([X0 + W], bf), "XA": ([W - S], bf), "XB": ([W - S], bf), "xr0": ([2048], bf), "xr1": ([2304], bf), "xr2": ([2560], bf), "xr3": ([2816], bf),
     "TT": ([2816], f32), "pt": ([2048], i32), "ac": ([1024], bf), "cv": ([128], i32), "wt": ([16], i32), "lf": ([16], i32),
-    "O": ([4096], bf), "XK": ([4096], bf), "SG": ([4096], bf), "C": ([2816], bf), "YP": ([1024], f32), "YC": ([1024], f32),
+    "O": ([4096], bf), "XK": ([4096], bf), "SG": ([4096], bf), "C": ([2816], bf), "YP": ([1024], f32), "YC": ([256], f32),
     "COV": ([192], u16), "PL": ([256], u16), "LU": ([16], u16), "LV": ([16], f32), "PV": ([256], f16),
     "xv": ([256], bf), "av": ([256], bf), "z0": ([256], bf), "z1": ([256], bf), "E": ([512], bf), "EM": ([256], bf),
-    "tx": ([8, 32], f32), "hi": ([16, 2], i32), "ha": ([16], i32), "hq": ([16], i32), "LA": ([16], u16), "LQ": ([16], u16),
+    "tx": ([128], f32), "hi": ([32], i32), "ha": ([32], i32), "LA": ([16], u16), "LQ": ([16], u16), "hp": ([2], u16),
     "ci": ([256], i32), "cj": ([256], i32), "CL": ([256], u16), "cs0": ([256], f16), "cs1": ([256], f16),
-    "F1": ([256], bf), "F2": ([256], bf), "OH": ([8, 32], bf), "lv0": ([8, 32], bf), "lv1": ([8, 32], bf), "M": ([8, 32], f16),
+    "F1": ([256], bf), "F2": ([256], bf), "lv0": ([8, 32], bf), "lv1": ([8, 32], bf), "MT": ([8, 32], f16),
     "LR": ([8, 32], f32), "NE": ([384], bf), "KP": ([384], bf), "RS": ([384], bf), "vt": ([16], f32), "vo": ([8], f32), "GL": ([16], u16),
     "TL": ([16], u16), "NV": ([256], bf), "la": ([16], f32), "Y": ([256], bf), "yq": ([256], f32), "tp": ([256], f32),
-    "cn": ([4], f32), "pi": ([4], i32), "pj": ([4], i32), "pb": ([4], f32), "FS": ([256], bf), "O2": ([256], bf), "M2": ([256], f16),
-    "GQ": ([160], bf), "MQ": ([160], bf), "QQ": ([160], bf), "KEY": ([160], bf), "k1": ([160], bf), "k2": ([160], bf), "k3": ([160], bf),
-    "pc": ([4], i32), "pd": ([8], i32), "col": ([44], f32), "XC": ([512], bf), "SB2": ([128], bf), "IL": ([64], f32), "io16": ([16], f32), "IOT": ([256], bf), "SM": ([256], bf),
-    "I": ([160], bf), "NI": ([128], bf), "I128": ([128], bf), "NI64": ([128], bf), "BD": ([160], bf), "SBD": ([128], bf),
+    "cn": ([4], f32), "pi": ([4], i32), "pj": ([4], i32), "pb": ([4], f32), "FS": ([256], bf), "M2": ([1024], f16),
+    "KEY": ([160], bf), "k1": ([128], bf), "k2": ([160], bf), "k3": ([128], bf), "SI": ([128], bf),
+    "pc": ([4], i32), "pd": ([10], i32), "col": ([52], f32), "XC": ([512], bf), "SB2": ([128], bf), "IL": ([64], f32), "io16": ([16], f32), "IOT": ([256], bf),
+    "SM": ([8, 32], bf), "I": ([160], bf), "NI": ([128], bf), "BD": ([160], bf), "SBD": ([128], bf),
     "BK": ([160], bf), "PK": ([160], bf), "U0": ([128], bf), "U1": ([128], bf), "U2": ([128], bf), "HB": ([128], bf),
-    "SH": ([128], bf), "TOP": ([128], bf), "LW": ([512], bf), "BS": ([320], bf), "IS": ([320], bf), "WS": ([640], bf),
-    "WB": ([320], bf), "G8": ([8], bf), "ZR": ([128], bf), "CM": ([16, 32], bf), "wh": ([32], i32), "wf": ([32], f32),
-    "wl": ([10], u16), "p1": ([16], u16), "p2": ([8], u16), "c16": ([128], f16), "tc": ([128], f32),
+    "SH": ([128], bf), "TOP": ([128], bf), "BS": ([320], bf), "IS": ([320], bf), "ZW": ([320], f16),
+    "WB": ([128], f16), "GT": ([36], bf), "CM": ([8, 48], bf), "wa": ([16], f32), "wf": ([16], f32),
+    "wl": ([8], u16), "p1": ([16], u16), "p2": ([8], u16), "c16": ([128], f16), "tc": ([128], f32),
 }
-PS = ["A0", "A1", "CB", "P1", "P2", "M0", "M1", "M2b"]
+PS = {"A0": [16, 32], "A1": [16, 32], "CB": [16, 32], "P1": [16, 32], "P2": [16, 32], "M0": [8, 64], "M1": [16, 32], "M2b": [16, 32]}
 SCRATCH = {k: ("sbuf", [128] + v[0], v[1]) for k, v in SB.items()}
-SCRATCH.update({k: ("psum", [128, 16, 32], f32) for k in PS})
-NDMA = 20
+SCRATCH.update({k: ("psum", [128] + v, f32) for k, v in PS.items()})
+NDMA = 40
 SEMAPHORES = ["v", "s", "p", "g"] + ["d%d" % i for i in range(NDMA)] + ["arr%d" % t for t in range(RO)] + ["snt%d" % t for t in range(RO)]
-CY, PCY, HOP, GA, SCA = 1.04, 0.52, 120.0, 1.55, 3.8
-RATE, LAT, PASSES = 200.0, 2000.0, 4500
-COPY = ["ssss", "vvsss", "vvsss", "vvssss"]
+SETS = [dict(cy=0.9, ga=1.56, sc=3.8, pe=0.47, hop=200.0, rate=250.0, xr=170.0, lat=1300.0),
+        dict(cy=1.04, ga=1.56, sc=3.8, pe=0.53, hop=110.0, rate=300.0, xr=200.0, lat=1100.0),
+        dict(cy=1.15, ga=1.85, sc=5.0, pe=0.62, hop=280.0, rate=200.0, xr=130.0, lat=1500.0)]
+PASSES, MOVES, HEAT = 300, 40000, 60.0
+COPY = ["svsv", "vvggg", "vvggg", "vvgggg"]
 MV = [8, 8, 8, 8]
+XE = ["ssssssss"] * 4
 HS = [0, 0, 0, 0]
-HC = 1024
+SMALL = "vvss"
+LATE = ("U0", "RS", "CM", "SM", "IOT", "GT")
+HC = 512
 ORDER = []
 CG = 512
 
@@ -51,23 +59,23 @@ def build(g, T, rank, core, topo):
         lo = 0 if lo is None else lo
         hi = n if hi is None else hi
         p = slice(0, 128) if parts is None else slice(parts[0], parts[1])
-        return {"ap": T[name][p, lo:hi:step] if step != 1 else T[name][p, lo:hi], "rg": [(name, lo, hi)],
+        return {"ap": T[name][p, lo:hi:step] if step != 1 else T[name][p, lo:hi], "rg": [(name, lo, hi, lo % 2 if step == 2 else -1)],
                 "n": len(range(lo, hi, step)), "two": SB[name][1] in (bf, u16, f16), "ps": False, "ind": False}
 
     def r3(name, a0=None, a1=None, b0=None, b1=None, step=1, parts=None):
         ps = name in PS
-        sh = [16, 32] if ps else SB[name][0]
+        sh = PS[name] if ps else SB[name][0]
         a0 = 0 if a0 is None else a0
         a1 = sh[0] if a1 is None else a1
         b0 = 0 if b0 is None else b0
         b1 = sh[1] if b1 is None else b1
         p = slice(0, 128) if parts is None else slice(parts[0], parts[1])
         ap = T[name][p, a0:a1, b0:b1:step] if step != 1 else T[name][p, a0:a1, b0:b1]
-        return {"ap": ap, "rg": [(name, a0 * sh[1] + b0, (a1 - 1) * sh[1] + b1)], "n": (a1 - a0) * len(range(b0, b1, step)),
+        return {"ap": ap, "rg": [(name, a0 * sh[1] + b0, (a1 - 1) * sh[1] + b1, -1)], "n": (a1 - a0) * len(range(b0, b1, step)),
                 "two": (not ps) and SB[name][1] in (bf, u16, f16), "ps": ps, "ind": False}
 
     def pq(name, lo, hi, parts=None):
-        return r3(name, lo // 32, hi // 32, parts=parts)
+        return r3(name, lo // PS[name][1], hi // PS[name][1], parts=parts)
 
     def ind(win, off):
         return {"ap": win["ap"].indirect(off["ap"]), "rg": win["rg"], "off": off["rg"], "n": 16 * off["n"], "two": False, "ps": False, "ind": True}
@@ -85,17 +93,21 @@ def build(g, T, rank, core, topo):
             R += x.get("off", [])
         o = {"e": eng, "fn": fn, "R": R, "W": Wr, "c": cost, "id": len(ops)}
         o.update(kw)
+        if eng == "g" and early[0] and outs and outs[0]["rg"][0][0] in LATE:
+            o["after"] = first[0]
         ops.append(o)
+
+    first = []
 
     def ap(x):
         return x["ap"] if isinstance(x, dict) else x
 
     def vc(out, ins, per):
         if out["ind"]:
-            return 55 + SCA * CY * out["n"]
+            return (50, out["n"], "sc")
         if ins[0]["ind"]:
-            return 55 + GA * CY * out["n"]
-        return max(64, per * ins[0]["n"]) * CY
+            return (50, out["n"], "ga")
+        return (0, max(64, per * ins[0]["n"]), "cy")
 
     def cp(out, a):
         add("v", lambda: g.vector.tensor_copy(out["ap"], a["ap"]), [out], [a], vc(out, [a], 0.5 if out["two"] and a["two"] else 1))
@@ -118,10 +130,10 @@ def build(g, T, rank, core, topo):
         add("v", fn, [out], [a, s1, s2], vc(out, [a], 0.5 if out["two"] and a["two"] else 1))
 
     def ms(out, v):
-        add("v", lambda: g.vector.memset(out["ap"], v), [out], [], max(64, out["n"] * 0.5) * CY)
+        add("v", lambda: g.vector.memset(out["ap"], v), [out], [], (0, max(64, out["n"] * 0.5), "cy"))
 
     def tr(out, a):
-        add("v", lambda: g.vector.transpose(out["ap"], a["ap"]), [out], [a], a["n"] * CY)
+        add("v", lambda: g.vector.transpose(out["ap"], a["ap"]), [out], [a], (0, a["n"], "cy"))
 
     def act(out, a, fn, bias=0.0, scale=1.0, acc=None):
         kw = {}
@@ -131,15 +143,24 @@ def build(g, T, rank, core, topo):
             kw["scale"] = ap(scale)
         if acc is not None:
             kw["accum_out"] = acc["ap"]
-        c = 70 + GA * CY * out["n"] if a["ind"] else max(64, out["n"]) * CY + 40
+        c = (65, out["n"], "ga") if a["ind"] else (20, max(64, out["n"]), "cy")
         add("s", lambda: g.scalar.activation(out["ap"], a["ap"], fn, **kw), [out] + ([acc] if acc else []), [a, bias, scale], c)
 
-    def mm(out, l, r, start, stop):
-        add("p", lambda: g.tensor.matmul(out["ap"], l["ap"], r["ap"], start, stop), [out], [l, r], max(64, r["n"]) * PCY)
+    def mms(lst):
+        fn = lambda: [g.tensor.matmul(o["ap"], l["ap"], r["ap"], a, b) for o, l, r, a, b in lst][-1]
+        add("p", fn, [x[0] for x in lst], [x[1] for x in lst] + [x[2] for x in lst], (0, sum(max(min(64, x[1]["n"]), x[2]["n"]) for x in lst), "pe"))
 
-    def group(out, pairs):
-        for i, (l, r) in enumerate(pairs):
-            mm(out, l, r, i == 0, i == len(pairs) - 1)
+    def chain(out, pairs):
+        return [(out, l, r, i == 0, i == len(pairs) - 1) for i, (l, r) in enumerate(pairs)]
+
+    def group(out, pairs, cut=0):
+        lst = chain(out, pairs)
+        if cut:
+            mms(lst[:cut])
+        mms(lst[cut:])
+
+    def sel(out, a, pat, cmp, fill, base, cm):
+        add("g", lambda: g.affine_select(out["ap"], a["ap"], pat, cmp, fill, base, cm), [out], [a], (170, 2 * a["n"], "cy"))
 
     def iota(out, pat, base, cm):
         small = SB[out["rg"][0][0]][1] != i32
@@ -147,15 +168,24 @@ def build(g, T, rank, core, topo):
             fn = lambda: g.iota(out["ap"], pat, base, cm, allow_small_or_imprecise_dtypes=True)
         else:
             fn = lambda: g.iota(out["ap"], pat, base, cm)
-        add("g", fn, [out], [], 130 + 2 * CY * out["n"])
+        add("g", fn, [out], [], (130, 2 * out["n"], "cy"))
 
     nd = [0]
 
-    def dma(out, a, nbytes, load):
+    def dma(out, a, nbytes):
         sem = "d%d" % nd[0]
         nd[0] += 1
-        oa, ia = (out["ap"], a) if load else (out, a["ap"])
-        add("y", lambda: g.sync.dma_start(oa, ia), [out] if load else [], [] if load else [a], 60, sem=sem, nb=nbytes)
+        add("y", lambda: g.sync.dma_start(ap(out), ap(a)), [out] if isinstance(out, dict) else [], [a], (60, 0, "cy"), sem=sem, nb=nbytes)
+
+    def copy(eng, out, a):
+        if eng == "s":
+            act(out, a, F.Copy)
+        elif eng == "v":
+            cp(out, a)
+        elif eng == "g":
+            sel(out, a, [[1, a["n"]]], A.is_ge, 0.0, 0, 0)
+        else:
+            dma(out, a, 256 * out["n"])
 
     def push(t):
         B = B0 + S * t
@@ -164,148 +194,143 @@ def build(g, T, rank, core, topo):
         src = ref("X", X0, X0 + B)
         o = ref("xr%d" % t)
         add("g", lambda: g.remote_dma(o["ap"], src["ap"], T.sem["arr%d" % t], T.sem["snt%d" % t], pid, rid, topo.mask(core, dst)),
-            [], [src], 600, sem="snt%d" % t, nb=B * 256, cnt=len(topo.engines(core, dst)), remote=True)
+            [], [src], (600, 0, "cy"), sem="snt%d" % t, nb=B * 256, cnt=len(topo.engines(core, dst)), remote=True)
         frm = T.cores[(rank + JUMPS[t]) % len(T.cores)]
-        add("x", None, [o], [], 0, sem="arr%d" % t, cnt=len(topo.engines(frm, core)), after=len(ops) - 1)
+        add("x", None, [o], [], (0, 0, "cy"), sem="arr%d" % t, cnt=len(topo.engines(frm, core)), after=len(ops) - 1)
 
-    def swapped(bank, mats, srcs, rows, first=None):
-        lst = []
-        for (mat, base), src in zip(mats, srcs):
-            for c in range(2):
-                for h in range(2):
-                    o = base + 160 * c + 16 + 16 * (c - h)
-                    lst.append((c, ref(mat, o, o + 128), src(h)))
-        if first is not None:
-            mm(pq(bank, 0, 32 * rows), first[0], first[1], True, False)
-            for i, (c, l, r) in enumerate(lst):
-                mm(r3(bank, 0, rows, 16 * c, 16 * c + 16), l, r, False, i == len(lst) - 1)
-        else:
-            for c in range(2):
-                group(r3(bank, 0, rows, 16 * c, 16 * c + 16), [(l, r) for cc, l, r in lst if cc == c])
+    def swapped(bank, rows, mats, nh, start):
+        mms([x for c in range(2) for x in chain(r3(bank, 0, rows, 16 * c, 16 * c + 16), [
+            (ref(mat, 160 * c + start(c, h), 160 * c + start(c, h) + 128), src(h)) for mat, src in mats for h in range(nh)])])
 
-    dma(ref("lf"), T.leaf[:], 8192, True)
-    dma(ref("wt"), T.wts[:], 8192, True)
-    dma(ref("cv"), T.cov[:], 65536, True)
-    dma(ref("X", X0, X0 + B0), T.lab[:], 524288, True)
-    dma(ref("ac"), T.act[:], 262144, True)
-    dma(ref("pt"), T.pth[:], 1048576, True)
+    halves = lambda c, h: 16 + 16 * (c - h)
+
+    dma(ref("lf"), T.leaf[:], 8192)
+    dma(ref("wt"), T.wts[:], 8192)
+    dma(ref("cv"), T.cov[:], 65536)
+    dma(ref("X", X0, X0 + B0), T.lab[:], 524288)
+    dma(ref("ac"), T.act[:], 262144)
+    dma(ref("pt"), T.pth[:], 1048576)
+    first.append(len(ops))
+    push(0)
     iota(ref("pc", 0, 1), [[0, 1]], 0, 1)
-    iota(ref("GQ"), [[1, 10], [0, 16]], -1, 0)
-    iota(ref("MQ"), [[0, 10], [1, 16]], 0, 0)
-    iota(ref("QQ"), [[1, 160]], 0, 0)
+    iota(ref("KEY"), [[0, 10], [1, 16]], 100, 0)
+    sel(ref("KEY"), ref("KEY"), [[-16, 10], [0, 16]], A.is_ge, 0.0, 16, 1)
+    sel(ref("KEY"), ref("KEY"), [[16, 10], [0, 16]], A.is_ge, 0.0, -1, -1)
     iota(ref("io16"), [[1, 16]], 0, 0)
-    iota(ref("IL"), [[16, 64]], B0, 0)
-    iota(ref("SM"), [[0, 16], [1, 16]], 0, 0)
+    iota(ref("IL"), [[16, 64]], B0, 1)
+    iota(r3("SM"), [[0, 16], [1, 16]], 0, 0)
     iota(ref("IOT"), [[1, 256]], 0, 0)
-    ms(ref("X", 0, X0), 300.0)
-    ms(ref("ZR"), 0.0)
+    iota(ref("X", 0, X0), [[0, X0]], 300, 0)
     p = ref("pc", 0, 1)
     ts(ref("pd", 0, 1), p, 4, A.arith_shift_right)
     ts(ref("pd", 1, 2), p, 15, A.bitwise_and)
-    ts(ref("pd", 2, 3), p, 4, A.arith_shift_right, 1, A.bitwise_and)
-    ts(ref("pd", 3, 4), p, 3, A.arith_shift_right, 1, A.bitwise_and)
-    ts(ref("pd", 4, 5), p, 7, A.bitwise_and)
+    ts(ref("pd", 2, 3), p, 3, A.arith_shift_right, 1, A.bitwise_and)
+    ts(ref("pd", 3, 4), p, 3, A.bitwise_and)
+    ts(ref("pd", 4, 5), p, 5, A.arith_shift_right)
     cp(ref("col", 0, 5), ref("pd", 0, 5))
-    cg, pm, hf, up, lo8 = col(0), col(1), col(2), col(3), col(4)
-    ts(ref("BD"), ref("GQ"), cg, A.is_equal)
-    ts(ref("k1"), ref("BD"), 100.0, A.mult)
-    tt(ref("KEY"), ref("k1"), ref("MQ"), A.add)
+    cg, pm, up, lo4, pr, hf, lo8, hi4, b2 = [col(i) for i in range(9)]
+    ts(hf, pr, -2.0, A.mult, cg, A.add)
+    ts(lo8, up, -8.0, A.mult, pm, A.add)
+    ts(col(41), lo4, -0.25, A.mult)
+    ts(hi4, pm, 0.25, A.mult, col(41), A.add)
+    ts(b2, up, -2.0, A.mult, hi4, A.add)
+    ts(ref("BD"), ref("KEY"), 99.5, A.is_gt)
     K = ref("KEY", 16, 144)
-    ts(col(5), pm, 100.0, A.add)
-    ts(ref("I"), ref("KEY"), col(5), A.is_equal)
-    I_, NI = ref("I", 16, 144), ref("NI")
+    own = col(9)
+    ts(own, pm, 100.0, A.add)
+    ts(ref("I"), ref("KEY"), own, A.is_equal)
+    I_, NI, BDm = ref("I", 16, 144), ref("NI"), ref("BD", 16, 144)
     ts(NI, I_, -1.0, A.mult)
-    ts(col(6), hf, -1.0, A.mult, 1.0, A.add)
-    half = [col(6), hf]
+    ts(col(10), hf, -1.0, A.mult, 1.0, A.add)
+    half = [col(10), hf]
     for c in range(2):
         ts(ref("IS", 160 * c, 160 * c + 160), ref("I"), half[c], A.mult)
         ts(ref("BS", 160 * c, 160 * c + 160), ref("BD"), half[c], A.mult)
-    ts(ref("wh", 0, 16), ref("wt"), 4032, A.bitwise_and)
-    ts(ref("wh", 16, 32), ref("wt"), 63, A.bitwise_and)
-    cp(ref("wf"), ref("wh"))
-    ts(ref("wl"), ref("io16", 0, 10), 0.0, A.mult, pm, A.add)
-    for h in range(2):
-        wn = ref("wf", 16 * h, 16 * h + 16)
-        tt(ref("WB", 160 * h, 160 * h + 160), ind(wn, ref("wl")), ref("BD"), A.mult)
-        for c in range(2):
-            ts(ref("WS", 320 * h + 160 * c, 320 * h + 160 * c + 160), ref("WB", 160 * h, 160 * h + 160), half[c], A.mult)
+    ts(ref("wa"), ref("wt"), 2047.5, A.is_ge, -4096.0, A.mult)
+    tt(ref("wf"), ref("wt"), ref("wa"), A.add)
+    ts(ref("pd", 9, 10), ref("wt", 0, 1), 1023, A.bitwise_and)
+    ts(col(11), ref("pd", 9, 10), 4.0, A.mult)
+    ts(ref("wl"), ref("io16", 0, 8), 0.0, A.mult, pm, A.add)
+    tt(ref("WB"), ind(ref("wf"), ref("wl")), BDm, A.mult)
+    ms(ref("ZW"), 0.0)
+    for c in range(2):
+        ts(col(12 + c), half[1 - c], 100.0, A.mult, pr, A.add)
+        for m, wc in enumerate((col(11), ref("wf", 1, 2))):
+            ts(ref("ZW", 160 * c + 32 + m, 160 * c + 160, 32), ref("io16", 0, 4), col(12 + c), A.is_equal, wc, A.mult)
+    ts(col(14), lo4, 32.0, A.mult)
+    ts(col(15), hi4, 2.0, A.mult, col(14), A.add)
+    ts(ref("hp"), ref("io16", 0, 2), col(15), A.add)
     cp(ref("LU"), ref("lf"))
     cp(ref("LV"), ref("lf"))
     ts(ref("c16"), ref("cv"), -960.0, A.add)
-    swapped("M1", [("IS", 0)], [lambda h: ref("c16", 64 * h, 64 * h + 64)], 4)
+    swapped("M1", 4, [("IS", lambda h: ref("c16", 64 * h, 64 * h + 64))], 2, halves)
     tr(ref("tc"), pq("M1", 0, 128))
-    ts(ref("pd", 5, 6), p, 3, A.bitwise_and)
-    ts(ref("pd", 6, 7), p, 2, A.arith_shift_right, 1, A.bitwise_and)
-    cp(ref("col", 12, 14), ref("pd", 5, 7))
-    ts(col(14), col(12), 32.0, A.mult, up, A.add)
-    ts(col(15), col(13), 16.0, A.mult, col(14), A.add)
-    ts(ref("p2"), ref("io16", 0, 8), 2.0, A.mult, col(15), A.add)
+    ts(col(16), up, col(14), A.add)
+    ts(col(17), b2, 16.0, A.mult, col(16), A.add)
+    ts(ref("p2"), ref("io16", 0, 8), 2.0, A.mult, col(17), A.add)
     ts(ref("COV", 0, 128), ind(ref("tc"), ref("p2")), 1024.0, A.add)
-    ts(ref("k1", 0, 128), ref("MQ", 16, 144), -7.5, A.add, 4096.0, A.mult)
-    ts(ref("k2", 0, 128), ref("k1", 0, 128), 1024.0, A.min, -1024.0, A.max)
-    tt(ref("SBD"), ref("k2", 0, 128), ref("BD", 16, 144), A.mult)
-    ts(col(16), cg, 16.0, A.mult, 16.0, A.add)
-    ts(col(17), cg, 16.0, A.mult, 24.0, A.add)
-    ts(col(18), up, 2.0, A.mult, -1.0, A.add)
+    sg = col(20)
+    ts(sg, up, 2.0, A.mult, -1.0, A.add)
+    ts(ref("SI"), I_, sg, A.mult)
+    ts(ref("SBD"), BDm, 1024.0, A.mult)
     if any(HS):
-        ts(col(8), col(18), 8192.0, A.mult, C0, A.add)
-        ts(ref("SB2"), ref("SBD"), 0.5, A.mult)
-    for j, mv in enumerate(sorted(set(MV))):
-        ts(col(9), pm, mv - 0.5, A.is_ge)
-        ts(col(36 + 2 * j), col(9), 1.0, A.mult, -2.0, A.add)
-        ts(col(37 + 2 * j), col(9), -4.5, A.mult, -7.0, A.add)
-    ts(ref("BK"), ref("QQ"), col(16), A.is_equal)
-    ts(ref("k3"), ref("QQ"), col(17), A.is_equal, col(18), A.mult)
-    tt(ref("PK"), ref("k3"), ref("BK"), A.subtract)
-    ts(col(19), lo8, 32.0, A.mult)
-    ts(col(20), up, 16.0, A.mult, col(19), A.add)
-    ts(ref("p1"), ref("io16"), col(20), A.add)
-    ts(col(21), up, -188416.0 - 1577216.0, A.mult, 1577216.0, A.add)
-    ts(col(22), pm, -512.0, A.mult, -7680.0, A.add)
-    ts(col(23), pm, -512.0, A.mult, -512.0, A.add)
-    ts(col(24), pm, 16.0, A.add)
-    for nm, base in (("U1", 0.0), ("U2", 8.0)):
-        ts(col(25), up, 200.0, A.mult, col(5), A.add)
-        ts(col(26), col(25), base, A.add)
-        ts(col(27), col(26), 200.0, A.is_lt, col(26), A.mult)
-        ts(col(28), col(27), 99.0, A.max)
-        ts(ref("k1", 0, 128), K, col(26), A.is_equal)
-        ts(ref("k2", 0, 128), K, col(28), A.is_gt)
-        tt(ref(nm), ref("k1", 0, 128), ref("k2", 0, 128), A.subtract)
-    ts(ref("k3", 0, 128), K, col(5), A.is_gt)
-    tt(ref("U0"), I_, ref("k3", 0, 128), A.subtract)
-    ts(ref("HB"), ref("BD", 16, 144), up, A.mult)
-    ts(col(30), pm, 101.0, A.add)
-    ts(ref("SH"), K, col(30), A.is_equal, 1024.0, A.mult)
-    ts(col(31), pm, 0.0, A.is_equal)
-    ts(ref("TOP"), I_, col(31), A.mult)
+        ts(col(21), sg, 8192.0, A.mult, C0, A.add)
+        ts(ref("SB2"), BDm, 512.0, A.mult)
+    kinds = sorted(set(MV))
+    for j, mv in enumerate(kinds):
+        ts(col(22), pm, mv - 0.5, A.is_ge)
+        ts(col(44 + 2 * j), col(22), 1.0, A.mult, -2.0, A.add)
+        ts(col(45 + 2 * j), col(22), -4.5, A.mult, -7.0, A.add)
+    for nm in ("BK", "PK", "GT", "RS"):
+        iota(ref(nm), [[0, SB[nm][0][0]]], 0, 0)
+    ts(ref("BK", 16, 144, 16), ref("io16", 0, 8), cg, A.is_equal)
+    ts(ref("PK", 16, 144, 16), ref("BK", 16, 144, 16), -1.0, A.mult)
+    ts(ref("PK", 24, 152, 16), ref("BK", 16, 144, 16), sg, A.mult)
+    ts(ref("GT", 3, 35, 4), ref("BK", 16, 144, 16), 1.0, A.mult)
+    ts(col(23), lo8, 32.0, A.mult)
+    ts(col(24), up, 16.0, A.mult, col(23), A.add)
+    ts(ref("p1"), ref("io16"), col(24), A.add)
+    ts(col(25), up, -188416.0 - 1577216.0, A.mult, 1577216.0, A.add)
+    ts(col(26), pm, -K2, A.mult, -17 * K2, A.add)
+    ts(col(27), pm, -K2, A.mult, -K2 - LIVE, A.add)
+    ts(col(28), pm, 16.0, A.add)
+    ts(ref("k1"), BDm, -K2, A.mult)
+    sel(ref("U0"), ref("k1"), [[1, 128]], A.is_gt, 0.0, 0, -1)
+    sel(ref("U0"), ref("U0"), [[1, 128]], A.not_equal, K2, 0, -1)
+    ts(ref("k2"), ref("I"), up, A.mult)
+    ts(col(29), up, -1.0, A.mult, 1.0, A.add)
+    ts(ref("k3"), I_, col(29), A.mult)
+    for j, (nm, low) in enumerate((("U1", ref("k3")), ("U2", ref("k2", 24, 152)))):
+        group(pq("A%d" % j, 0, 128), [(low, ref("U0")), (ref("k2", 16, 144), ref("k1"))])
+        act(ref(nm), pq("A%d" % j, 0, 128), F.Copy)
+    ts(ref("HB"), BDm, up, A.mult)
+    ts(col(33), pm, 101.0, A.add)
+    ts(ref("SH"), K, col(33), A.is_equal)
+    ts(col(34), pm, 0.0, A.is_equal)
+    ts(ref("TOP"), I_, col(34), A.mult)
     for t in range(RO):
-        ts(col(32 + t), col(31), 4.25 + t, A.mult, 16.0, A.add)
-        ts(ref("LW", 128 * t, 128 * t + 128), I_, col(32 + t), A.mult)
-    ts(ref("I128"), I_, 1.0 / 128, A.mult)
-    ts(ref("NI64"), I_, -1.0 / 64, A.mult)
-    ts(ref("G8"), ref("QQ", 0, 8), cg, A.is_equal)
-    ts(r3("CM", 0, 8), ref("SM"), pm, A.is_lt, 8192.0, A.mult)
-    ts(r3("CM", 0, 8), r3("CM", 0, 8), -4096.0, A.add)
-    ms(r3("CM", 8, 16), 4096.0)
-    ts(ref("RS", 0, 256), ref("SM"), 0.0, A.is_equal)
-    ts(ref("RS", 256, 384), ref("SM", 0, 128), 0.0, A.is_equal)
-    ts(ref("IL"), ref("IL"), pm, A.add)
+        ts(col(36 + t), col(34), B0 + S * t - 1024.0, A.mult, 1024.0 - LIVE, A.add)
+    ts(r3("CM", 0, 8, 0, 32), r3("SM"), pm, A.is_lt, 16 * LIVE, A.mult)
+    iota(r3("CM", 0, 8, 32, 48), [[0, 128]], int(16 * LIVE), 0)
+    iota(ref("RS", 0, 128, 16), [[0, 8]], 1, 0)
+    iota(ref("RS", 128, 384, 32), [[0, 8]], 1, 0)
+    ts(col(40), cg, -16.0, A.mult)
+    ts(ref("IL"), ref("IL"), col(40), A.add)
     early[0] = False
 
     def path_list():
-        swapped("M1", [("IS", 0)], [lambda h: ref("PV", 128 * h, 128 * h + 128)], 8)
+        swapped("M1", 8, [("IS", lambda h: ref("PV", 128 * h, 128 * h + 128))], 2, halves)
         tr(ref("tp"), pq("M1", 0, 256))
-        ts(ref("PL"), ind(ref("tp"), ref("p1")), 1024.0, A.mult, 960.0, A.add)
+        ts(ref("PL"), ind(ref("tp"), ref("p1")), 1024.0, A.add)
 
     def hold(t, lo, hi, banks):
         B = B0 + S * t
-        tt(ref("C", lo, hi), ind(ref("X", 0, X0 + B), ref("COV", lo // 16, hi // 16)), ref("X2", X0 + lo, X0 + hi), A.is_le)
+        tt(ref("C", lo, hi), ind(ref("X", 0, X0 + B), ref("COV", lo // 16, hi // 16)), ref("X" + "AB"[t & 1], lo, hi), A.is_le)
         for i, a in enumerate(range(lo, hi, 512)):
             b = min(hi, a + 512)
             bank = pq(banks[i % len(banks)], 0, b - a)
-            group(bank, [(I_, ref("X", X0 + a, X0 + b)), (ref("SBD"), ref("C", a, b))])
-            act(ref("TT", a, b), bank, F.Identity, bias=C0)
+            group(bank, [(ref("SI"), ref("X", X0 + a, X0 + b)), (ref("SBD"), ref("C", a, b))], 1)
+            act(ref("TT", a, b), bank, F.Identity, bias=C0, scale=sg)
 
     def hold_s(t, a, b, bank):
         bank = pq(bank, 0, b - a)
@@ -313,88 +338,83 @@ def build(g, T, rank, core, topo):
         act(ref("XC", 0, b - a), ind(ref("X", 0, X0 + B0 + S * t), ref("COV", a // 16, b // 16)), F.Copy)
         group(bank, [(I_, xs), (NI, ref("XC", 0, b - a))])
         act(ref("C", a, b), bank, F.Sign, bias=0.5)
-        group(bank, [(I_, xs), (ref("SB2"), ref("C", a, b))])
-        act(ref("TT", a, b), bank, F.Identity, bias=col(8))
+        group(bank, [(ref("SI"), xs), (ref("SB2"), ref("C", a, b))])
+        act(ref("TT", a, b), bank, F.Identity, bias=col(21), scale=sg)
 
     for t in range(RO):
         B = B0 + S * t
         last = t == RO - 1
         z, cs, lvn = ref("z%d" % (t & 1)), ref("cs%d" % (t & 1)), "lv%d" % (t & 1)
         lv = r3(lvn)
+        snap = "X" + "AB"[t & 1]
         Xw = ref("X", X0, X0 + B)
         fr = (8 + t) / 16.0
-        push(t)
-        for i, a in enumerate(range(X0, X0 + B, 512)):
-            b = min(a + 512, X0 + B)
-            if COPY[t][i] == "s":
-                act(ref("X2", a, b), ref("X", a, b), F.Copy)
-            else:
-                cp(ref("X2", a, b), ref("X", a, b))
-        act(ref("xv"), ind(Xw, ref("LU")), F.Copy)
-        xh = lambda h: ref("xv", 128 * h, 128 * h + 128)
-        swapped("M0", [("WS", 0), ("WS", 320)], [xh, xh], 8)
-        tr(r3("tx"), pq("M0", 0, 256))
-        for h in range(2):
-            cp(r3("hi", 8 * h, 8 * h + 8), r3("tx", 0, 8, 16 * h, 16 * h + 2))
-        ts(ref("ha"), r3("hi", 0, 16, 0, 1), 1023, A.bitwise_and)
-        cp(ref("LA"), ref("ha"))
-        ts(ref("hq"), r3("hi", 0, 16, 1, 2), 4095, A.bitwise_and)
-        ts(ref("LQ"), ref("hq"), fr, A.mult, -15.0 / 32, A.add)
+        old = B if t == 0 else B - S
+        if t:
+            push(t)
+        cuts = list(range(0, old, 512)) + [old] + ([B] if t else [])
+        for i in range(len(cuts) - 1):
+            a, b = cuts[i], cuts[i + 1]
+            e = COPY[t][min(i, len(COPY[t]) - 1)]
+            copy(e, ref(snap, a, b), T.lab[:, a:b] if t == 0 and e == "d" else ref("X", X0 + a, X0 + b))
+        copy(SMALL[3], ref("xv"), ind(Xw, ref("LU")))
+        swapped("M1", 4, [("ZW", lambda h: ref("xv", 64 * h, 64 * h + 64))], 4, lambda c, h: 32 - 2 * h)
+        tr(ref("tx"), pq("M1", 0, 128))
+        cp(ref("hi"), ind(ref("tx"), ref("hp")))
+        ts(ref("ha"), ref("hi"), 4095, A.bitwise_and)
+        ts(ref("LA"), ref("ha", 0, 16), 0.25, A.mult)
+        ts(ref("LQ"), ref("ha", 16, 32), fr, A.mult, -15.0 / 32, A.add)
         act(ref("av"), ind(ref("ac"), ref("LA")), F.Copy)
-        group(pq("M1", 0, 256), [(I_, ref("xv")), (NI, ref("av"))])
-        act(z, pq("M1", 0, 256), F.Abs)
-        group(pq("M2b", 0, 256), [(ref("WB", 16, 144), z), (ref("WB", 176, 304), z)])
+        group(pq("M0", 0, 256), [(I_, ref("xv")), (NI, ref("av"))])
+        act(z, pq("M0", 0, 256), F.Abs)
+        group(pq("M2b", 0, 256), [(ref("WB"), z)])
         cp(ref("ci"), pq("M2b", 0, 256))
         ts(ref("cj"), ref("ci"), 4095, A.bitwise_and)
         ts(ref("CL"), ref("cj"), fr, A.mult, -15.0 / 32, A.add)
-        ts(cs, ref("CL"), -1023.0, A.add, 1.0 / 1024, A.mult)
+        ts(cs, ref("CL"), -1024.0, A.add)
         for a in range(0, 4096, CG):
-            act(ref("XK", a, a + CG), ind(ref("X2", X0, X0 + B), ref("CL", a // 16, (a + CG) // 16)), F.Copy)
+            copy(XE[t][a // CG], ref("XK", a, a + CG), ind(ref(snap, 0, B), ref("CL", a // 16, (a + CG) // 16)))
         act(ref("E", 0, 256), ind(ref("xr%d" % t), ref("LQ")), F.Copy)
-        act(ref("E", 256, 512), ref("E", 0, 256), F.Copy)
-        act(ref("EM"), ref("E", 0, 256), F.Relu, bias=-510.0, scale=2.0)
+        copy(SMALL[0], ref("E", 256, 512), ref("E", 0, 256))
+        if SMALL[1] == "s":
+            act(ref("EM"), ref("E", 0, 256), F.Relu, bias=-255 * LIVE, scale=LIVE)
+        else:
+            ts(ref("EM"), ref("E", 0, 256), 255.5, A.is_gt, LIVE, A.mult)
         if t == 0:
-            ts(ref("PV"), ind(ref("pt"), ref("LU")), -960.0, A.add, 1.0 / 1024, A.mult)
+            ts(ref("PV"), ind(ref("pt"), ref("LU")), -1024.0, A.add)
             path_list()
-        old = B if t == 0 else B - S
         if HS[t]:
             hold_s(t, 0, HS[t], "M2b")
         for a in range(HS[t], old, HC):
             hold(t, a, min(old, a + HC), ["P1", "P2"] if HC > 512 or ((a - HS[t]) // HC) % 2 else ["P2"])
-        for k in range(15, -1, -1):
-            if k % 2:
-                if k == 1 and t:
-                    hold(t, old, B, ["M1"])
-                tt(ref("O", 256 * k - 256, 256 * k + 256), ind(ref("TT", 0, old if k > 1 else B), ref("PL", 16 * k - 16, 16 * k + 16)), ref("E"), A.subtract)
-            j = k % 8
-            mm(pq("P2" if k >= 8 else "P1", 0, 256), ref("PK", 16 - j, 144 - j), ref("O", 256 * k, 256 * k + 256), j == 7, j == 0)
-            if j == 0:
-                act(ref("F2" if k else "F1"), pq("P2" if k else "P1", 0, 256), F.Sign, bias=col(21))
-        group(pq("M0", 0, 256), [(NI, ref("EM")), (ref("U2"), ref("F2")), (ref("U1"), ref("F1"))])
-        group(pq("M1", 0, 256), [(ref("HB"), ref("F2")), (ref("HB"), ref("F1"))])
-        act(r3("OH"), pq("M0", 0, 256), F.Relu, bias=col(22), scale=512.0)
-        ts(lv, pq("M1", 0, 256), -15.0, A.is_lt, 256.0, A.mult)
-        act(ref("Y"), lv, F.Identity, acc=ref("cn", t, t + 1))
-        tt(r3("M"), r3("OH"), ref("PV"), A.mult)
+        for k in range(14, -1, -2):
+            if k == 0 and t:
+                hold(t, old, B, ["M1"])
+            tt(ref("O", 256 * k, 256 * k + 512), ind(ref("TT", 0, old if k else B), ref("PL", 16 * k, 16 * k + 32)), ref("E"), A.subtract)
+            bank = pq("P2" if k >= 8 else "P1", 0, 256)
+            mms([(bank, ref("PK", 16 - j % 8, 144 - j % 8), ref("O", 256 * j, 256 * j + 256), j % 8 == 7, j % 8 == 0) for j in (k + 1, k)])
+            if k % 8 == 0:
+                act(ref("F2" if k else "F1"), bank, F.Sign, bias=col(25))
+        group(pq("M2b", 0, 256), [(I_, ref("PV")), (NI, ref("EM")), (ref("U2"), ref("F2")), (ref("U1"), ref("F1"))], 3)
+        group(pq("M1", 0, 256), [(ref("HB"), ref("F2")), (ref("HB"), ref("F1"))], 1)
+        ts(r3("MT"), pq("M2b", 0, 256), col(26), A.add, -1088.0, A.max)
+        act(lv, pq("M1", 0, 256), F.Relu, bias=-7 * LIVE, scale=-LIVE / 2, acc=ref("cn", t, t + 1))
         hv = lambda nm: (lambda h: r3(nm, 0, 8, 16 * h, 16 * h + 16))
-        swapped("M2b", [("BS", 0)] * 3, [hv(lvn), hv("OH"), hv("M")], 8, first=(ref("ZR"), ref("IOT")))
-        BDm = ref("BD", 16, 144)
-        mm(pq("M0", 0, 512), I_, r3("CM"), True, False)
-        mm(pq("M0", 0, 256), BDm, r3("OH"), False, False)
-        mm(r3("M0", 8, 16, 0, 16), BDm, r3("OH", 0, 8, 0, 16), False, False)
-        mm(pq("M0", 0, 256), BDm, r3("M"), False, False)
-        mm(r3("M0", 8, 16, 0, 16), BDm, r3("M", 0, 8, 0, 16), False, True)
+        swapped("M2b", 8, [("BS", hv("MT")), ("BS", hv(lvn))], 2, halves)
+        mms([(r3("M0", 0, 8, 0, 48), I_, r3("CM"), True, False)])
+        mms([(r3("M0", 0, 8, 0, 32), BDm, r3("MT"), False, False), (r3("M0", 0, 8, 32, 48), BDm, r3("MT", 0, 8, 0, 16), False, True)])
         tr(r3("LR"), pq("M2b", 0, 256))
         L = r3("LR", 0, 8, 0, 32, 16)
-        ts(ref("GL"), L, -4096.0, A.add, 0.0, A.max)
-        tt(ref("NE", 0, 256), r3("LR"), pq("M0", 0, 256), A.not_equal)
-        tt(ref("NE", 256, 384), r3("LR", 0, 8, 16, 32), r3("M0", 8, 16, 0, 16), A.not_equal)
+        ts(ref("GL"), L, -OFF, A.add)
+        tt(ref("NE", 0, 128), r3("LR", 0, 8, 0, 16), r3("M0", 0, 8, 0, 16), A.not_equal)
+        tt(ref("NE", 128, 384, 2), r3("LR", 0, 8, 16, 32), r3("M0", 0, 8, 16, 32), A.not_equal)
+        tt(ref("NE", 129, 384, 2), r3("LR", 0, 8, 16, 32), r3("M0", 0, 8, 32, 48), A.not_equal)
         kp, rs, ne = ref("KP"), ref("RS"), ref("NE")
-        add("v", lambda kp=kp, rs=rs, ne=ne: g.vector.tensor_tensor_scan(kp["ap"], rs["ap"], ne["ap"], 0.0, A.max, A.mult), [kp], [rs, ne], 200 * CY)
-        tt(ref("vt"), ref("KP", 15, 256, 16), L, A.mult)
-        tt(ref("vo"), ref("vt", 1, 16, 2), ref("KP", 271, 384, 16), A.mult)
-        ts(ref("TL", 0, 16, 2), ref("vt", 0, 16, 2), -4096.0, A.add, pm, A.max)
-        ts(ref("TL", 1, 16, 2), ref("vo"), -4096.0, A.add, col(24), A.max)
+        add("v", lambda kp=kp, rs=rs, ne=ne: g.vector.tensor_tensor_scan(kp["ap"], rs["ap"], ne["ap"], 0.0, A.max, A.mult), [kp], [rs, ne], (0, 192, "cy"))
+        tt(ref("vt", 0, 8), ref("KP", 15, 128, 16), r3("LR", 0, 8, 0, 1), A.mult)
+        tt(ref("vt", 8, 16), ref("KP", 159, 384, 32), r3("LR", 0, 8, 16, 17), A.mult)
+        ts(ref("TL", 0, 16, 2), ref("vt", 0, 8), -OFF, A.add, pm, A.max)
+        ts(ref("TL", 1, 16, 2), ref("vt", 8, 16), -OFF, A.add, col(28), A.max)
         Xa = ref("X", 0, X0 + B)
         tt(ref("NV"), ind(Xa, ref("GL")), ref("E", 0, 256), A.max)
         for b in range(7, -1, -1):
@@ -404,17 +424,23 @@ def build(g, T, rank, core, topo):
         if not last:
             cp(ref("LU"), ref("LV"))
         group(pq("M1", 0, 256), [(I_, z), (NI, lv)])
-        act(ref("Y"), pq("M1", 0, 256), F.Relu, scale=-1.0)
-        act(ref("X", X0 + B, X0 + B + S), ref("Y"), F.Identity, bias=256.0, scale=-1.0)
-        group(pq("P2", 0, 256), [(ref("SH"), ref("PV")), (ref("TOP"), ref("IOT")), (ref("LW", 128 * t, 128 * t + 128), lv)])
+        if SMALL[2] == "s":
+            act(ref("Y"), pq("M1", 0, 256), F.Relu, scale=-1.0, bias=256.0 - LIVE)
+            act(ref("X", X0 + B, X0 + B + S), ref("Y"), F.Identity, bias=256.0, scale=-1.0)
+        else:
+            ts(ref("X", X0 + B, X0 + B + S), pq("M1", 0, 256), LIVE, A.add, 256.0, A.min)
+        group(pq("P2", 0, 256), [(ref("SH"), ref("PV")), (ref("TOP"), ref("IOT")), (I_, lv)])
         yp = ref("YP", S * t, S * t + S)
-        act(yp, pq("P2", 0, 256), F.Relu, bias=-3136.0)
-        dma(T.yp[:, S * t:S * t + S], yp, 131072, False)
+        act(yp, pq("P2", 0, 256), F.Relu, bias=col(36 + t))
+        dma(T.yp[:, S * t:S * t + S], yp, 131072)
+        yc = pq("P1", 0, 256, (0, 32))
         if not last:
-            act(ref("yq"), yp, F.Identity, bias=-0.9375, scale=1.0 / 1024)
-            group(pq("P1", 0, 256), [(I_, ref("PV")), (ref("NI64"), lv)])
+            act(ref("yq"), yp, F.Identity, bias=-1024.0)
+            group(pq("P1", 0, 256), [(I_, ref("PV")), (NI, lv)])
             tt(ref("PV"), pq("P1", 0, 256), ref("yq"), A.max)
             path_list()
+        else:
+            mms([(yc, ref("GT", 3 - r, 35 - r), ref("M2", S * r, S * r + S), r == 0, False) for r in range(t)])
         n = 0
         mv = MV[t]
         if mv < 16:
@@ -424,35 +450,33 @@ def build(g, T, rank, core, topo):
                 bank = "A%d" % (n & 1) if mv == 16 else "A0"
                 n += 1
                 m1 = min(mv, m0 + 4)
-                for m in range(m0, m1):
-                    o = pq(bank, 128 * (m - m0), 128 * (m - m0) + 128)
-                    group(o, [(I_, ref("z%d" % (t & 1), 128 * q, 128 * q + 128)), (NI, ref("XK", 2048 * q + m, 2048 * q + 2048, 16))])
+                mms([x for m in range(m0, m1) for x in chain(pq(bank, 128 * (m - m0), 128 * (m - m0) + 128), [
+                    (I_, ref("z%d" % (t & 1), 128 * q, 128 * q + 128)), (NI, ref("XK", 2048 * q + m, 2048 * q + 2048, 16))])])
                 a = 2048 * q + 128 * m0
                 act(ref("SG", a, a + 128 * (m1 - m0)), pq(bank, 0, 128 * (m1 - m0)), F.Sign, bias=0.5)
             for m in range(mv, 16):
                 a = 2048 * q + 128 * m
                 tt(ref("SG", a, a + 128), ref("XK", 2048 * q + m, 2048 * q + 2048, 16), pq("A1", 128 * q, 128 * q + 128), A.is_le)
-            for m in range(16):
-                a = 2048 * q + 128 * m
-                mm(pq("CB", 128 * q, 128 * q + 128), ref("BK", 16 - m, 144 - m), ref("SG", a, a + 128), m == 0, m == 15)
-        ts(ref("pi", t, t + 1), ref("cn", t, t + 1), 1.0 / 256, A.mult)
-        ts(ref("pj", t, t + 1), ref("pi", t, t + 1), 1, A.bitwise_and)
-        j = 36 + 2 * sorted(set(MV)).index(mv)
+            for m0 in range(0, 16, 4):
+                mms([(pq("CB", 128 * q, 128 * q + 128), ref("BK", 16 - m, 144 - m), ref("SG", 2048 * q + 128 * m, 2048 * q + 128 * m + 128), m == 0, m == 15)
+                     for m in range(m0, m0 + 4)])
+        cp(ref("pi", t, t + 1), ref("cn", t, t + 1))
+        ts(ref("pj", t, t + 1), ref("pi", t, t + 1), 12, A.arith_shift_right, 1, A.bitwise_and)
+        j = 44 + 2 * kinds.index(mv)
         ts(ref("pb", t, t + 1), ref("pj", t, t + 1), col(j), A.mult, col(j + 1), A.add)
         act(ref("FS"), pq("CB", 0, 256), F.Sign, bias=ref("pb", t, t + 1))
-        group(pq("A0", 0, 256), [(ref("I128"), lv), (ref("U0"), ref("FS"))])
-        act(ref("O2"), pq("A0", 0, 256), F.Relu, bias=col(23), scale=512.0)
-        act(pq("CB", 0, 256), pq("A0", 0, 256), F.Relu, bias=col(23), scale=512.0)
-        tt(ref("M2"), pq("CB", 0, 256), cs, A.mult)
+        group(pq("CB", 0, 256), [(ref("U0"), ref("FS")), (I_, lv), (I_, cs)])
+        ts(ref("M2", S * t, S * t + S), pq("CB", 0, 256), col(27), A.add, -1025.0, A.max)
         if not last:
-            group(r3("CB", 0, 1, 0, 16), [(ref("BK", 16 - i, 144 - i), ref(nm, i, 256, 16)) for nm in ("O2", "M2") for i in range(16)])
-            ts(ref("COV", B // 16, B // 16 + 16), r3("CB", 0, 1, 0, 16), 63.0, A.add)
-        group(pq("A0", 0, 256, (0, 8)), [(ref("G8"), ref("O2")), (ref("G8"), ref("M2"))])
-        act(ref("YC", S * t, S * t + S, parts=(0, 8)), pq("A0", 0, 256, (0, 8)), F.Identity, bias=-1.0)
-    dma(T.yx[:, 0:W - S], ref("X", X0, X0 + W - S), 720896, False)
-    dma(T.yx[:, W - S:W], ref("X", X0 + W - S, X0 + W), 65536, False)
-    dma(T.yv[:], ref("LV"), 8192, False)
-    dma(T.yc[:], ref("YC", parts=(0, 8)), 32768, False)
+            group(r3("CB", 0, 1, 0, 16), [(ref("BK", 16 - i, 144 - i), ref("M2", S * t + i, S * t + S, 16)) for i in range(16)])
+            ts(ref("COV", B // 16, B // 16 + 16), r3("CB", 0, 1, 0, 16), 16400.0 + 63.0, A.add)
+        else:
+            mms([(yc, ref("GT", 3 - t, 35 - t), ref("M2", S * t, S * t + S), False, True)])
+            act(ref("YC", parts=(0, 32)), yc, F.Identity, bias=16399.0)
+    dma(T.yx[:, 0:W - S], ref("X", X0, X0 + W - S), 720896)
+    dma(T.yx[:, W - S:W], ref("X", X0 + W - S, X0 + W), 65536)
+    dma(T.yv[:], ref("LV"), 8192)
+    dma(T.yc[:], ref("YC", parts=(0, 32)), 32768)
     return ops
 
 
@@ -463,39 +487,42 @@ def depend(ops):
         if "after" in o:
             d[o["after"]] = False
         for kind in ("R", "W"):
-            for (nm, lo, hi) in o[kind]:
+            for (nm, lo, hi, par) in o[kind]:
                 ps = nm in PS
-                for (j, k2, l2, h2) in seen.get(nm, []):
+                for (j, k2, l2, h2, p2) in seen.get(nm, []):
                     if j == o["id"]:
                         continue
                     same = ops[j]["e"] == o["e"]
                     if ps:
                         d[j] = d.get(j, False) or not same
-                    elif (kind == "W" or k2 == "W") and lo < h2 and l2 < hi:
+                    elif (kind == "W" or k2 == "W") and lo < h2 and l2 < hi and (par, p2) not in ((0, 1), (1, 0)):
                         d[j] = True
         o["d"] = d
         for kind in ("R", "W"):
-            for (nm, lo, hi) in o[kind]:
+            for (nm, lo, hi, par) in o[kind]:
                 lst = seen.setdefault(nm, [])
                 if nm in PS:
                     lst[:] = [x for x in lst if ops[x[0]]["e"] != o["e"]][-3:]
                 elif kind == "W":
-                    lst[:] = [x for x in lst if not (lo <= x[2] and x[3] <= hi)]
-                lst.append((o["id"], kind, lo, hi))
+                    lst[:] = [x for x in lst if not (lo <= x[2] and x[3] <= hi and par in (-1, x[4]))]
+                lst.append((o["id"], kind, lo, hi, par))
 
 
 def schedule(ops):
     n = len(ops)
-    succ = [[] for _ in ops]
-    for o in ops:
-        for j in o["d"]:
-            succ[j].append(o["id"])
-
     res = ["dma" if "nb" in o else o["e"] for o in ops]
-    dur = [o["nb"] / RATE + 60 if "nb" in o else o["c"] for o in ops]
-    tail = [LAT if "nb" in o else 0 for o in ops]
-    pred = [[(j, tail[j] + (HOP if w else 0)) for j, w in o["d"].items()] for o in ops]
-    post = [[(j, tail[i] + (HOP if ops[j]["d"][i] else 0)) for j in succ[i]] for i in range(n)]
+    sets = []
+    for m in SETS:
+        per = {"cy": m["cy"], "ga": m["cy"] * m["ga"], "sc": m["cy"] * m["sc"], "pe": m["pe"]}
+        dur = [o["nb"] / m["xr" if o.get("remote") else "rate"] + 60 if "nb" in o else o["c"][0] + o["c"][1] * per[o["c"][2]] for o in ops]
+        tail = [m["lat"] + (600 if o.get("remote") else 0) if "nb" in o else 0 for o in ops]
+        pred = [[(j, tail[j] + m["hop"] if w else tail[j] if o["e"] != "g" else -dur[j]) for j, w in o["d"].items()] for o in ops]
+        sets.append((dur, tail, pred))
+    dur, tail, pred = sets[0]
+    post = [[] for _ in ops]
+    for i in range(n):
+        for j, lag in pred[i]:
+            post[j].append((i, lag))
 
     def place(seq, before):
         st = [0.0] * n
@@ -516,6 +543,32 @@ def schedule(ops):
             b.insert(lo, (t, t + dur[i]))
             st[i] = t
         return st
+
+    que = ["vspgyx".index(o["e"]) for o in ops]
+    issue = [o["c"][0] if "nb" in o else -1 for o in ops]
+    ends = [i for i in range(n) if not post[i]]
+
+    def replay(seq, s, start=0, base=None):
+        du, ta, pr = s
+        k = start // 32
+        end, snaps = (base[1][:], base[2][:k + 1]) if base else ([0.0] * n, [[0.0] * 7])
+        free = snaps[k][:]
+        for a in range(32 * k, n, 32):
+            for i in seq[a:a + 32]:
+                e = que[i]
+                t = free[e]
+                for j, lag in pr[i]:
+                    x = end[j] + lag
+                    if x > t:
+                        t = x
+                if issue[i] >= 0:
+                    free[e] = t + issue[i]
+                    e = 6
+                    if free[6] > t:
+                        t = free[6]
+                end[i] = free[e] = t + du[i]
+            snaps.append(free[:])
+        return max(end[i] + ta[i] for i in ends), end, snaps
 
     seed = [12345]
 
@@ -546,7 +599,8 @@ def schedule(ops):
     def both(key):
         back = place(topo_by(key, post, pred), post)
         st = place(topo_by([-(back[i] + dur[i]) for i in range(n)], pred, post), pred)
-        return max(st[i] + dur[i] + tail[i] for i in range(n)), st
+        seq = topo_by(st, pred, post)
+        return sum(replay(seq, s)[0] for s in sets) / len(sets), st, seq
 
     best = both([-float(i) for i in range(n)])
     cur = best
@@ -561,10 +615,71 @@ def schedule(ops):
             cur = new
         if new[0] < best[0]:
             best = new
-    st = best[1]
-    for i, o in enumerate(ops):
-        o["t"], o["f"] = st[i], st[i] + dur[i] + tail[i]
-    return [ops[i] for i in topo_by(st, pred, post)]
+
+    def critical(seq, du, ta, pr):
+        end, why, free, last = [0.0] * n, [-1] * n, {}, {}
+        for i in seq:
+            e = ops[i]["e"]
+            t, w = free.get(e, 0.0), (last.get(e, -1), True)
+            for j, lag in pr[i]:
+                if end[j] + lag > t:
+                    t, w = end[j] + lag, (j, False)
+            last[e] = i
+            if res[i] == "dma":
+                free[e] = t + ops[i]["c"][0]
+                if free.get("dma", 0.0) > t:
+                    t, w = free["dma"], (last["dma"], True)
+                last["dma"] = i
+            end[i] = free[res[i]] = t + du[i]
+            why[i] = w
+        i = max(range(n), key=lambda k: end[k] + ta[k])
+        out = []
+        while i >= 0:
+            if why[i][1] and why[i][0] >= 0:
+                out.append((why[i][0], i))
+            i = why[i][0]
+        return out
+
+    seq, now = best[2], best[0]
+    base = [replay(seq, s) for s in sets]
+    best = (now, seq)
+    crit = []
+    for it in range(MOVES):
+        if not crit:
+            crit = critical(seq, *sets[int(len(sets) * rnd())])
+        u, v = crit[int(len(crit) * rnd())]
+        pu, pv = seq.index(u), seq.index(v)
+        if rnd() < 0.5:
+            for _ in range(int(4 * rnd() ** 2)):
+                q = pu - 1
+                while q >= 0 and res[seq[q]] != res[v]:
+                    q -= 1
+                pu = max(q, 0)
+            need = {v}
+            for q in range(pv, pu - 1, -1):
+                if seq[q] in need:
+                    need.update(j for j, lag in pred[seq[q]])
+            mid = seq[pu:pv + 1]
+            new = seq[:pu] + [i for i in mid if i in need] + [i for i in mid if i not in need] + seq[pv + 1:]
+        else:
+            for _ in range(int(6 * rnd() ** 2)):
+                q = pv + 1
+                while q < n and res[seq[q]] != res[u]:
+                    q += 1
+                pv = min(q, n - 1)
+            need = {u}
+            for q in range(pu, pv + 1):
+                if seq[q] in need:
+                    need.update(j for j, lag in post[seq[q]])
+            mid = seq[pu:pv + 1]
+            new = seq[:pu] + [i for i in mid if i not in need] + [i for i in mid if i in need] + seq[pv + 1:]
+        got = [replay(new, s, pu, b) for s, b in zip(sets, base)]
+        c = sum(x[0] for x in got) / len(sets)
+        if c <= now + HEAT * (1.0 - it / MOVES) * rnd():
+            seq, now, crit, base = new, c, [], got
+            if c < best[0]:
+                best = (c, seq)
+    return [ops[i] for i in best[1]]
 
 
 def rank_program(g, core, T, topo):

@@ -4,44 +4,49 @@ A = AluOpType
 F = ActivationFunctionType
 B0, S, RO, W = 2048, 256, 4, 3072
 JUMPS = [1, 2, 3, 1]
-X0 = 64
+X0 = 80
 C0 = 98560.5
 K2 = 2048.0
 LIVE = 4096.0
-OFF = 16 * LIVE - 16 * 1088
+NONE = 1024.0 + X0
+BIG = 12582912.0
+LOFF = 16 * LIVE - 1024
+NH = 4
+RUN = [256 // NH * h * (h + 1) // 2 for h in range(NH + 1)]
 bf, f32, i32, u16, f16 = "bfloat16", "float32", "int32", "uint16", "float16"
 SB = {
     "X": ([X0 + W], bf), "XA": ([W - S], bf), "XB": ([W - S], bf), "xr0": ([2048], bf), "xr1": ([2304], bf), "xr2": ([2560], bf), "xr3": ([2816], bf),
     "TT": ([2816], f32), "pt": ([2048], i32), "ac": ([1024], bf), "cv": ([128], i32), "wt": ([16], i32), "lf": ([16], i32),
-    "O": ([4096], bf), "XK": ([4096], bf), "SG": ([4096], bf), "C": ([2816], bf), "YP": ([1024], f32), "YC": ([256], f32),
+    "O": ([4096], bf), "OG": ([2048], f32), "XK": ([4096], bf), "SG": ([4096], bf), "C": ([2816], bf), "YP": ([1024], f32), "YC": ([256], f32),
     "COV": ([192], u16), "PL": ([256], u16), "LU": ([16], u16), "LV": ([16], f32), "PV": ([256], f16),
     "xv": ([256], bf), "av": ([256], bf), "z0": ([256], bf), "z1": ([256], bf), "E": ([512], bf), "EM": ([256], bf),
     "tx": ([128], f32), "hi": ([32], i32), "ha": ([32], i32), "LA": ([16], u16), "LQ": ([16], u16), "hp": ([2], u16),
-    "ci": ([256], i32), "cj": ([256], i32), "CL": ([256], u16), "cs0": ([256], f16), "cs1": ([256], f16),
-    "F1": ([256], bf), "F2": ([256], bf), "lv0": ([8, 32], bf), "lv1": ([8, 32], bf), "MT": ([8, 32], f16),
-    "LR": ([8, 32], f32), "NE": ([384], bf), "KP": ([384], bf), "RS": ([384], bf), "vt": ([16], f32), "vo": ([8], f32), "GL": ([16], u16),
+    "cq": ([256], f16), "NH": ([128], bf), "HF": ([256], bf), "k4": ([128], bf), "LO": ([16], f32), "I16": ([64], f16), "py": ([4], bf), "CL": ([256], u16), "cs0": ([256], f16), "cs1": ([256], f16),
+    "F1": ([256], bf), "F2": ([256], bf), "lv0": ([16, 16], bf), "lv1": ([16, 16], bf), "MT": ([16, 16], f16),
+    "LR": ([16, 16], f32), "NE": ([RUN[NH]], bf), "KP": ([RUN[NH]], bf), "RS": ([RUN[NH]], bf), "vt": ([16], f32), "GL": ([16], u16),
     "TL": ([16], u16), "NV": ([256], bf), "la": ([16], f32), "Y": ([256], bf), "yq": ([256], f32), "tp": ([256], f32),
-    "cn": ([4], f32), "pi": ([4], i32), "pj": ([4], i32), "pb": ([4], f32), "FS": ([256], bf), "M2": ([1024], f16),
+    "cn": ([4], f32), "pi": ([4], f32), "pb": ([4], f32), "FS": ([256], bf), "M2": ([1024], f16),
     "KEY": ([160], bf), "k1": ([128], bf), "k2": ([160], bf), "k3": ([128], bf), "SI": ([128], bf),
-    "pc": ([4], i32), "pd": ([10], i32), "col": ([52], f32), "XC": ([512], bf), "SB2": ([128], bf), "IL": ([64], f32), "io16": ([16], f32), "IOT": ([256], bf),
-    "SM": ([8, 32], bf), "I": ([160], bf), "NI": ([128], bf), "BD": ([160], bf), "SBD": ([128], bf),
+    "pc": ([4], i32), "pd": ([10], i32), "col": ([64], f32), "XC": ([512], bf), "SB2": ([128], bf), "IL": ([64], f32), "io16": ([16], f32), "IOT": ([256], bf),
+    "SM": ([256], bf), "I": ([160], bf), "NI": ([128], bf), "BD": ([160], bf), "SBD": ([128], bf),
     "BK": ([160], bf), "PK": ([160], bf), "U0": ([128], bf), "U1": ([128], bf), "U2": ([128], bf), "HB": ([128], bf),
     "SH": ([128], bf), "TOP": ([128], bf), "BS": ([320], bf), "IS": ([320], bf), "ZW": ([320], f16),
-    "WB": ([128], f16), "GT": ([36], bf), "CM": ([8, 48], bf), "wa": ([16], f32), "wf": ([16], f32),
+    "WB": ([128], f16), "GT": ([36], bf), "CM": ([256], bf), "wa": ([16], f32), "wf": ([16], f32),
     "wl": ([8], u16), "p1": ([16], u16), "p2": ([8], u16), "c16": ([128], f16), "tc": ([128], f32),
 }
-PS = {"A0": [16, 32], "A1": [16, 32], "CB": [16, 32], "P1": [16, 32], "P2": [16, 32], "M0": [8, 64], "M1": [16, 32], "M2b": [16, 32]}
+PS = {"A0": [16, 32], "A1": [16, 32], "CB": [16, 32], "P1": [16, 32], "P2": [16, 32], "M0": [32, 16], "M1": [16, 32], "M2b": [16, 32]}
 SCRATCH = {k: ("sbuf", [128] + v[0], v[1]) for k, v in SB.items()}
 SCRATCH.update({k: ("psum", [128] + v, f32) for k, v in PS.items()})
 NDMA = 40
 SEMAPHORES = ["v", "s", "p", "g"] + ["d%d" % i for i in range(NDMA)] + ["arr%d" % t for t in range(RO)] + ["snt%d" % t for t in range(RO)]
-SETS = [dict(cy=0.9, ga=1.56, sc=3.8, pe=0.47, hop=200.0, rate=250.0, xr=170.0, lat=1300.0),
-        dict(cy=1.04, ga=1.56, sc=3.8, pe=0.53, hop=110.0, rate=300.0, xr=200.0, lat=1100.0),
-        dict(cy=1.15, ga=1.85, sc=5.0, pe=0.62, hop=280.0, rate=200.0, xr=130.0, lat=1500.0)]
-PASSES, MOVES, HEAT = 300, 40000, 60.0
+SETS = [dict(cy=0.86, ga=1.56, sc=3.8, pe=0.44, hop=210.0, rate=300.0, xr=270.0, lat=1200.0),
+        dict(cy=1.0, ga=1.45, sc=3.3, pe=0.52, hop=170.0, rate=270.0, xr=190.0, lat=1300.0),
+        dict(cy=1.17, ga=1.85, sc=5.0, pe=0.62, hop=280.0, rate=250.0, xr=170.0, lat=1500.0)]
+PASSES, MOVES, HEAT, REACH = 100, 40000, 400.0, 12
 COPY = ["svsv", "vvggg", "vvggg", "vvgggg"]
-MV = [8, 8, 8, 8]
+MV = [8, 8, 8, 4]
 XE = ["ssssssss"] * 4
+OS = [3, 3, 3, 3]
 HS = [0, 0, 0, 0]
 SMALL = "vvss"
 LATE = ("U0", "RS", "CM", "SM", "IOT", "GT")
@@ -59,10 +64,10 @@ def build(g, T, rank, core, topo):
         lo = 0 if lo is None else lo
         hi = n if hi is None else hi
         p = slice(0, 128) if parts is None else slice(parts[0], parts[1])
-        return {"ap": T[name][p, lo:hi:step] if step != 1 else T[name][p, lo:hi], "rg": [(name, lo, hi, lo % 2 if step == 2 else -1)],
+        return {"ap": T[name][p, lo:hi:step] if step != 1 else T[name][p, lo:hi], "rg": [(name, lo, hi, (step, lo % step))],
                 "n": len(range(lo, hi, step)), "two": SB[name][1] in (bf, u16, f16), "ps": False, "ind": False}
 
-    def r3(name, a0=None, a1=None, b0=None, b1=None, step=1, parts=None):
+    def r3(name, a0=None, a1=None, b0=None, b1=None, step=1, parts=None, step0=1):
         ps = name in PS
         sh = PS[name] if ps else SB[name][0]
         a0 = 0 if a0 is None else a0
@@ -70,8 +75,8 @@ def build(g, T, rank, core, topo):
         b0 = 0 if b0 is None else b0
         b1 = sh[1] if b1 is None else b1
         p = slice(0, 128) if parts is None else slice(parts[0], parts[1])
-        ap = T[name][p, a0:a1, b0:b1:step] if step != 1 else T[name][p, a0:a1, b0:b1]
-        return {"ap": ap, "rg": [(name, a0 * sh[1] + b0, (a1 - 1) * sh[1] + b1, -1)], "n": (a1 - a0) * len(range(b0, b1, step)),
+        ap = T[name][p, a0:a1:step0, b0:b1:step]
+        return {"ap": ap, "rg": [(name, a0 * sh[1] + b0, (a1 - 1) * sh[1] + b1, (1, 0))], "n": len(range(a0, a1, step0)) * len(range(b0, b1, step)),
                 "two": (not ps) and SB[name][1] in (bf, u16, f16), "ps": ps, "ind": False}
 
     def pq(name, lo, hi, parts=None):
@@ -218,7 +223,7 @@ def build(g, T, rank, core, topo):
     sel(ref("KEY"), ref("KEY"), [[16, 10], [0, 16]], A.is_ge, 0.0, -1, -1)
     iota(ref("io16"), [[1, 16]], 0, 0)
     iota(ref("IL"), [[16, 64]], B0, 1)
-    iota(r3("SM"), [[0, 16], [1, 16]], 0, 0)
+    iota(ref("SM"), [[0, 16], [1, 16]], 0, 0)
     iota(ref("IOT"), [[1, 256]], 0, 0)
     iota(ref("X", 0, X0), [[0, X0]], 300, 0)
     p = ref("pc", 0, 1)
@@ -251,7 +256,10 @@ def build(g, T, rank, core, topo):
     ts(ref("pd", 9, 10), ref("wt", 0, 1), 1023, A.bitwise_and)
     ts(col(11), ref("pd", 9, 10), 4.0, A.mult)
     ts(ref("wl"), ref("io16", 0, 8), 0.0, A.mult, pm, A.add)
-    tt(ref("WB"), ind(ref("wf"), ref("wl")), BDm, A.mult)
+    ts(ref("k4"), BDm, 1.0 / 4096, A.mult)
+    tt(ref("WB"), ind(ref("wf"), ref("wl")), ref("k4"), A.mult)
+    ts(ref("NH"), I_, -63.0 / 64, A.mult)
+    ts(ref("HF"), ref("ac", 0, 256), 0.0, A.mult, 65.0 / 128, A.add)
     ms(ref("ZW"), 0.0)
     for c in range(2):
         ts(col(12 + c), half[1 - c], 100.0, A.mult, pr, A.add)
@@ -261,8 +269,8 @@ def build(g, T, rank, core, topo):
     ts(col(15), hi4, 2.0, A.mult, col(14), A.add)
     ts(ref("hp"), ref("io16", 0, 2), col(15), A.add)
     cp(ref("LU"), ref("lf"))
-    cp(ref("LV"), ref("lf"))
-    ts(ref("c16"), ref("cv"), -960.0, A.add)
+    ts(ref("LO"), ref("lf"), LOFF, A.add)
+    ts(ref("c16"), ref("cv"), X0 - 1024.0, A.add)
     swapped("M1", 4, [("IS", lambda h: ref("c16", 64 * h, 64 * h + 64))], 2, halves)
     tr(ref("tc"), pq("M1", 0, 128))
     ts(col(16), up, col(14), A.add)
@@ -279,9 +287,10 @@ def build(g, T, rank, core, topo):
     kinds = sorted(set(MV))
     for j, mv in enumerate(kinds):
         ts(col(22), pm, mv - 0.5, A.is_ge)
-        ts(col(44 + 2 * j), col(22), 1.0, A.mult, -2.0, A.add)
-        ts(col(45 + 2 * j), col(22), -4.5, A.mult, -7.0, A.add)
-    for nm in ("BK", "PK", "GT", "RS"):
+        ts(col(52 + 3 * j), col(22), 1.0 / LIVE, A.mult, -2.0 / LIVE, A.add)
+        ts(col(53 + 3 * j), col(22), 251.5, A.mult, -519.0, A.add)
+        ts(col(54 + 3 * j), col(22), -2.0, A.mult, 4.0, A.add)
+    for nm in ("BK", "PK", "GT"):
         iota(ref(nm), [[0, SB[nm][0][0]]], 0, 0)
     ts(ref("BK", 16, 144, 16), ref("io16", 0, 8), cg, A.is_equal)
     ts(ref("PK", 16, 144, 16), ref("BK", 16, 144, 16), -1.0, A.mult)
@@ -293,7 +302,6 @@ def build(g, T, rank, core, topo):
     ts(col(25), up, -188416.0 - 1577216.0, A.mult, 1577216.0, A.add)
     ts(col(26), pm, -K2, A.mult, -17 * K2, A.add)
     ts(col(27), pm, -K2, A.mult, -K2 - LIVE, A.add)
-    ts(col(28), pm, 16.0, A.add)
     ts(ref("k1"), BDm, -K2, A.mult)
     sel(ref("U0"), ref("k1"), [[1, 128]], A.is_gt, 0.0, 0, -1)
     sel(ref("U0"), ref("U0"), [[1, 128]], A.not_equal, K2, 0, -1)
@@ -310,12 +318,14 @@ def build(g, T, rank, core, topo):
     ts(ref("TOP"), I_, col(34), A.mult)
     for t in range(RO):
         ts(col(36 + t), col(34), B0 + S * t - 1024.0, A.mult, 1024.0 - LIVE, A.add)
-    ts(r3("CM", 0, 8, 0, 32), r3("SM"), pm, A.is_lt, 16 * LIVE, A.mult)
-    iota(r3("CM", 0, 8, 32, 48), [[0, 128]], int(16 * LIVE), 0)
-    iota(ref("RS", 0, 128, 16), [[0, 8]], 1, 0)
-    iota(ref("RS", 128, 384, 32), [[0, 8]], 1, 0)
-    ts(col(40), cg, -16.0, A.mult)
-    ts(ref("IL"), ref("IL"), col(40), A.add)
+    ts(ref("CM"), ref("SM"), pm, A.is_ge, 65536.0, A.mult)
+    iota(ref("RS"), [[0, RUN[NH]]], 1, 0)
+    for h in range(NH):
+        iota(ref("RS", RUN[h], RUN[h + 1], 16 * h + 16), [[0, 16 // NH]], 0, 0)
+        iota(ref("RS", RUN[h] + 16 * h + 15, RUN[h + 1], 16 * h + 16), [[0, 16 // NH]], 32768, 0)
+        ts(col(48 + h), pm, 16.0 * h, A.add)
+    ts(col(40), cg, -16.0, A.mult, -1024.0, A.add)
+    ts(ref("I16"), ref("IL"), col(40), A.add)
     early[0] = False
 
     def path_list():
@@ -367,10 +377,11 @@ def build(g, T, rank, core, topo):
         act(ref("av"), ind(ref("ac"), ref("LA")), F.Copy)
         group(pq("M0", 0, 256), [(I_, ref("xv")), (NI, ref("av"))])
         act(z, pq("M0", 0, 256), F.Abs)
-        group(pq("M2b", 0, 256), [(ref("WB"), z)])
-        cp(ref("ci"), pq("M2b", 0, 256))
-        ts(ref("cj"), ref("ci"), 4095, A.bitwise_and)
-        ts(ref("CL"), ref("cj"), fr, A.mult, -15.0 / 32, A.add)
+        hs = [(ref("NH"), ref("HF")), (ref("WB"), z)]
+        group(pq("M2b", 0, 256), hs, 1)
+        ts(ref("cq"), pq("M2b", 0, 256), BIG, A.add, BIG, A.subtract)
+        group(pq("M2b", 0, 256), hs + [(NI, ref("cq"))])
+        ts(ref("CL"), pq("M2b", 0, 256), float(B), A.mult, B * 4095 / 8192.0 - 15.0 / 32, A.add)
         ts(cs, ref("CL"), -1024.0, A.add)
         for a in range(0, 4096, CG):
             copy(XE[t][a // CG], ref("XK", a, a + CG), ind(ref(snap, 0, B), ref("CL", a // 16, (a + CG) // 16)))
@@ -387,42 +398,50 @@ def build(g, T, rank, core, topo):
             hold_s(t, 0, HS[t], "M2b")
         for a in range(HS[t], old, HC):
             hold(t, a, min(old, a + HC), ["P1", "P2"] if HC > 512 or ((a - HS[t]) // HC) % 2 else ["P2"])
-        for k in range(14, -1, -2):
+        if OS[t]:
+            mms([(pq("M0", a, a + 256), I_, ref("E", 0, 256), True, True) for a in (0, 256)])
+        for n, k in enumerate([8, 10, 12, 14, 6, 4, 2, 0]):
             if k == 0 and t:
                 hold(t, old, B, ["M1"])
-            tt(ref("O", 256 * k, 256 * k + 512), ind(ref("TT", 0, old if k else B), ref("PL", 16 * k, 16 * k + 32)), ref("E"), A.subtract)
+            o, src = ref("O", 256 * k, 256 * k + 512), ind(ref("TT", 0, old if k else B), ref("PL", 16 * k, 16 * k + 32))
+            if k >= 16 - 2 * OS[t]:
+                act(ref("OG", 256 * k - 2048, 256 * k - 1536), src, F.Copy)
+                tt(o, ref("OG", 256 * k - 2048, 256 * k - 1536), pq("M0", 0, 512), A.subtract)
+            else:
+                tt(o, src, ref("E"), A.subtract)
             bank = pq("P2" if k >= 8 else "P1", 0, 256)
-            mms([(bank, ref("PK", 16 - j % 8, 144 - j % 8), ref("O", 256 * j, 256 * j + 256), j % 8 == 7, j % 8 == 0) for j in (k + 1, k)])
-            if k % 8 == 0:
+            mms([(bank, ref("PK", 16 - j % 8, 144 - j % 8), ref("O", 256 * j, 256 * j + 256), n % 4 == 0 and j > k, n % 4 == 3 and j == k) for j in (k + 1, k)])
+            if n % 4 == 3:
                 act(ref("F2" if k else "F1"), bank, F.Sign, bias=col(25))
         group(pq("M2b", 0, 256), [(I_, ref("PV")), (NI, ref("EM")), (ref("U2"), ref("F2")), (ref("U1"), ref("F1"))], 3)
         group(pq("M1", 0, 256), [(ref("HB"), ref("F2")), (ref("HB"), ref("F1"))], 1)
-        ts(r3("MT"), pq("M2b", 0, 256), col(26), A.add, -1088.0, A.max)
+        ts(r3("MT"), pq("M2b", 0, 256), col(26), A.add, -NONE, A.max)
         act(lv, pq("M1", 0, 256), F.Relu, bias=-7 * LIVE, scale=-LIVE / 2, acc=ref("cn", t, t + 1))
-        hv = lambda nm: (lambda h: r3(nm, 0, 8, 16 * h, 16 * h + 16))
-        swapped("M2b", 8, [("BS", hv("MT")), ("BS", hv(lvn))], 2, halves)
-        mms([(r3("M0", 0, 8, 0, 48), I_, r3("CM"), True, False)])
-        mms([(r3("M0", 0, 8, 0, 32), BDm, r3("MT"), False, False), (r3("M0", 0, 8, 32, 48), BDm, r3("MT", 0, 8, 0, 16), False, True)])
+        swapped("M2b", 8, [("BS", lambda h: r3("MT", h, 16, step0=2))], 2, halves)
+        group(r3("M0", 0, 16), [(I_, ref("CM")), (BDm, r3("MT"))], 1)
+        group(r3("M0", 16, 32), [(BDm, r3("MT"))])
         tr(r3("LR"), pq("M2b", 0, 256))
-        L = r3("LR", 0, 8, 0, 32, 16)
-        ts(ref("GL"), L, -OFF, A.add)
-        tt(ref("NE", 0, 128), r3("LR", 0, 8, 0, 16), r3("M0", 0, 8, 0, 16), A.not_equal)
-        tt(ref("NE", 128, 384, 2), r3("LR", 0, 8, 16, 32), r3("M0", 0, 8, 16, 32), A.not_equal)
-        tt(ref("NE", 129, 384, 2), r3("LR", 0, 8, 16, 32), r3("M0", 0, 8, 32, 48), A.not_equal)
+        ts(ref("GL"), r3("LR", 0, 16, 0, 1), 16 * NONE, A.add)
+        for h in range(NH):
+            for d in range(h + 1):
+                tt(ref("NE", RUN[h] + d, RUN[h + 1], h + 1), r3("LR", h, 16, step0=NH), r3("M0", h, 16, step0=NH) if d == h else r3("M0", 16 + d, 32, step0=NH), A.is_equal)
         kp, rs, ne = ref("KP"), ref("RS"), ref("NE")
-        add("v", lambda kp=kp, rs=rs, ne=ne: g.vector.tensor_tensor_scan(kp["ap"], rs["ap"], ne["ap"], 0.0, A.max, A.mult), [kp], [rs, ne], (0, 192, "cy"))
-        tt(ref("vt", 0, 8), ref("KP", 15, 128, 16), r3("LR", 0, 8, 0, 1), A.mult)
-        tt(ref("vt", 8, 16), ref("KP", 159, 384, 32), r3("LR", 0, 8, 16, 17), A.mult)
-        ts(ref("TL", 0, 16, 2), ref("vt", 0, 8), -OFF, A.add, pm, A.max)
-        ts(ref("TL", 1, 16, 2), ref("vt", 8, 16), -OFF, A.add, col(28), A.max)
+        add("v", lambda kp=kp, rs=rs, ne=ne: g.vector.tensor_tensor_scan(kp["ap"], rs["ap"], ne["ap"], 0.0, A.mult, A.subtract), [kp], [rs, ne], (0, RUN[NH] // 2, "cy"))
+        nb = 16 // NH
+        for h in range(NH):
+            tt(ref("vt", nb * h, nb * h + nb), ref("KP", RUN[h] + 16 * h + 15, RUN[h + 1], 16 * h + 16), r3("LR", h, 16, 0, 1, step0=NH), A.min)
+        for h in range(NH):
+            ts(ref("TL", h, 16, NH), ref("vt", nb * h, nb * h + nb), 16 * NONE, A.add, col(48 + h), A.max)
         Xa = ref("X", 0, X0 + B)
         tt(ref("NV"), ind(Xa, ref("GL")), ref("E", 0, 256), A.max)
-        for b in range(7, -1, -1):
-            cp(ind(Xa, ref("TL", 2 * b, 2 * b + 2)), ref("NV", 32 * b, 32 * b + 32))
-        tt(ref("la"), L, ref("IL", 16 * t, 16 * t + 16), A.min)
-        tt(ref("LV"), ref("LV"), ref("la"), A.max)
+        for b in range(nb - 1, -1, -1):
+            cp(ind(Xa, ref("TL", NH * b, NH * b + NH)), ref("NV", 16 * NH * b, 16 * NH * (b + 1)))
+        group(r3("P1", 0, 1, 0, 16), [(I_, ref("I16", 16 * t, 16 * t + 16))] + [(ref("BK", 16 - i, 144 - i), r3(lvn, 0, 16, i, i + 1)) for i in range(16)])
+        tt(ref("LO"), r3("P1", 0, 1, 0, 16), ref("LO"), A.max)
         if not last:
-            cp(ref("LU"), ref("LV"))
+            ts(ref("LU"), ref("LO"), -LOFF, A.add)
+        else:
+            act(ref("LV"), ref("LO"), F.Identity, bias=-LOFF)
         group(pq("M1", 0, 256), [(I_, z), (NI, lv)])
         if SMALL[2] == "s":
             act(ref("Y"), pq("M1", 0, 256), F.Relu, scale=-1.0, bias=256.0 - LIVE)
@@ -460,16 +479,16 @@ def build(g, T, rank, core, topo):
             for m0 in range(0, 16, 4):
                 mms([(pq("CB", 128 * q, 128 * q + 128), ref("BK", 16 - m, 144 - m), ref("SG", 2048 * q + 128 * m, 2048 * q + 128 * m + 128), m == 0, m == 15)
                      for m in range(m0, m0 + 4)])
-        cp(ref("pi", t, t + 1), ref("cn", t, t + 1))
-        ts(ref("pj", t, t + 1), ref("pi", t, t + 1), 12, A.arith_shift_right, 1, A.bitwise_and)
-        j = 44 + 2 * kinds.index(mv)
-        ts(ref("pb", t, t + 1), ref("pj", t, t + 1), col(j), A.mult, col(j + 1), A.add)
+        j = 52 + 3 * kinds.index(mv)
+        act(ref("py", t, t + 1), ref("cn", t, t + 1), F.Identity, bias=127.75, scale=0.5 / LIVE)
+        act(ref("pi", t, t + 1), ref("cn", t, t + 1), F.Identity, bias=col(j + 1), scale=col(j))
+        act(ref("pb", t, t + 1), ref("py", t, t + 1), F.Identity, bias=ref("pi", t, t + 1), scale=col(j + 2))
         act(ref("FS"), pq("CB", 0, 256), F.Sign, bias=ref("pb", t, t + 1))
         group(pq("CB", 0, 256), [(ref("U0"), ref("FS")), (I_, lv), (I_, cs)])
         ts(ref("M2", S * t, S * t + S), pq("CB", 0, 256), col(27), A.add, -1025.0, A.max)
         if not last:
             group(r3("CB", 0, 1, 0, 16), [(ref("BK", 16 - i, 144 - i), ref("M2", S * t + i, S * t + S, 16)) for i in range(16)])
-            ts(ref("COV", B // 16, B // 16 + 16), r3("CB", 0, 1, 0, 16), 16400.0 + 63.0, A.add)
+            ts(ref("COV", B // 16, B // 16 + 16), r3("CB", 0, 1, 0, 16), 16399.0 + X0, A.add)
         else:
             mms([(yc, ref("GT", 3 - t, 35 - t), ref("M2", S * t, S * t + S), False, True)])
             act(ref("YC", parts=(0, 32)), yc, F.Identity, bias=16399.0)
@@ -495,7 +514,7 @@ def depend(ops):
                     same = ops[j]["e"] == o["e"]
                     if ps:
                         d[j] = d.get(j, False) or not same
-                    elif (kind == "W" or k2 == "W") and lo < h2 and l2 < hi and (par, p2) not in ((0, 1), (1, 0)):
+                    elif (kind == "W" or k2 == "W") and lo < h2 and l2 < hi and (par[0] != p2[0] or par == p2):
                         d[j] = True
         o["d"] = d
         for kind in ("R", "W"):
@@ -504,7 +523,7 @@ def depend(ops):
                 if nm in PS:
                     lst[:] = [x for x in lst if ops[x[0]]["e"] != o["e"]][-3:]
                 elif kind == "W":
-                    lst[:] = [x for x in lst if not (lo <= x[2] and x[3] <= hi and par in (-1, x[4]))]
+                    lst[:] = [x for x in lst if not (lo <= x[2] and x[3] <= hi and par in ((1, 0), x[4]))]
                 lst.append((o["id"], kind, lo, hi, par))
 
 
@@ -650,7 +669,7 @@ def schedule(ops):
         u, v = crit[int(len(crit) * rnd())]
         pu, pv = seq.index(u), seq.index(v)
         if rnd() < 0.5:
-            for _ in range(int(4 * rnd() ** 2)):
+            for _ in range(int(REACH * rnd() ** 2)):
                 q = pu - 1
                 while q >= 0 and res[seq[q]] != res[v]:
                     q -= 1
@@ -662,7 +681,7 @@ def schedule(ops):
             mid = seq[pu:pv + 1]
             new = seq[:pu] + [i for i in mid if i in need] + [i for i in mid if i not in need] + seq[pv + 1:]
         else:
-            for _ in range(int(6 * rnd() ** 2)):
+            for _ in range(int(REACH * rnd() ** 2)):
                 q = pv + 1
                 while q < n and res[seq[q]] != res[u]:
                     q += 1

@@ -1,14 +1,16 @@
+import math
 from concourse.mybir import AluOpType, ActivationFunctionType
 
 A = AluOpType
 F = ActivationFunctionType
 B0, S, RO, W = 2048, 256, 4, 3072
 JUMPS = [1, 2, 3, 1]
-X0 = 80
+X0 = 144
 C0 = 98560.5
 K2 = 2048.0
 LIVE = 4096.0
-NONE = 1024.0 + X0
+NOT = 128
+NONE = 1024.0 + X0 - NOT
 BIG = 12582912.0
 LOFF = 16 * LIVE - 1024
 NH = 4
@@ -17,42 +19,58 @@ bf, f32, i32, u16, f16 = "bfloat16", "float32", "int32", "uint16", "float16"
 SB = {
     "X": ([X0 + W], bf), "XA": ([W - S], bf), "XB": ([W - S], bf), "xr0": ([2048], bf), "xr1": ([2304], bf), "xr2": ([2560], bf), "xr3": ([2816], bf),
     "TT": ([2816], f32), "pt": ([2048], i32), "ac": ([1024], bf), "cv": ([128], i32), "wt": ([16], i32), "lf": ([16], i32),
-    "O": ([4096], bf), "OG": ([2048], f32), "XK": ([4096], bf), "SG": ([4096], bf), "C": ([2816], bf), "YP": ([1024], f32), "YC": ([256], f32),
+    "O": ([4096], bf), "OG": ([4096], f32), "XK": ([4096], bf), "SG": ([4096], bf), "C": ([2816], bf), "YP": ([1024], f32), "YC": ([256], f32),
     "COV": ([192], u16), "PL": ([256], u16), "LU": ([16], u16), "LV": ([16], f32), "PV": ([256], f16),
     "xv": ([256], bf), "av": ([256], bf), "z0": ([256], bf), "z1": ([256], bf), "E": ([512], bf), "EM": ([256], bf),
     "tx": ([128], f32), "hi": ([32], i32), "ha": ([32], i32), "LA": ([16], u16), "LQ": ([16], u16), "hp": ([2], u16),
     "cq": ([256], f16), "NH": ([128], bf), "HF": ([256], bf), "k4": ([128], bf), "LO": ([16], f32), "I16": ([64], f16), "py": ([4], bf), "CL": ([256], u16), "cs0": ([256], f16), "cs1": ([256], f16),
     "F1": ([256], bf), "F2": ([256], bf), "lv0": ([16, 16], bf), "lv1": ([16, 16], bf), "MT": ([16, 16], f16),
-    "LR": ([16, 16], f32), "NE": ([RUN[NH]], bf), "KP": ([RUN[NH]], bf), "RS": ([RUN[NH]], bf), "vt": ([16], f32), "GL": ([16], u16),
+    "LR": ([16, 16], f32), "NE": ([RUN[NH]], bf), "KP": ([RUN[NH]], bf), "RS": ([RUN[NH]], bf), "vt": ([32], f32), "GL": ([16], u16),
     "TL": ([16], u16), "NV": ([256], bf), "la": ([16], f32), "Y": ([256], bf), "yq": ([256], f32), "tp": ([256], f32),
-    "cn": ([4], f32), "pi": ([4], f32), "pb": ([4], f32), "FS": ([256], bf), "M2": ([1024], f16),
+    "BA": ([160], f16), "KC": ([256], bf), "EL": ([4], u16), "GF": ([24], f32), "EE": ([1024], bf), "RS2": ([192], bf), "RS4": ([320], bf), "io2": ([16], f32), "B2": ([160], bf), "I32": ([128], f16), "cn": ([4], f32), "pb": ([4], f32), "FS": ([256], bf), "M2": ([1024], f16),
     "KEY": ([160], bf), "k1": ([128], bf), "k2": ([160], bf), "k3": ([128], bf), "SI": ([128], bf),
-    "pc": ([4], i32), "pd": ([10], i32), "col": ([64], f32), "XC": ([512], bf), "SB2": ([128], bf), "IL": ([64], f32), "io16": ([16], f32), "IOT": ([256], bf),
+    "pc": ([4], i32), "pd": ([10], i32), "col": ([64], f32), "XC": ([1536], bf), "SB2": ([128], bf), "IL": ([64], f32), "io16": ([16], f32), "IOT": ([256], bf),
     "SM": ([256], bf), "I": ([160], bf), "NI": ([128], bf), "BD": ([160], bf), "SBD": ([128], bf),
     "BK": ([160], bf), "PK": ([160], bf), "U0": ([128], bf), "U1": ([128], bf), "U2": ([128], bf), "HB": ([128], bf),
     "SH": ([128], bf), "TOP": ([128], bf), "BS": ([320], bf), "IS": ([320], bf), "ZW": ([320], f16),
     "WB": ([128], f16), "GT": ([36], bf), "CM": ([256], bf), "wa": ([16], f32), "wf": ([16], f32),
     "wl": ([8], u16), "p1": ([16], u16), "p2": ([8], u16), "c16": ([128], f16), "tc": ([128], f32),
 }
-PS = {"A0": [16, 32], "A1": [16, 32], "CB": [16, 32], "P1": [16, 32], "P2": [16, 32], "M0": [32, 16], "M1": [16, 32], "M2b": [16, 32]}
+PS = {"A0": [16, 32], "A1": [16, 32], "CB": [16, 32], "P1": [16, 32], "P2": [16, 32], "M0": [32, 16], "M1": [32, 16], "M2b": [32, 16]}
 SCRATCH = {k: ("sbuf", [128] + v[0], v[1]) for k, v in SB.items()}
 SCRATCH.update({k: ("psum", [128] + v, f32) for k, v in PS.items()})
 NDMA = 40
 SEMAPHORES = ["v", "s", "p", "g"] + ["d%d" % i for i in range(NDMA)] + ["arr%d" % t for t in range(RO)] + ["snt%d" % t for t in range(RO)]
-SETS = [dict(cy=0.86, ga=1.56, sc=3.8, pe=0.44, hop=210.0, rate=300.0, xr=270.0, lat=1200.0),
-        dict(cy=1.0, ga=1.45, sc=3.3, pe=0.52, hop=170.0, rate=270.0, xr=190.0, lat=1300.0),
-        dict(cy=1.17, ga=1.85, sc=5.0, pe=0.62, hop=280.0, rate=250.0, xr=170.0, lat=1500.0)]
-PASSES, MOVES, HEAT, REACH = 100, 40000, 400.0, 12
-COPY = ["svsv", "vvggg", "vvggg", "vvgggg"]
-MV = [8, 8, 8, 4]
-XE = ["ssssssss"] * 4
+SETS = [dict(cy=0.86, ga=1.25, sc=3.0, pe=0.48, hop=260.0, rate=300.0, xr=230.0, lat=1200.0),
+        dict(cy=0.92, ga=1.85, sc=4.5, pe=0.46, hop=210.0, rate=270.0, xr=230.0, lat=1300.0),
+        dict(cy=0.85, ga=1.4, sc=3.8, pe=0.6, hop=200.0, rate=300.0, xr=230.0, lat=1200.0)]
+PASSES, MOVES, HEAT, REACH, SPAN, SWEEPS, NEAR = 20, 600000, 85.0, 10, 150, 60, 150.0
+COPY = ["vvvv", "vsggg", "vsggg", "vsgggg"]
+CAND = [[("c", 128), ("c", 64), ("a", 64)]] * 4
+AL, FK = 16.0, 1025.0
 OS = [3, 3, 3, 3]
 HS = [0, 0, 0, 0]
-SMALL = "vvss"
-LATE = ("U0", "RS", "CM", "SM", "IOT", "GT")
+HB = ["P1", "P2", "P1"]
+SMALL = "vvvs"
+LATE = ("U0", "RS", "RS2", "RS4", "CM", "SM", "IOT", "GT")
+SEED = 12345
+ACL = True
+LOT = True
+HALF = True
+NHQ = (2, 2)
+OQ = [(3, 0)] * 4
+EW = (256, 512)
+EC = "vv"
+
+
+def runs_of(nh):
+    return [128 // nh * h * (h + 1) // 2 for h in range(nh + 1)]
+
+
 HC = 512
 ORDER = []
-CG = 512
+CG = {"a": 128, "b": 512, "c": 512}
+WIN = 8192
 
 
 def build(g, T, rank, core, topo):
@@ -203,8 +221,8 @@ def build(g, T, rank, core, topo):
         frm = T.cores[(rank + JUMPS[t]) % len(T.cores)]
         add("x", None, [o], [], (0, 0, "cy"), sem="arr%d" % t, cnt=len(topo.engines(frm, core)), after=len(ops) - 1)
 
-    def swapped(bank, rows, mats, nh, start):
-        mms([x for c in range(2) for x in chain(r3(bank, 0, rows, 16 * c, 16 * c + 16), [
+    def swapped(bank, rows, mats, nh, start, *more):
+        mms([x for c in range(2) for x in chain(r3(bank, c, 2 * rows, step0=2), list(more) + [
             (ref(mat, 160 * c + start(c, h), 160 * c + start(c, h) + 128), src(h)) for mat, src in mats for h in range(nh)])])
 
     halves = lambda c, h: 16 + 16 * (c - h)
@@ -213,10 +231,13 @@ def build(g, T, rank, core, topo):
     dma(ref("wt"), T.wts[:], 8192)
     dma(ref("cv"), T.cov[:], 65536)
     dma(ref("X", X0, X0 + B0), T.lab[:], 524288)
-    dma(ref("ac"), T.act[:], 262144)
+    if not ACL:
+        dma(ref("ac"), T.act[:], 262144)
     dma(ref("pt"), T.pth[:], 1048576)
     first.append(len(ops))
     push(0)
+    if ACL:
+        dma(ref("ac"), T.act[:], 262144)
     iota(ref("pc", 0, 1), [[0, 1]], 0, 1)
     iota(ref("KEY"), [[0, 10], [1, 16]], 100, 0)
     sel(ref("KEY"), ref("KEY"), [[-16, 10], [0, 16]], A.is_ge, 0.0, 16, 1)
@@ -226,6 +247,7 @@ def build(g, T, rank, core, topo):
     iota(ref("SM"), [[0, 16], [1, 16]], 0, 0)
     iota(ref("IOT"), [[1, 256]], 0, 0)
     iota(ref("X", 0, X0), [[0, X0]], 300, 0)
+    iota(ref("KC"), [[0, 256]], int(16 * NONE) + NOT, 0)
     p = ref("pc", 0, 1)
     ts(ref("pd", 0, 1), p, 4, A.arith_shift_right)
     ts(ref("pd", 1, 2), p, 15, A.bitwise_and)
@@ -259,7 +281,7 @@ def build(g, T, rank, core, topo):
     ts(ref("k4"), BDm, 1.0 / 4096, A.mult)
     tt(ref("WB"), ind(ref("wf"), ref("wl")), ref("k4"), A.mult)
     ts(ref("NH"), I_, -63.0 / 64, A.mult)
-    ts(ref("HF"), ref("ac", 0, 256), 0.0, A.mult, 65.0 / 128, A.add)
+    ts(ref("HF"), ref("KC"), 0.0, A.mult, 65.0 / 128, A.add)
     ms(ref("ZW"), 0.0)
     for c in range(2):
         ts(col(12 + c), half[1 - c], 100.0, A.mult, pr, A.add)
@@ -284,21 +306,18 @@ def build(g, T, rank, core, topo):
     if any(HS):
         ts(col(21), sg, 8192.0, A.mult, C0, A.add)
         ts(ref("SB2"), BDm, 512.0, A.mult)
-    kinds = sorted(set(MV))
-    for j, mv in enumerate(kinds):
-        ts(col(22), pm, mv - 0.5, A.is_ge)
-        ts(col(52 + 3 * j), col(22), 1.0 / LIVE, A.mult, -2.0 / LIVE, A.add)
-        ts(col(53 + 3 * j), col(22), 251.5, A.mult, -519.0, A.add)
-        ts(col(54 + 3 * j), col(22), -2.0, A.mult, 4.0, A.add)
     for nm in ("BK", "PK", "GT"):
         iota(ref(nm), [[0, SB[nm][0][0]]], 0, 0)
     ts(ref("BK", 16, 144, 16), ref("io16", 0, 8), cg, A.is_equal)
+    ts(ref("BA"), ref("BK"), 2.0 / 3, A.mult)
     ts(ref("PK", 16, 144, 16), ref("BK", 16, 144, 16), -1.0, A.mult)
     ts(ref("PK", 24, 152, 16), ref("BK", 16, 144, 16), sg, A.mult)
     ts(ref("GT", 3, 35, 4), ref("BK", 16, 144, 16), 1.0, A.mult)
     ts(col(23), lo8, 32.0, A.mult)
-    ts(col(24), up, 16.0, A.mult, col(23), A.add)
-    ts(ref("p1"), ref("io16"), col(24), A.add)
+    ts(col(24), up, 1.0 if HALF else 16.0, A.mult, col(23), A.add)
+    if HALF:
+        iota(ref("io2"), [[16, 2], [2, 8]], 0, 0)
+    ts(ref("p1"), ref("io2" if HALF else "io16"), col(24), A.add)
     ts(col(25), up, -188416.0 - 1577216.0, A.mult, 1577216.0, A.add)
     ts(col(26), pm, -K2, A.mult, -17 * K2, A.add)
     ts(col(27), pm, -K2, A.mult, -K2 - LIVE, A.add)
@@ -319,13 +338,43 @@ def build(g, T, rank, core, topo):
     for t in range(RO):
         ts(col(36 + t), col(34), B0 + S * t - 1024.0, A.mult, 1024.0 - LIVE, A.add)
     ts(ref("CM"), ref("SM"), pm, A.is_ge, 65536.0, A.mult)
-    iota(ref("RS"), [[0, RUN[NH]]], 1, 0)
-    for h in range(NH):
-        iota(ref("RS", RUN[h], RUN[h + 1], 16 * h + 16), [[0, 16 // NH]], 0, 0)
-        iota(ref("RS", RUN[h] + 16 * h + 15, RUN[h + 1], 16 * h + 16), [[0, 16 // NH]], 32768, 0)
+    if HALF:
+        ms(ref("GF"), 0.0)
+        for h in range(max(NHQ)):
+            ts(col(48 + h), pm, 16.0 * h, A.add)
+        for nh in sorted(set(NHQ)):
+            run = runs_of(nh)
+            for h in range(nh):
+                ts(ref("RS%d" % nh, run[h], run[h + 1]), ref("KC", 0, run[h + 1] - run[h]), 0.0, A.mult, col(48 + h), A.add)
+                iota(ref("RS%d" % nh, run[h] + 16 * h + 15, run[h + 1], 16 * h + 16), [[0, 8 // nh]], WIN, 0)
+            hh = lo4 if nh == 4 else col(55)
+            if nh == 2:
+                ts(ref("pd", 5, 6), p, 1, A.bitwise_and)
+                cp(hh, ref("pd", 5, 6))
+            ts(col(56), lo8, 1.0 / nh, A.mult)
+            ts(col(52), hh, 3.0 / nh, A.mult, col(56), A.add)
+            ts(col(53), hh, 16.0, A.mult, 16.0, A.add)
+            ts(col(54), col(52), col(53), A.mult, col(53), A.add)
+            ts(ref("EL", nh - 2, nh - 1), col(54), -2.0, A.add)
+    for h in range(0 if HALF else NH):
         ts(col(48 + h), pm, 16.0 * h, A.add)
+        for a in range(RUN[h], RUN[h + 1], 256):
+            b = min(a + 256, RUN[h + 1])
+            ts(ref("RS", a, b), ref("KC", 0, b - a), 0.0, A.mult, col(48 + h), A.add)
+        iota(ref("RS", RUN[h] + 16 * h + 15, RUN[h + 1], 16 * h + 16), [[0, 16 // NH]], WIN, 0)
+    if not HALF:
+        ts(col(52), lo4, 2.0, A.mult, hi4, A.add)
+        ts(col(53), lo4, 16.0, A.mult, 16.0, A.add)
+        ts(col(54), col(52), col(53), A.mult, col(53), A.add)
+        ts(ref("EL", 0, 1), col(54), -2.0, A.add)
     ts(col(40), cg, -16.0, A.mult, -1024.0, A.add)
     ts(ref("I16"), ref("IL"), col(40), A.add)
+    if LOT:
+        iota(ref("B2"), [[0, 160]], 0, 0)
+        for u in range(2):
+            ts(ref("B2", 16 + u, 144, 16), ref("BK", 16, 144, 16), 1.0, A.mult)
+            ts(col(57 + u), col(55), 1.0 - u, A.is_equal, -32768.0, A.mult)
+            ts(ref("I32", u, 128, 2), ref("I16"), col(57 + u), A.add)
     early[0] = False
 
     def path_list():
@@ -345,8 +394,8 @@ def build(g, T, rank, core, topo):
     def hold_s(t, a, b, bank):
         bank = pq(bank, 0, b - a)
         xs = ref("X", X0 + a, X0 + b)
-        act(ref("XC", 0, b - a), ind(ref("X", 0, X0 + B0 + S * t), ref("COV", a // 16, b // 16)), F.Copy)
-        group(bank, [(I_, xs), (NI, ref("XC", 0, b - a))])
+        act(ref("XC", a, b), ind(ref("X", 0, X0 + B0 + S * t), ref("COV", a // 16, b // 16)), F.Copy)
+        group(bank, [(I_, xs), (NI, ref("XC", a, b))], 1)
         act(ref("C", a, b), bank, F.Sign, bias=0.5)
         group(bank, [(ref("SI"), xs), (ref("SB2"), ref("C", a, b))])
         act(ref("TT", a, b), bank, F.Identity, bias=col(21), scale=sg)
@@ -380,64 +429,135 @@ def build(g, T, rank, core, topo):
         hs = [(ref("NH"), ref("HF")), (ref("WB"), z)]
         group(pq("M2b", 0, 256), hs, 1)
         ts(ref("cq"), pq("M2b", 0, 256), BIG, A.add, BIG, A.subtract)
-        group(pq("M2b", 0, 256), hs + [(NI, ref("cq"))])
-        ts(ref("CL"), pq("M2b", 0, 256), float(B), A.mult, B * 4095 / 8192.0 - 15.0 / 32, A.add)
+        group(pq("M2b", 0, 256), [hs[1], (NI, ref("cq"))])
+        ts(ref("CL"), pq("M2b", 0, 256), float(B), A.mult, -15.0 / 32, A.add)
         ts(cs, ref("CL"), -1024.0, A.add)
-        for a in range(0, 4096, CG):
-            copy(XE[t][a // CG], ref("XK", a, a + CG), ind(ref(snap, 0, B), ref("CL", a // 16, (a + CG) // 16)))
-        act(ref("E", 0, 256), ind(ref("xr%d" % t), ref("LQ")), F.Copy)
-        copy(SMALL[0], ref("E", 256, 512), ref("E", 0, 256))
-        if SMALL[1] == "s":
-            act(ref("EM"), ref("E", 0, 256), F.Relu, bias=-255 * LIVE, scale=LIVE)
+        runs, s0 = [], 0
+        for kind, n in CAND[t]:
+            runs.append((kind, s0, s0 + n))
+            s0 += n
+        for kind, s0, s1 in runs:
+            if kind == "a":
+                for m in range(16):
+                    copy("g", ref("XK", 16 * s0 + m, 16 * s1, 16), ref("z%d" % (t & 1), s0, s1))
+            for a in range(s0, s1, CG[kind] // 16):
+                b = min(s1, a + CG[kind] // 16)
+                src = ind(ref(snap, 0, B), ref("CL", a, b))
+                if kind == "a":
+                    tt(ref("SG", 16 * a, 16 * b), src, ref("XK", 16 * a, 16 * b), A.is_le)
+                else:
+                    copy("s", ref("XK", 16 * a, 16 * b), src)
+        e1 = ref("EE", 384, 640) if HALF else ref("E", 0, 256)
+        act(e1, ind(ref("xr%d" % t), ref("LQ")), F.Copy)
+        if HALF:
+            for q in (1, 0):
+                for w in (128, 256)[:EW[q] // 256]:
+                    copy(EC[q], ref("EE", 512 + w, 512 + 2 * w) if q else ref("EE", 512 - 2 * w, 512 - w), ref("EE", 512, 512 + w) if q else ref("EE", 512 - w, 512))
         else:
-            ts(ref("EM"), ref("E", 0, 256), 255.5, A.is_gt, LIVE, A.mult)
+            copy(SMALL[0], ref("E", 256, 512), ref("E", 0, 256))
+        if SMALL[1] == "s":
+            act(ref("EM"), e1, F.Relu, bias=-255 * LIVE, scale=LIVE)
+        else:
+            ts(ref("EM"), e1, 255.5, A.is_gt, LIVE, A.mult)
         if t == 0:
             ts(ref("PV"), ind(ref("pt"), ref("LU")), -1024.0, A.add)
             path_list()
-        if HS[t]:
-            hold_s(t, 0, HS[t], "M2b")
+        for a in range(0, HS[t], 512):
+            hold_s(t, a, min(HS[t], a + 512), HB[a // 512])
         for a in range(HS[t], old, HC):
             hold(t, a, min(old, a + HC), ["P1", "P2"] if HC > 512 or ((a - HS[t]) // HC) % 2 else ["P2"])
-        if OS[t]:
+        Xa = ref("X", 0, X0 + B)
+        if HALF:
+            mms([(pq("M0", 128 * j, 128 * j + 128), I_, ref("EE", 384 + 128 * (j // 2), 512 + 128 * (j // 2)), True, True) for j in range(4) if OQ[t][j // 2]])
+        for q in ((1, 0) if HALF else ()):
+            s0, pb, wb, nh = 128 * q, "P%d" % (q + 1), ("M0", "M2b")[q], NHQ[q]
+            for n, k in enumerate((12, 8, 4, 0)):
+                if k == 0 and t and q:
+                    hold(t, old, B, ["M1"])
+                a = 2048 * q + 128 * k
+                win = ref("TT", 0, old if k else B)
+                if n < OQ[t][q]:
+                    act(ref("OG", a, a + 512), ind(win, ref("PL", a // 16, a // 16 + 32)), F.Copy)
+                    for b in (a, a + 256):
+                        tt(ref("O", b, b + 256), ref("OG", b, b + 256), pq("M0", 256 * q, 256 * q + 256), A.subtract)
+                else:
+                    w = EW[q]
+                    for b in range(a, a + 512, w):
+                        tt(ref("O", b, b + w), ind(win, ref("PL", b // 16, (b + w) // 16)), ref("EE", 512, 512 + w) if q else ref("EE", 512 - w, 512), A.subtract)
+                for j0 in (k + 2, k):
+                    mms([(pq(pb, 128 * (n // 2), 128 * (n // 2) + 128), ref("PK", 16 - j % 8, 144 - j % 8), ref("O", 2048 * q + 128 * j, 2048 * q + 128 * j + 128),
+                          j % 8 == 7, j % 8 == 0) for j in (j0 + 1, j0)])
+            fq = "F%d" % (q + 1)
+            act(ref(fq), pq(pb, 0, 256), F.Sign, bias=col(25))
+            group(pq(wb, 0, 128), [(I_, ref("PV", s0, s0 + 128)), (NI, ref("EM", s0, s0 + 128)), (ref("U2"), ref(fq, 0, 128)), (ref("U1"), ref(fq, 128, 256))], 2)
+            group(pq("M1", s0, s0 + 128), [(ref("HB"), ref(fq, 0, 128)), (ref("HB"), ref(fq, 128, 256))])
+            mt = r3("MT", 8 * q, 8 * q + 8)
+            ts(mt, pq(wb, 0, 128), col(26), A.add, -NONE, A.max)
+            swapped(wb, 4, [("BS", lambda h: r3("MT", 8 * q + h, 8 * q + 8, step0=2))], 2, halves)
+            group(pq(wb, 128, 256), [(I_, ref("CM", 0, 128)), (BDm, mt)])
+            group(r3(wb, 16, 24, step0=2), [(BDm, r3("MT", 8 * q, 8 * q + 8, step0=2))]) if nh == 2 else group(pq(wb, 256, 384), [(BDm, mt)])
+            tr(r3("LR", 8 * q, 8 * q + 8), pq(wb, 0, 128))
+            top = r3("LR", 8 * q, 8 * q + 8, 0, 1)
+            ts(ref("GL", 8 * q, 8 * q + 8), top, 16 * NONE + NOT - X0, A.add)
+            act(ref("GF", 8 * q, 8 * q + 8), top, F.Identity, bias=16 * NONE + NOT)
+            run = [320 * q + x for x in runs_of(nh)]
+            for h in range(nh):
+                for d in range(h + 1):
+                    tt(ref("NE", run[h] + d, run[h + 1], h + 1), r3("LR", 8 * q + h, 8 * q + 8, step0=nh),
+                       r3(wb, 8 + h, 16, step0=nh) if d == h else r3(wb, 16 + d, 24, step0=nh), A.not_equal)
+            kp, rs, ne = ref("KP", run[0], run[nh]), ref("RS%d" % nh), ref("NE", run[0], run[nh])
+            add("v", lambda kp=kp, rs=rs, ne=ne: g.vector.tensor_tensor_scan(kp["ap"], ne["ap"], rs["ap"], float(WIN), A.mult, A.max), [kp], [rs, ne], (0, max(64, kp["n"] // 2), "cy"))
+            tt(ref("vt", 16 * q, 16 * q + 16), ind(kp, ref("EL", nh - 2, nh - 1)), ref("GF", 8 * q, 8 * q + 16), A.min)
+            cp(ref("TL", 8 * q, 8 * q + 8), ref("vt", 16 * q, 16 * q + 8))
+            tt(ref("NV", s0, s0 + 128), ind(ref(snap, 0, B), ref("GL", 8 * q, 8 * q + 8)), ref("EE", 384 + s0, 512 + s0), A.max)
+            for b in range(8 * q + 8 - nh, 8 * q - 1, -nh):
+                cp(ind(Xa, ref("TL", b, b + nh)), ref("NV", 16 * b, 16 * (b + nh)))
+        if HALF:
+            act(lv, pq("M1", 0, 256), F.Relu, bias=-7 * LIVE, scale=-LIVE / 2, acc=ref("cn", t, t + 1))
+        if OS[t] and not HALF:
             mms([(pq("M0", a, a + 256), I_, ref("E", 0, 256), True, True) for a in (0, 256)])
-        for n, k in enumerate([8, 10, 12, 14, 6, 4, 2, 0]):
+        for n, k in enumerate([] if HALF else [8, 10, 12, 14, 6, 4, 2, 0]):
             if k == 0 and t:
                 hold(t, old, B, ["M1"])
             o, src = ref("O", 256 * k, 256 * k + 512), ind(ref("TT", 0, old if k else B), ref("PL", 16 * k, 16 * k + 32))
             if k >= 16 - 2 * OS[t]:
-                act(ref("OG", 256 * k - 2048, 256 * k - 1536), src, F.Copy)
-                tt(o, ref("OG", 256 * k - 2048, 256 * k - 1536), pq("M0", 0, 512), A.subtract)
+                act(ref("OG", 256 * k, 256 * k + 512), src, F.Copy)
+                tt(o, ref("OG", 256 * k, 256 * k + 512), pq("M0", 0, 512), A.subtract)
             else:
                 tt(o, src, ref("E"), A.subtract)
             bank = pq("P2" if k >= 8 else "P1", 0, 256)
             mms([(bank, ref("PK", 16 - j % 8, 144 - j % 8), ref("O", 256 * j, 256 * j + 256), n % 4 == 0 and j > k, n % 4 == 3 and j == k) for j in (k + 1, k)])
             if n % 4 == 3:
                 act(ref("F2" if k else "F1"), bank, F.Sign, bias=col(25))
-        group(pq("M2b", 0, 256), [(I_, ref("PV")), (NI, ref("EM")), (ref("U2"), ref("F2")), (ref("U1"), ref("F1"))], 3)
-        group(pq("M1", 0, 256), [(ref("HB"), ref("F2")), (ref("HB"), ref("F1"))], 1)
-        ts(r3("MT"), pq("M2b", 0, 256), col(26), A.add, -NONE, A.max)
-        act(lv, pq("M1", 0, 256), F.Relu, bias=-7 * LIVE, scale=-LIVE / 2, acc=ref("cn", t, t + 1))
-        swapped("M2b", 8, [("BS", lambda h: r3("MT", h, 16, step0=2))], 2, halves)
-        group(r3("M0", 0, 16), [(I_, ref("CM")), (BDm, r3("MT"))], 1)
-        group(r3("M0", 16, 32), [(BDm, r3("MT"))])
-        tr(r3("LR"), pq("M2b", 0, 256))
-        ts(ref("GL"), r3("LR", 0, 16, 0, 1), 16 * NONE, A.add)
-        for h in range(NH):
-            for d in range(h + 1):
-                tt(ref("NE", RUN[h] + d, RUN[h + 1], h + 1), r3("LR", h, 16, step0=NH), r3("M0", h, 16, step0=NH) if d == h else r3("M0", 16 + d, 32, step0=NH), A.is_equal)
-        kp, rs, ne = ref("KP"), ref("RS"), ref("NE")
-        add("v", lambda kp=kp, rs=rs, ne=ne: g.vector.tensor_tensor_scan(kp["ap"], rs["ap"], ne["ap"], 0.0, A.mult, A.subtract), [kp], [rs, ne], (0, RUN[NH] // 2, "cy"))
-        nb = 16 // NH
-        for h in range(NH):
-            tt(ref("vt", nb * h, nb * h + nb), ref("KP", RUN[h] + 16 * h + 15, RUN[h + 1], 16 * h + 16), r3("LR", h, 16, 0, 1, step0=NH), A.min)
-        for h in range(NH):
-            ts(ref("TL", h, 16, NH), ref("vt", nb * h, nb * h + nb), 16 * NONE, A.add, col(48 + h), A.max)
-        Xa = ref("X", 0, X0 + B)
-        tt(ref("NV"), ind(Xa, ref("GL")), ref("E", 0, 256), A.max)
-        for b in range(nb - 1, -1, -1):
-            cp(ind(Xa, ref("TL", NH * b, NH * b + NH)), ref("NV", 16 * NH * b, 16 * NH * (b + 1)))
-        group(r3("P1", 0, 1, 0, 16), [(I_, ref("I16", 16 * t, 16 * t + 16))] + [(ref("BK", 16 - i, 144 - i), r3(lvn, 0, 16, i, i + 1)) for i in range(16)])
-        tt(ref("LO"), r3("P1", 0, 1, 0, 16), ref("LO"), A.max)
+        if not HALF:
+            group(pq("M2b", 0, 256), [(I_, ref("PV")), (NI, ref("EM")), (ref("U2"), ref("F2")), (ref("U1"), ref("F1"))], 3)
+            group(pq("M1", 0, 256), [(ref("HB"), ref("F2")), (ref("HB"), ref("F1"))], 1)
+            ts(r3("MT"), pq("M2b", 0, 256), col(26), A.add, -NONE, A.max)
+            act(lv, pq("M1", 0, 256), F.Relu, bias=-7 * LIVE, scale=-LIVE / 2, acc=ref("cn", t, t + 1))
+            swapped("M2b", 8, [("BS", lambda h: r3("MT", h, 16, step0=2))], 2, halves)
+            group(r3("M0", 0, 16), [(I_, ref("CM")), (BDm, r3("MT"))], 1)
+            group(r3("M0", 16, 32), [(BDm, r3("MT"))])
+            tr(r3("LR"), pq("M2b", 0, 256))
+            ts(ref("GL"), r3("LR", 0, 16, 0, 1), 16 * NONE + NOT, A.add)
+            act(ref("GF", 0, 16), r3("LR", 0, 16, 0, 1), F.Identity, bias=16 * NONE + NOT)
+            for h in range(NH):
+                for d in range(h + 1):
+                    tt(ref("NE", RUN[h] + d, RUN[h + 1], h + 1), r3("LR", h, 16, step0=NH), r3("M0", h, 16, step0=NH) if d == h else r3("M0", 16 + d, 32, step0=NH), A.not_equal)
+            kp, rs, ne = ref("KP"), ref("RS"), ref("NE")
+            add("v", lambda kp=kp, rs=rs, ne=ne: g.vector.tensor_tensor_scan(kp["ap"], ne["ap"], rs["ap"], float(WIN), A.mult, A.max), [kp], [rs, ne], (0, RUN[NH] // 2, "cy"))
+            nb = 16 // NH
+            tt(ref("vt", 0, 16), ind(kp, ref("EL", 0, 1)), ref("GF", 0, 16), A.min)
+            cp(ref("TL"), ref("vt", 0, 16))
+            tt(ref("NV"), ind(Xa, ref("GL")), ref("E", 0, 256), A.max)
+            for b in range(nb - 1, -1, -1):
+                cp(ind(Xa, ref("TL", NH * b, NH * b + NH)), ref("NV", 16 * NH * b, 16 * NH * (b + 1)))
+        if LOT:
+            group(r3("P1", 0, 1), [(I_, ref("I32", 32 * t, 32 * t + 32))] + [(ref("B2", 16 - i, 144 - i), r3(lvn, 0, 16, i, i + 2)) for i in range(0, 16, 2)])
+            for u in range(2):
+                tt(ref("LO"), r3("P1", 0, 1, u, 32, 2), ref("LO"), A.max)
+        else:
+            group(r3("P1", 0, 1, 0, 16), [(I_, ref("I16", 16 * t, 16 * t + 16))] + [(ref("BK", 16 - i, 144 - i), r3(lvn, 0, 16, i, i + 1)) for i in range(16)])
+            tt(ref("LO"), r3("P1", 0, 1, 0, 16), ref("LO"), A.max)
         if not last:
             ts(ref("LU"), ref("LO"), -LOFF, A.add)
         else:
@@ -461,29 +581,30 @@ def build(g, T, rank, core, topo):
         else:
             mms([(yc, ref("GT", 3 - r, 35 - r), ref("M2", S * r, S * r + S), r == 0, False) for r in range(t)])
         n = 0
-        mv = MV[t]
-        if mv < 16:
-            group(pq("A1", 0, 256), [(I_, z)])
-        for q in range(2):
-            for m0 in range(0, mv, 4):
-                bank = "A%d" % (n & 1) if mv == 16 else "A0"
-                n += 1
-                m1 = min(mv, m0 + 4)
-                mms([x for m in range(m0, m1) for x in chain(pq(bank, 128 * (m - m0), 128 * (m - m0) + 128), [
-                    (I_, ref("z%d" % (t & 1), 128 * q, 128 * q + 128)), (NI, ref("XK", 2048 * q + m, 2048 * q + 2048, 16))])])
-                a = 2048 * q + 128 * m0
-                act(ref("SG", a, a + 128 * (m1 - m0)), pq(bank, 0, 128 * (m1 - m0)), F.Sign, bias=0.5)
-            for m in range(mv, 16):
-                a = 2048 * q + 128 * m
-                tt(ref("SG", a, a + 128), ref("XK", 2048 * q + m, 2048 * q + 2048, 16), pq("A1", 128 * q, 128 * q + 128), A.is_le)
+        two = all(kind != "b" for kind, s0, s1 in runs)
+        for kind, s0, s1 in runs:
+            w = s1 - s0
+            zs = ref("z%d" % (t & 1), s0, s1)
+            if kind == "c":
+                per = 512 // w
+                for m0 in range(0, 16, per):
+                    bank = "A%d" % (n & 1) if two else "A0"
+                    n += 1
+                    m1 = min(16, m0 + per)
+                    mms([x for m in range(m0, m1) for x in chain(pq(bank, w * (m - m0), w * (m - m0 + 1)), [
+                        (I_, zs), (NI, ref("XK", 16 * s0 + m, 16 * s1, 16))])])
+                    act(ref("SG", 16 * s0 + w * m0, 16 * s0 + w * m1), pq(bank, 0, w * (m1 - m0)), F.Sign, bias=0.5)
+            if kind == "b":
+                group(pq("A1", 0, w), [(I_, zs)])
+                for m in range(16):
+                    tt(ref("SG", 16 * s0 + w * m, 16 * s0 + w * m + w), ref("XK", 16 * s0 + m, 16 * s1, 16), pq("A1", 0, w), A.is_le)
             for m0 in range(0, 16, 4):
-                mms([(pq("CB", 128 * q, 128 * q + 128), ref("BK", 16 - m, 144 - m), ref("SG", 2048 * q + 128 * m, 2048 * q + 128 * m + 128), m == 0, m == 15)
+                mms([(pq("CB", s0, s1), ref("BK" if kind == "c" else "BA", 16 - m, 144 - m),
+                      ref("SG", 16 * s0 + m, 16 * s1, 16) if kind == "a" else ref("SG", 16 * s0 + w * m, 16 * s0 + w * m + w), m == 0, m == 15)
                      for m in range(m0, m0 + 4)])
-        j = 52 + 3 * kinds.index(mv)
-        act(ref("py", t, t + 1), ref("cn", t, t + 1), F.Identity, bias=127.75, scale=0.5 / LIVE)
-        act(ref("pi", t, t + 1), ref("cn", t, t + 1), F.Identity, bias=col(j + 1), scale=col(j))
-        act(ref("pb", t, t + 1), ref("py", t, t + 1), F.Identity, bias=ref("pi", t, t + 1), scale=col(j + 2))
-        act(ref("FS"), pq("CB", 0, 256), F.Sign, bias=ref("pb", t, t + 1))
+        act(ref("py", t, t + 1), ref("cn", t, t + 1), F.Identity, bias=-512.5 * AL, scale=AL / LIVE)
+        act(ref("pb", t, t + 1), ref("cn", t, t + 1), F.Identity, bias=ref("py", t, t + 1), scale=-AL / LIVE)
+        act(ref("FS"), pq("CB", 0, 256), F.Sign, bias=ref("pb", t, t + 1), scale=FK)
         group(pq("CB", 0, 256), [(ref("U0"), ref("FS")), (I_, lv), (I_, cs)])
         ts(ref("M2", S * t, S * t + S), pq("CB", 0, 256), col(27), A.add, -1025.0, A.max)
         if not last:
@@ -589,7 +710,7 @@ def schedule(ops):
             snaps.append(free[:])
         return max(end[i] + ta[i] for i in ends), end, snaps
 
-    seed = [12345]
+    seed = [SEED]
 
     def rnd():
         seed[0] = (seed[0] * 1103515245 + 12345) % 2147483648
@@ -635,69 +756,221 @@ def schedule(ops):
         if new[0] < best[0]:
             best = new
 
-    def critical(seq, du, ta, pr):
-        end, why, free, last = [0.0] * n, [-1] * n, {}, {}
-        for i in seq:
-            e = ops[i]["e"]
-            t, w = free.get(e, 0.0), (last.get(e, -1), True)
+    anc = []
+    for i in range(n):
+        far = set()
+        for j, w in ops[i]["d"].items():
+            if w:
+                far |= anc[j]
+        for du, ta, pr in sets:
+            pr[i] = [(j, lag) for j, lag in pr[i] if j not in far or issue[j] >= 0]
+        anc.append(set(ops[i]["d"]).union(*[anc[j] for j in ops[i]["d"]]))
+    succ = []
+    for du, ta, pr in sets:
+        sc = [[] for _ in ops]
+        for i in range(n):
             for j, lag in pr[i]:
-                if end[j] + lag > t:
-                    t, w = end[j] + lag, (j, False)
+                sc[j].append((i, lag))
+        succ.append(sc)
+    before = [[j for j, lag in x] for x in pred]
+    after = [[j for j, lag in x] for x in succ[0]]
+    seq = best[2][:]
+    pos, bq, aq, bd, ad = [0] * n, [n] * (n + 1), [n] * (n + 1), [n] * (n + 1), [n] * (n + 1)
+    tm = [[[0.0] * (n + 1) for _ in range(5)] for _ in sets]
+
+    def links():
+        last = [n] * 7
+        for p, i in enumerate(seq):
+            pos[i] = p
+            e = que[i]
+            bq[i] = k = last[e]
+            aq[i] = n
+            if k < n:
+                aq[k] = i
             last[e] = i
-            if res[i] == "dma":
-                free[e] = t + ops[i]["c"][0]
-                if free.get("dma", 0.0) > t:
-                    t, w = free["dma"], (last["dma"], True)
-                last["dma"] = i
-            end[i] = free[res[i]] = t + du[i]
-            why[i] = w
-        i = max(range(n), key=lambda k: end[k] + ta[k])
+            if issue[i] >= 0:
+                bd[i] = k = last[6]
+                ad[i] = n
+                if k < n:
+                    ad[k] = i
+                last[6] = i
+
+    def times(lo, hi, r0, r1):
+        for (du, ta, pr), sc, (st, end, fr, up, dn) in zip(sets, succ, tm):
+            for i in seq[lo:r1]:
+                t = fr[bq[i]]
+                for j, lag in pr[i]:
+                    x = end[j] + lag
+                    if x > t:
+                        t = x
+                st[i] = t
+                if issue[i] >= 0:
+                    fr[i] = t + issue[i]
+                    end[i] = max(t, end[bd[i]]) + du[i]
+                else:
+                    end[i] = fr[i] = t + du[i]
+            for i in reversed(seq[r0:hi + 1]):
+                t = ta[i]
+                for j, lag in sc[i]:
+                    x = up[j] + lag
+                    if x > t:
+                        t = x
+                if issue[i] >= 0:
+                    dn[i] = max(t, dn[ad[i]]) + du[i]
+                    up[i] = max(dn[i], issue[i] + up[aq[i]])
+                else:
+                    x = up[aq[i]]
+                    up[i] = (x if x > t else t) + du[i]
+
+    def total(r0, r1, rest):
+        return [max([top] + [st[i] + up[i] if issue[i] < 0 else max(st[i] + up[i], end[i] - du[i] + dn[i]) for i in seq[r0:r1]])
+                for (du, ta, pr), (st, end, fr, up, dn), top in zip(sets, tm, rest)]
+
+    def passing(r0, r1):
         out = []
-        while i >= 0:
-            if why[i][1] and why[i][0] >= 0:
-                out.append((why[i][0], i))
-            i = why[i][0]
+        for (du, ta, pr), (st, end, fr, up, dn) in zip(sets, tm):
+            top = max([end[i] + ta[i] for i in seq[:r0]] + [0.0])
+            for i in seq[r1:]:
+                t = fr[bq[i]] if bq[i] == n or pos[bq[i]] < r0 else 0.0
+                for j, lag in pr[i]:
+                    if pos[j] < r0 and end[j] + lag > t:
+                        t = end[j] + lag
+                top = max(top, t + up[i])
+                if issue[i] >= 0 and bd[i] < n and pos[bd[i]] < r0:
+                    top = max(top, end[bd[i]] + dn[i])
+            out.append(top)
         return out
 
-    seq, now = best[2], best[0]
-    base = [replay(seq, s) for s in sets]
-    best = (now, seq)
-    crit = []
-    for it in range(MOVES):
-        if not crit:
-            crit = critical(seq, *sets[int(len(sets) * rnd())])
-        u, v = crit[int(len(crit) * rnd())]
-        pu, pv = seq.index(u), seq.index(v)
-        if rnd() < 0.5:
-            for _ in range(int(REACH * rnd() ** 2)):
-                q = pu - 1
-                while q >= 0 and res[seq[q]] != res[v]:
-                    q -= 1
-                pu = max(q, 0)
-            need = {v}
-            for q in range(pv, pu - 1, -1):
-                if seq[q] in need:
-                    need.update(j for j, lag in pred[seq[q]])
-            mid = seq[pu:pv + 1]
-            new = seq[:pu] + [i for i in mid if i in need] + [i for i in mid if i not in need] + seq[pv + 1:]
-        else:
-            for _ in range(int(REACH * rnd() ** 2)):
-                q = pv + 1
-                while q < n and res[seq[q]] != res[u]:
-                    q += 1
-                pv = min(q, n - 1)
-            need = {u}
-            for q in range(pu, pv + 1):
-                if seq[q] in need:
-                    need.update(j for j, lag in post[seq[q]])
-            mid = seq[pu:pv + 1]
-            new = seq[:pu] + [i for i in mid if i not in need] + [i for i in mid if i in need] + seq[pv + 1:]
-        got = [replay(new, s, pu, b) for s, b in zip(sets, base)]
-        c = sum(x[0] for x in got) / len(sets)
-        if c <= now + HEAT * (1.0 - it / MOVES) * rnd():
-            seq, now, crit, base = new, c, [], got
-            if c < best[0]:
-                best = (c, seq)
+    def critical(k, r0, r1, bar):
+        (du, ta, pr), (st, end, fr, up, dn) = sets[k], tm[k]
+        out = []
+        for i in seq[r0:r1]:
+            j = bq[i]
+            if j < n and st[i] + up[i] >= bar and fr[j] >= st[i] - 1e-6 and pos[j] >= r0:
+                out.append((j, i))
+            j = bd[i]
+            if j < n and end[i] - du[i] + dn[i] >= bar and end[j] > st[i] and pos[j] >= r0:
+                out.append((j, i))
+        return out
+
+    def relink(p, mid, free, nxt):
+        seq[p:p + len(mid)] = mid
+        last = dict(free)
+        for i in mid:
+            pos[i] = p
+            p += 1
+            bq[i] = k = last[que[i]]
+            aq[k] = last[que[i]] = i
+            if issue[i] >= 0:
+                bd[i] = k = last[6]
+                ad[k] = last[6] = i
+        for e, k in nxt.items():
+            (ad if e == 6 else aq)[last[e]] = k
+            (bd if e == 6 else bq)[k] = last[e]
+
+    def price(old, mid, tot):
+        free, nxt, low = {}, {}, 0.0
+        for i in old:
+            free.setdefault(que[i], bq[i])
+            nxt[que[i]] = aq[i]
+            if issue[i] >= 0:
+                free.setdefault(6, bd[i])
+                nxt[6] = ad[i]
+        for (du, ta, pr), sc, (st, end, fr, up, dn), was in zip(sets, succ, tm, tot):
+            f = {e: (end if e == 6 else fr)[k] for e, k in free.items()}
+            new, top, through = {}, 0.0, 0.0
+            for i in mid:
+                e = que[i]
+                t = f[e]
+                for j, lag in pr[i]:
+                    x = new.get(j, end[j]) + lag
+                    if x > t:
+                        t = x
+                if issue[i] >= 0:
+                    f[e] = t + issue[i]
+                    e = 6
+                    t = max(t, f[6])
+                new[i] = f[e] = t + du[i]
+                x = st[i] + up[i]
+                if x > through:
+                    through = x
+            for i in mid:
+                t = ta[i]
+                for j, lag in sc[i]:
+                    if j not in new and up[j] + lag > t:
+                        t = up[j] + lag
+                if new[i] + t > top:
+                    top = new[i] + t
+            for e, k in nxt.items():
+                top = max(top, f[e] + (dn if e == 6 else up)[k])
+            low += top if through > was - 1e-6 or top > was else was
+        return low / len(sets), free, nxt
+
+    best = (1e18, seq[:])
+    starts = list(range(0, n - SPAN // 2, SPAN // 2))
+    each = MOVES // (SWEEPS * len(starts))
+    for sweep in range(SWEEPS):
+        heat = HEAT * (1.0 - sweep / (SWEEPS - 1.0)) ** 1.5
+        links()
+        times(0, n - 1, 0, n)
+        old = seq[:]
+        seq.sort(key=lambda i: tm[0][0][i])
+        if [i for i in old if issue[i] >= 0] != [i for i in seq if issue[i] >= 0]:
+            seq[:] = old
+        links()
+        for r0 in starts:
+            r1 = min(n, r0 + SPAN)
+            times(max(0, r0 - SPAN), r1 - 1, r0, min(n, r1 + SPAN))
+            rest = passing(r0, r1)
+            tot = total(r0, r1, rest)
+            now = sum(tot) / len(sets)
+            crit = []
+            for it in range(each):
+                if not crit:
+                    k = int(len(sets) * rnd())
+                    crit = critical(k, r0, r1, tot[k] - NEAR * rnd() - 1e-6)
+                    if not crit:
+                        break
+                u, v = crit[int(len(crit) * rnd())]
+                back, step = (bd, ad) if bq[v] != u else (bq, aq)
+                if rnd() < 0.5:
+                    for _ in range(int(REACH * rnd() ** 2)):
+                        if back[u] < n and pos[back[u]] >= r0:
+                            u = back[u]
+                    old = seq[pos[u]:pos[v] + 1]
+                    need = {v}
+                    for i in reversed(old):
+                        if i in need:
+                            need.update(before[i])
+                    mid = [i for i in old if i in need] + [i for i in old if i not in need]
+                else:
+                    for _ in range(int(REACH * rnd() ** 2)):
+                        if step[v] < n and pos[step[v]] < r1:
+                            v = step[v]
+                    old = seq[pos[u]:pos[v] + 1]
+                    need = {u}
+                    for i in old:
+                        if i in need:
+                            need.update(after[i])
+                    mid = [i for i in old if i not in need] + [i for i in old if i in need]
+                if mid == old:
+                    continue
+                bar = now - heat * math.log(1.0 - rnd())
+                low, free, nxt = price(old, mid, tot)
+                if low > bar:
+                    continue
+                pu, pv = pos[u], pos[v]
+                relink(pu, mid, free, nxt)
+                times(pu, pv, r0, r1)
+                got = total(r0, r1, rest)
+                c = sum(got) / len(sets)
+                if c <= bar:
+                    now, tot, crit = c, got, []
+                    if c < best[0]:
+                        best = (c, seq[:])
+                else:
+                    relink(pu, old, free, nxt)
+                    times(pu, pv, r0, r1)
     return [ops[i] for i in best[1]]
 
 

@@ -5,11 +5,11 @@ A = AluOpType
 F = ActivationFunctionType
 B0, S, RO, W = 2048, 256, 4, 3072
 JUMPS = [1, 2, 3, 1]
-X0 = 144
+X0 = 48
 C0 = 98560.5
 K2 = 2048.0
 LIVE = 4096.0
-NOT = 128
+NOT = 32
 NONE = 1024.0 + X0 - NOT
 BIG = 12582912.0
 LOFF = 16 * LIVE - 1024
@@ -26,10 +26,10 @@ SB = {
     "cq": ([256], f16), "NH": ([128], bf), "HF": ([256], bf), "k4": ([128], bf), "LO": ([16], f32), "I16": ([64], f16), "py": ([4], bf), "CL": ([256], u16), "cs0": ([256], f16), "cs1": ([256], f16),
     "F1": ([256], bf), "F2": ([256], bf), "lv0": ([16, 16], bf), "lv1": ([16, 16], bf), "MT": ([16, 16], f16),
     "LR": ([16, 16], f32), "NE": ([RUN[NH]], bf), "KP": ([RUN[NH]], bf), "RS": ([RUN[NH]], bf), "vt": ([32], f32), "GL": ([16], u16),
-    "TL": ([16], u16), "NV": ([256], bf), "la": ([16], f32), "Y": ([256], bf), "yq": ([256], f32), "tp": ([256], f32),
-    "BA": ([160], f16), "KC": ([256], bf), "EL": ([4], u16), "GF": ([24], f32), "EE": ([1024], bf), "RS2": ([192], bf), "RS4": ([320], bf), "io2": ([16], f32), "B2": ([160], bf), "I32": ([128], f16), "cn": ([4], f32), "pb": ([4], f32), "FS": ([256], bf), "M2": ([1024], f16),
+    "TL": ([16], u16), "NV": ([256], bf), "Y": ([256], bf), "yq": ([256], f32), "tp": ([256], f32),
+    "BA": ([160], f16), "EL": ([4], u16), "GF": ([24], f32), "EE": ([1024], bf), "RS2": ([192], bf), "io2": ([16], f32), "B2": ([160], bf), "I32": ([128], f16), "cn": ([4], f32), "pb": ([4], f32), "FS": ([256], bf), "M2": ([64, 16], f16), "MK": ([32], bf), "cw": ([16], f32),
     "KEY": ([160], bf), "k1": ([128], bf), "k2": ([160], bf), "k3": ([128], bf), "SI": ([128], bf),
-    "pc": ([4], i32), "pd": ([10], i32), "col": ([64], f32), "XC": ([1536], bf), "SB2": ([128], bf), "IL": ([64], f32), "io16": ([16], f32), "IOT": ([256], bf),
+    "pc": ([4], i32), "GI": ([160], bf), "k5": ([256], bf), "pd": ([12], i32), "col": ([64], f32), "XC": ([1536], bf), "SB2": ([128], bf), "IL": ([64], f32), "io16": ([16], f32), "IOT": ([256], bf),
     "SM": ([256], bf), "I": ([160], bf), "NI": ([128], bf), "BD": ([160], bf), "SBD": ([128], bf),
     "BK": ([160], bf), "PK": ([160], bf), "U0": ([128], bf), "U1": ([128], bf), "U2": ([128], bf), "HB": ([128], bf),
     "SH": ([128], bf), "TOP": ([128], bf), "BS": ([320], bf), "IS": ([320], bf), "ZW": ([320], f16),
@@ -40,27 +40,28 @@ PS = {"A0": [16, 32], "A1": [16, 32], "CB": [16, 32], "P1": [16, 32], "P2": [16,
 SCRATCH = {k: ("sbuf", [128] + v[0], v[1]) for k, v in SB.items()}
 SCRATCH.update({k: ("psum", [128] + v, f32) for k, v in PS.items()})
 NDMA = 40
-SEMAPHORES = ["v", "s", "p", "g"] + ["d%d" % i for i in range(NDMA)] + ["arr%d" % t for t in range(RO)] + ["snt%d" % t for t in range(RO)]
-SETS = [dict(cy=0.86, ga=1.25, sc=3.0, pe=0.48, hop=260.0, rate=300.0, xr=230.0, lat=1200.0),
-        dict(cy=0.92, ga=1.85, sc=4.5, pe=0.46, hop=210.0, rate=270.0, xr=230.0, lat=1300.0),
-        dict(cy=0.85, ga=1.4, sc=3.8, pe=0.6, hop=200.0, rate=300.0, xr=230.0, lat=1200.0)]
-PASSES, MOVES, HEAT, REACH, SPAN, SWEEPS, NEAR = 20, 600000, 85.0, 10, 150, 60, 150.0
-COPY = ["vvvv", "vsggg", "vsggg", "vsgggg"]
+SEMAPHORES = ["v", "s", "p", "g"] + ["d%d" % i for i in range(NDMA)] + ["arr%d" % t for t in range(2 * RO)] + ["snt%d" % t for t in range(2 * RO)]
+SETS = [dict(cy=0.86, ga=1.25, sc=3.0, pe=0.48, hop=260.0, rate=470.0, xr=400.0, lat=550.0),
+        dict(cy=0.92, ga=1.85, sc=4.5, pe=0.46, hop=210.0, rate=400.0, xr=300.0, lat=750.0),
+        dict(cy=0.85, ga=1.4, sc=3.8, pe=0.62, hop=200.0, rate=440.0, xr=350.0, lat=620.0)]
+PASSES, MOVES, HEAT, REACH, SPAN, SWEEPS, NEAR = 10, 1350000, 85.0, 10, 150, 60, 150.0
+COPY = ["vvgg", "vsggg", "vsggg", "vsgggg"]
 CAND = [[("c", 128), ("c", 64), ("a", 64)]] * 4
 AL, FK = 16.0, 1025.0
 OS = [3, 3, 3, 3]
 HS = [0, 0, 0, 0]
 HB = ["P1", "P2", "P1"]
 SMALL = "vvvs"
-LATE = ("U0", "RS", "RS2", "RS4", "CM", "SM", "IOT", "GT")
+LATE = ("U0", "RS2", "k5", "CM", "SM", "IOT", "GT", "B2", "IL", "PK", "io2")
 SEED = 12345
 ACL = True
+HEAD, FIRST, BEHIND = 0, 1000.0, False
 LOT = True
 HALF = True
 NHQ = (2, 2)
-OQ = [(3, 0)] * 4
+OQ = [(3, 0)] * 3 + [(2, 0)]
 EW = (256, 512)
-EC = "vv"
+EC = "gv"
 
 
 def runs_of(nh):
@@ -69,7 +70,11 @@ def runs_of(nh):
 
 HC = 512
 ORDER = []
-CG = {"a": 128, "b": 512, "c": 512}
+BN = {"pl": "M1", "xn": "M1", "pv": "P1", "hn": "M1"}
+NVT, E1, CVT = True, True, False
+TAIL = "M2b"
+NEWP = False
+CG = {"a": [256, 256, 128], "b": [512], "c": [512]}
 WIN = 8192
 
 
@@ -195,10 +200,10 @@ def build(g, T, rank, core, topo):
 
     nd = [0]
 
-    def dma(out, a, nbytes):
+    def dma(out, a, nbytes, behind=None):
         sem = "d%d" % nd[0]
         nd[0] += 1
-        add("y", lambda: g.sync.dma_start(ap(out), ap(a)), [out] if isinstance(out, dict) else [], [a], (60, 0, "cy"), sem=sem, nb=nbytes)
+        add("y", lambda: g.sync.dma_start(ap(out), ap(a)), [out] if isinstance(out, dict) else [], [a, behind], (60, 0, "cy"), sem=sem, nb=nbytes)
 
     def copy(eng, out, a):
         if eng == "s":
@@ -210,16 +215,16 @@ def build(g, T, rank, core, topo):
         else:
             dma(out, a, 256 * out["n"])
 
-    def push(t):
-        B = B0 + S * t
+    def push(t, lo, hi, k):
         dst = T.cores[(rank - JUMPS[t]) % len(T.cores)]
         rid, pid, se = topo.addr(dst)
-        src = ref("X", X0, X0 + B)
-        o = ref("xr%d" % t)
-        add("g", lambda: g.remote_dma(o["ap"], src["ap"], T.sem["arr%d" % t], T.sem["snt%d" % t], pid, rid, topo.mask(core, dst)),
-            [], [src], (600, 0, "cy"), sem="snt%d" % t, nb=B * 256, cnt=len(topo.engines(core, dst)), remote=True)
+        src = ref("X", X0 + lo, X0 + hi)
+        o = ref("xr%d" % t, lo, hi)
+        add("g", lambda: g.remote_dma(o["ap"], src["ap"], T.sem["arr%d" % k], T.sem["snt%d" % k], pid, rid, topo.mask(core, dst)),
+            [], [src], (600, 0, "cy"), sem="snt%d" % k, nb=(hi - lo) * 256, cnt=len(topo.engines(core, dst)), remote=True,
+            pre=FIRST if t == lo == 0 else 0.0, **({"after": len(ops) - 2} if lo and not t else {}))
         frm = T.cores[(rank + JUMPS[t]) % len(T.cores)]
-        add("x", None, [o], [], (0, 0, "cy"), sem="arr%d" % t, cnt=len(topo.engines(frm, core)), after=len(ops) - 1)
+        add("x", None, [o], [], (0, 0, "cy"), sem="arr%d" % k, cnt=len(topo.engines(frm, core)), after=len(ops) - 1)
 
     def swapped(bank, rows, mats, nh, start, *more):
         mms([x for c in range(2) for x in chain(r3(bank, c, 2 * rows, step0=2), list(more) + [
@@ -227,45 +232,42 @@ def build(g, T, rank, core, topo):
 
     halves = lambda c, h: 16 + 16 * (c - h)
 
+    if HEAD:
+        dma(ref("X", X0, X0 + HEAD), T.lab[:, 0:HEAD], 256 * HEAD)
     dma(ref("lf"), T.leaf[:], 8192)
     dma(ref("wt"), T.wts[:], 8192)
     dma(ref("cv"), T.cov[:], 65536)
-    dma(ref("X", X0, X0 + B0), T.lab[:], 524288)
+    dma(ref("X", X0 + HEAD, X0 + B0), T.lab[:, HEAD:B0], 256 * (B0 - HEAD))
     if not ACL:
         dma(ref("ac"), T.act[:], 262144)
     dma(ref("pt"), T.pth[:], 1048576)
+    if HEAD:
+        push(0, 0, HEAD, RO)
     first.append(len(ops))
-    push(0)
+    push(0, HEAD, B0, 0)
     if ACL:
-        dma(ref("ac"), T.act[:], 262144)
+        iota(ref("IOT"), [[1, 256]], 0, 0)
+        dma(ref("ac"), T.act[:], 262144, ref("IOT") if BEHIND else None)
     iota(ref("pc", 0, 1), [[0, 1]], 0, 1)
-    iota(ref("KEY"), [[0, 10], [1, 16]], 100, 0)
-    sel(ref("KEY"), ref("KEY"), [[-16, 10], [0, 16]], A.is_ge, 0.0, 16, 1)
-    sel(ref("KEY"), ref("KEY"), [[16, 10], [0, 16]], A.is_ge, 0.0, -1, -1)
+    iota(ref("KEY"), [[1, 160]], -16, -1)
+    iota(ref("GI"), [[1, 10], [0, 16]], -1, 0)
     iota(ref("io16"), [[1, 16]], 0, 0)
     iota(ref("IL"), [[16, 64]], B0, 1)
     iota(ref("SM"), [[0, 16], [1, 16]], 0, 0)
-    iota(ref("IOT"), [[1, 256]], 0, 0)
+    if not ACL:
+        iota(ref("IOT"), [[1, 256]], 0, 0)
     iota(ref("X", 0, X0), [[0, X0]], 300, 0)
-    iota(ref("KC"), [[0, 256]], int(16 * NONE) + NOT, 0)
     p = ref("pc", 0, 1)
-    ts(ref("pd", 0, 1), p, 4, A.arith_shift_right)
-    ts(ref("pd", 1, 2), p, 15, A.bitwise_and)
-    ts(ref("pd", 2, 3), p, 3, A.arith_shift_right, 1, A.bitwise_and)
-    ts(ref("pd", 3, 4), p, 3, A.bitwise_and)
-    ts(ref("pd", 4, 5), p, 5, A.arith_shift_right)
-    cp(ref("col", 0, 5), ref("pd", 0, 5))
-    cg, pm, up, lo4, pr, hf, lo8, hi4, b2 = [col(i) for i in range(9)]
-    ts(hf, pr, -2.0, A.mult, cg, A.add)
-    ts(lo8, up, -8.0, A.mult, pm, A.add)
-    ts(col(41), lo4, -0.25, A.mult)
-    ts(hi4, pm, 0.25, A.mult, col(41), A.add)
-    ts(b2, up, -2.0, A.mult, hi4, A.add)
-    ts(ref("BD"), ref("KEY"), 99.5, A.is_gt)
+    fields = [(4, 7), (4, 1), (5, 3), (3, 1), (0, 3), (2, 1), (0, 15), (1, 6), (0, 7), (0, 1), (1, 3)]
+    for i, (sh, mk) in enumerate(fields):
+        ts(ref("pd", i, i + 1), p, sh, A.arith_shift_right, mk, A.bitwise_and)
+    cp(ref("col", 0, 6), ref("pd", 0, 6))
+    cp(ref("col", 41, 46), ref("pd", 6, 11))
+    cg, hf, pr, up, lo4, b2 = [col(i) for i in range(6)]
+    pm, h6, lo8, odd, j4 = [col(41 + i) for i in range(5)]
+    ts(ref("BD"), ref("GI"), cg, A.is_equal)
     K = ref("KEY", 16, 144)
-    own = col(9)
-    ts(own, pm, 100.0, A.add)
-    ts(ref("I"), ref("KEY"), own, A.is_equal)
+    ts(ref("I"), ref("KEY"), 0.0, A.is_equal)
     I_, NI, BDm = ref("I", 16, 144), ref("NI"), ref("BD", 16, 144)
     ts(NI, I_, -1.0, A.mult)
     ts(col(10), hf, -1.0, A.mult, 1.0, A.add)
@@ -275,34 +277,34 @@ def build(g, T, rank, core, topo):
         ts(ref("BS", 160 * c, 160 * c + 160), ref("BD"), half[c], A.mult)
     ts(ref("wa"), ref("wt"), 2047.5, A.is_ge, -4096.0, A.mult)
     tt(ref("wf"), ref("wt"), ref("wa"), A.add)
-    ts(ref("pd", 9, 10), ref("wt", 0, 1), 1023, A.bitwise_and)
-    ts(col(11), ref("pd", 9, 10), 4.0, A.mult)
+    ts(ref("pd", 11, 12), ref("wt", 0, 1), 1023, A.bitwise_and)
+    ts(col(11), ref("pd", 11, 12), 4.0, A.mult)
     ts(ref("wl"), ref("io16", 0, 8), 0.0, A.mult, pm, A.add)
     ts(ref("k4"), BDm, 1.0 / 4096, A.mult)
     tt(ref("WB"), ind(ref("wf"), ref("wl")), ref("k4"), A.mult)
-    ts(ref("NH"), I_, -63.0 / 64, A.mult)
-    ts(ref("HF"), ref("KC"), 0.0, A.mult, 65.0 / 128, A.add)
+    ts(ref("NH"), I_, -63.0 / 8192, A.mult)
+    iota(ref("HF"), [[0, 256]], 65, 0)
     ms(ref("ZW"), 0.0)
     for c in range(2):
         ts(col(12 + c), half[1 - c], 100.0, A.mult, pr, A.add)
         for m, wc in enumerate((col(11), ref("wf", 1, 2))):
             ts(ref("ZW", 160 * c + 32 + m, 160 * c + 160, 32), ref("io16", 0, 4), col(12 + c), A.is_equal, wc, A.mult)
-    ts(col(14), lo4, 32.0, A.mult)
-    ts(col(15), hi4, 2.0, A.mult, col(14), A.add)
+    ts(col(15), lo4, 32.0, A.mult, h6, A.add)
     ts(ref("hp"), ref("io16", 0, 2), col(15), A.add)
     cp(ref("LU"), ref("lf"))
     ts(ref("LO"), ref("lf"), LOFF, A.add)
     ts(ref("c16"), ref("cv"), X0 - 1024.0, A.add)
     swapped("M1", 4, [("IS", lambda h: ref("c16", 64 * h, 64 * h + 64))], 2, halves)
     tr(ref("tc"), pq("M1", 0, 128))
-    ts(col(16), up, col(14), A.add)
+    ts(col(16), lo4, 32.0, A.mult, up, A.add)
     ts(col(17), b2, 16.0, A.mult, col(16), A.add)
     ts(ref("p2"), ref("io16", 0, 8), 2.0, A.mult, col(17), A.add)
     ts(ref("COV", 0, 128), ind(ref("tc"), ref("p2")), 1024.0, A.add)
     sg = col(20)
     ts(sg, up, 2.0, A.mult, -1.0, A.add)
-    ts(ref("SI"), I_, sg, A.mult)
-    ts(ref("SBD"), BDm, 1024.0, A.mult)
+    ts(col(22), up, 2.0 / 1024, A.mult, -1.0 / 1024, A.add)
+    ts(col(23), up, 2048.0, A.mult, -1024.0, A.add)
+    ts(ref("SI"), K, 0.0, A.is_equal, col(22), A.mult)
     if any(HS):
         ts(col(21), sg, 8192.0, A.mult, C0, A.add)
         ts(ref("SB2"), BDm, 512.0, A.mult)
@@ -313,11 +315,9 @@ def build(g, T, rank, core, topo):
     ts(ref("PK", 16, 144, 16), ref("BK", 16, 144, 16), -1.0, A.mult)
     ts(ref("PK", 24, 152, 16), ref("BK", 16, 144, 16), sg, A.mult)
     ts(ref("GT", 3, 35, 4), ref("BK", 16, 144, 16), 1.0, A.mult)
-    ts(col(23), lo8, 32.0, A.mult)
-    ts(col(24), up, 1.0 if HALF else 16.0, A.mult, col(23), A.add)
-    if HALF:
-        iota(ref("io2"), [[16, 2], [2, 8]], 0, 0)
-    ts(ref("p1"), ref("io2" if HALF else "io16"), col(24), A.add)
+    ts(col(24), lo8, 32.0, A.mult, up, A.add)
+    iota(ref("io2"), [[16, 2], [2, 8]], 0, 0)
+    ts(ref("p1"), ref("io2"), col(24), A.add)
     ts(col(25), up, -188416.0 - 1577216.0, A.mult, 1577216.0, A.add)
     ts(col(26), pm, -K2, A.mult, -17 * K2, A.add)
     ts(col(27), pm, -K2, A.mult, -K2 - LIVE, A.add)
@@ -331,55 +331,38 @@ def build(g, T, rank, core, topo):
         group(pq("A%d" % j, 0, 128), [(low, ref("U0")), (ref("k2", 16, 144), ref("k1"))])
         act(ref(nm), pq("A%d" % j, 0, 128), F.Copy)
     ts(ref("HB"), BDm, up, A.mult)
-    ts(col(33), pm, 101.0, A.add)
-    ts(ref("SH"), K, col(33), A.is_equal)
+    ts(col(33), pm, 14.5, A.is_lt)
+    ts(ref("SH"), K, 1.0, A.is_equal, col(33), A.mult)
     ts(col(34), pm, 0.0, A.is_equal)
     ts(ref("TOP"), I_, col(34), A.mult)
     for t in range(RO):
         ts(col(36 + t), col(34), B0 + S * t - 1024.0, A.mult, 1024.0 - LIVE, A.add)
     ts(ref("CM"), ref("SM"), pm, A.is_ge, 65536.0, A.mult)
-    if HALF:
-        ms(ref("GF"), 0.0)
-        for h in range(max(NHQ)):
-            ts(col(48 + h), pm, 16.0 * h, A.add)
-        for nh in sorted(set(NHQ)):
-            run = runs_of(nh)
-            for h in range(nh):
-                ts(ref("RS%d" % nh, run[h], run[h + 1]), ref("KC", 0, run[h + 1] - run[h]), 0.0, A.mult, col(48 + h), A.add)
-                iota(ref("RS%d" % nh, run[h] + 16 * h + 15, run[h + 1], 16 * h + 16), [[0, 8 // nh]], WIN, 0)
-            hh = lo4 if nh == 4 else col(55)
-            if nh == 2:
-                ts(ref("pd", 5, 6), p, 1, A.bitwise_and)
-                cp(hh, ref("pd", 5, 6))
-            ts(col(56), lo8, 1.0 / nh, A.mult)
-            ts(col(52), hh, 3.0 / nh, A.mult, col(56), A.add)
-            ts(col(53), hh, 16.0, A.mult, 16.0, A.add)
-            ts(col(54), col(52), col(53), A.mult, col(53), A.add)
-            ts(ref("EL", nh - 2, nh - 1), col(54), -2.0, A.add)
-    for h in range(0 if HALF else NH):
-        ts(col(48 + h), pm, 16.0 * h, A.add)
-        for a in range(RUN[h], RUN[h + 1], 256):
-            b = min(a + 256, RUN[h + 1])
-            ts(ref("RS", a, b), ref("KC", 0, b - a), 0.0, A.mult, col(48 + h), A.add)
-        iota(ref("RS", RUN[h] + 16 * h + 15, RUN[h + 1], 16 * h + 16), [[0, 16 // NH]], WIN, 0)
-    if not HALF:
-        ts(col(52), lo4, 2.0, A.mult, hi4, A.add)
-        ts(col(53), lo4, 16.0, A.mult, 16.0, A.add)
-        ts(col(54), col(52), col(53), A.mult, col(53), A.add)
-        ts(ref("EL", 0, 1), col(54), -2.0, A.add)
+    ms(ref("GF"), 0.0)
+    run = runs_of(2)
+    iota(ref("k5"), [[16, 2], [0, 128]], 0, 0)
+    ts(ref("RS2"), ref("k5", 64, 256), pm, A.add)
+    for h in range(2):
+        iota(ref("RS2", run[h] + 16 * h + 15, run[h + 1], 16 * h + 16), [[0, 4]], WIN, 0)
+    ts(col(52), odd, 2.0, A.mult, j4, A.add)
+    ts(col(53), odd, 16.0, A.mult, 16.0, A.add)
+    ts(col(54), col(52), col(53), A.mult, col(53), A.add)
+    ts(ref("EL", 0, 1), col(54), -2.0, A.add)
     ts(col(40), cg, -16.0, A.mult, -1024.0, A.add)
     ts(ref("I16"), ref("IL"), col(40), A.add)
     if LOT:
         iota(ref("B2"), [[0, 160]], 0, 0)
         for u in range(2):
             ts(ref("B2", 16 + u, 144, 16), ref("BK", 16, 144, 16), 1.0, A.mult)
-            ts(col(57 + u), col(55), 1.0 - u, A.is_equal, -32768.0, A.mult)
+            ts(col(57 + u), odd, 1.0 - u, A.is_equal, -32768.0, A.mult)
             ts(ref("I32", u, 128, 2), ref("I16"), col(57 + u), A.add)
+            if CVT:
+                ts(ref("MK", u, 32, 2), ref("io16"), 0.0, A.mult, col(57 + u), A.add)
     early[0] = False
 
     def path_list():
-        swapped("M1", 8, [("IS", lambda h: ref("PV", 128 * h, 128 * h + 128))], 2, halves)
-        tr(ref("tp"), pq("M1", 0, 256))
+        swapped(BN["pl"], 8, [("IS", lambda h: ref("PV", 128 * h, 128 * h + 128))], 2, halves)
+        tr(ref("tp"), pq(BN["pl"], 0, 256))
         ts(ref("PL"), ind(ref("tp"), ref("p1")), 1024.0, A.add)
 
     def hold(t, lo, hi, banks):
@@ -388,8 +371,8 @@ def build(g, T, rank, core, topo):
         for i, a in enumerate(range(lo, hi, 512)):
             b = min(hi, a + 512)
             bank = pq(banks[i % len(banks)], 0, b - a)
-            group(bank, [(ref("SI"), ref("X", X0 + a, X0 + b)), (ref("SBD"), ref("C", a, b))], 1)
-            act(ref("TT", a, b), bank, F.Identity, bias=C0, scale=sg)
+            group(bank, [(ref("SI"), ref("X", X0 + a, X0 + b)), (BDm, ref("C", a, b))], 1)
+            act(ref("TT", a, b), bank, F.Identity, bias=C0, scale=col(23))
 
     def hold_s(t, a, b, bank):
         bank = pq(bank, 0, b - a)
@@ -410,7 +393,9 @@ def build(g, T, rank, core, topo):
         fr = (8 + t) / 16.0
         old = B if t == 0 else B - S
         if t:
-            push(t)
+            if NEWP:
+                push(t, old, B, RO + t)
+            push(t, 0, old if NEWP else B, t)
         cuts = list(range(0, old, 512)) + [old] + ([B] if t else [])
         for i in range(len(cuts) - 1):
             a, b = cuts[i], cuts[i + 1]
@@ -440,8 +425,10 @@ def build(g, T, rank, core, topo):
             if kind == "a":
                 for m in range(16):
                     copy("g", ref("XK", 16 * s0 + m, 16 * s1, 16), ref("z%d" % (t & 1), s0, s1))
-            for a in range(s0, s1, CG[kind] // 16):
-                b = min(s1, a + CG[kind] // 16)
+            cuts = [s0]
+            while cuts[-1] < s1:
+                cuts.append(min(s1, cuts[-1] + CG[kind][min(len(cuts), len(CG[kind])) - 1] // 16))
+            for a, b in zip(cuts, cuts[1:]):
                 src = ind(ref(snap, 0, B), ref("CL", a, b))
                 if kind == "a":
                     tt(ref("SG", 16 * a, 16 * b), src, ref("XK", 16 * a, 16 * b), A.is_le)
@@ -473,7 +460,7 @@ def build(g, T, rank, core, topo):
             s0, pb, wb, nh = 128 * q, "P%d" % (q + 1), ("M0", "M2b")[q], NHQ[q]
             for n, k in enumerate((12, 8, 4, 0)):
                 if k == 0 and t and q:
-                    hold(t, old, B, ["M1"])
+                    hold(t, old, B, [BN["hn"]])
                 a = 2048 * q + 128 * k
                 win = ref("TT", 0, old if k else B)
                 if n < OQ[t][q]:
@@ -481,7 +468,7 @@ def build(g, T, rank, core, topo):
                     for b in (a, a + 256):
                         tt(ref("O", b, b + 256), ref("OG", b, b + 256), pq("M0", 256 * q, 256 * q + 256), A.subtract)
                 else:
-                    w = EW[q]
+                    w = 256 if q and n == OQ[t][q] and E1 else EW[q]
                     for b in range(a, a + 512, w):
                         tt(ref("O", b, b + w), ind(win, ref("PL", b // 16, (b + w) // 16)), ref("EE", 512, 512 + w) if q else ref("EE", 512 - w, 512), A.subtract)
                 for j0 in (k + 2, k):
@@ -498,7 +485,8 @@ def build(g, T, rank, core, topo):
             group(r3(wb, 16, 24, step0=2), [(BDm, r3("MT", 8 * q, 8 * q + 8, step0=2))]) if nh == 2 else group(pq(wb, 256, 384), [(BDm, mt)])
             tr(r3("LR", 8 * q, 8 * q + 8), pq(wb, 0, 128))
             top = r3("LR", 8 * q, 8 * q + 8, 0, 1)
-            ts(ref("GL", 8 * q, 8 * q + 8), top, 16 * NONE + NOT - X0, A.add)
+            if not (q and NVT):
+                ts(ref("GL", 8 * q, 8 * q + 8), top, 16 * NONE + NOT - X0, A.add)
             act(ref("GF", 8 * q, 8 * q + 8), top, F.Identity, bias=16 * NONE + NOT)
             run = [320 * q + x for x in runs_of(nh)]
             for h in range(nh):
@@ -509,7 +497,7 @@ def build(g, T, rank, core, topo):
             add("v", lambda kp=kp, rs=rs, ne=ne: g.vector.tensor_tensor_scan(kp["ap"], ne["ap"], rs["ap"], float(WIN), A.mult, A.max), [kp], [rs, ne], (0, max(64, kp["n"] // 2), "cy"))
             tt(ref("vt", 16 * q, 16 * q + 16), ind(kp, ref("EL", nh - 2, nh - 1)), ref("GF", 8 * q, 8 * q + 16), A.min)
             cp(ref("TL", 8 * q, 8 * q + 8), ref("vt", 16 * q, 16 * q + 8))
-            tt(ref("NV", s0, s0 + 128), ind(ref(snap, 0, B), ref("GL", 8 * q, 8 * q + 8)), ref("EE", 384 + s0, 512 + s0), A.max)
+            tt(ref("NV", s0, s0 + 128), ind(Xa, ref("TL", 8, 16)) if q and NVT else ind(ref(snap, 0, B), ref("GL", 8 * q, 8 * q + 8)), ref("EE", 384 + s0, 512 + s0), A.max)
             for b in range(8 * q + 8 - nh, 8 * q - 1, -nh):
                 cp(ind(Xa, ref("TL", b, b + nh)), ref("NV", 16 * b, 16 * (b + nh)))
         if HALF:
@@ -562,12 +550,12 @@ def build(g, T, rank, core, topo):
             ts(ref("LU"), ref("LO"), -LOFF, A.add)
         else:
             act(ref("LV"), ref("LO"), F.Identity, bias=-LOFF)
-        group(pq("M1", 0, 256), [(I_, z), (NI, lv)])
+        group(pq(BN["xn"], 0, 256), [(I_, z), (NI, lv)])
         if SMALL[2] == "s":
             act(ref("Y"), pq("M1", 0, 256), F.Relu, scale=-1.0, bias=256.0 - LIVE)
             act(ref("X", X0 + B, X0 + B + S), ref("Y"), F.Identity, bias=256.0, scale=-1.0)
         else:
-            ts(ref("X", X0 + B, X0 + B + S), pq("M1", 0, 256), LIVE, A.add, 256.0, A.min)
+            ts(ref("X", X0 + B, X0 + B + S), pq(BN["xn"], 0, 256), LIVE, A.add, 256.0, A.min)
         group(pq("P2", 0, 256), [(ref("SH"), ref("PV")), (ref("TOP"), ref("IOT")), (I_, lv)])
         yp = ref("YP", S * t, S * t + S)
         act(yp, pq("P2", 0, 256), F.Relu, bias=col(36 + t))
@@ -575,11 +563,11 @@ def build(g, T, rank, core, topo):
         yc = pq("P1", 0, 256, (0, 32))
         if not last:
             act(ref("yq"), yp, F.Identity, bias=-1024.0)
-            group(pq("P1", 0, 256), [(I_, ref("PV")), (NI, lv)])
-            tt(ref("PV"), pq("P1", 0, 256), ref("yq"), A.max)
+            group(pq(BN["pv"], 0, 256), [(I_, ref("PV")), (NI, lv)])
+            tt(ref("PV"), pq(BN["pv"], 0, 256), ref("yq"), A.max)
             path_list()
-        else:
-            mms([(yc, ref("GT", 3 - r, 35 - r), ref("M2", S * r, S * r + S), r == 0, False) for r in range(t)])
+        elif not TAIL:
+            mms([(yc, ref("GT", 3 - r, 35 - r), r3("M2", 16 * r, 16 * r + 16), r == 0, False) for r in range(t)])
         n = 0
         two = all(kind != "b" for kind, s0, s1 in runs)
         for kind, s0, s1 in runs:
@@ -599,19 +587,35 @@ def build(g, T, rank, core, topo):
                 for m in range(16):
                     tt(ref("SG", 16 * s0 + w * m, 16 * s0 + w * m + w), ref("XK", 16 * s0 + m, 16 * s1, 16), pq("A1", 0, w), A.is_le)
             for m0 in range(0, 16, 4):
-                mms([(pq("CB", s0, s1), ref("BK" if kind == "c" else "BA", 16 - m, 144 - m),
+                mms([(pq(TAIL if last and TAIL and s0 >= 128 else "CB", s0, s1), ref("BK" if kind == "c" else "BA", 16 - m, 144 - m),
                       ref("SG", 16 * s0 + m, 16 * s1, 16) if kind == "a" else ref("SG", 16 * s0 + w * m, 16 * s0 + w * m + w), m == 0, m == 15)
                      for m in range(m0, m0 + 4)])
         act(ref("py", t, t + 1), ref("cn", t, t + 1), F.Identity, bias=-512.5 * AL, scale=AL / LIVE)
         act(ref("pb", t, t + 1), ref("cn", t, t + 1), F.Identity, bias=ref("py", t, t + 1), scale=-AL / LIVE)
+        if last and TAIL:
+            for a, cb, yb in ((0, "CB", "P1"), (128, TAIL, "P2")):
+                yc = pq(yb, 0, 128, (0, 32))
+                m2 = lambda r: r3("M2", 16 * r + a // 16, 16 * r + a // 16 + 8)
+                mms([(yc, ref("GT", 3 - r, 35 - r), m2(r), r == 0, False) for r in range(t)])
+                act(ref("FS", a, a + 128), pq(cb, a, a + 128), F.Sign, bias=ref("pb", t, t + 1), scale=FK)
+                group(pq(cb, a, a + 128), [(ref("U0"), ref("FS", a, a + 128)), (I_, r3(lvn, a // 16, a // 16 + 8)), (I_, ref("cs%d" % (t & 1), a, a + 128))])
+                ts(m2(t), pq(cb, a, a + 128), col(27), A.add, -1025.0, A.max)
+                mms([(yc, ref("GT", 3 - t, 35 - t), m2(t), False, True)])
+                act(ref("YC", a, a + 128, parts=(0, 32)), yc, F.Identity, bias=16399.0)
+            continue
         act(ref("FS"), pq("CB", 0, 256), F.Sign, bias=ref("pb", t, t + 1), scale=FK)
         group(pq("CB", 0, 256), [(ref("U0"), ref("FS")), (I_, lv), (I_, cs)])
-        ts(ref("M2", S * t, S * t + S), pq("CB", 0, 256), col(27), A.add, -1025.0, A.max)
-        if not last:
-            group(r3("CB", 0, 1, 0, 16), [(ref("BK", 16 - i, 144 - i), ref("M2", S * t + i, S * t + S, 16)) for i in range(16)])
+        ts(r3("M2", 16 * t, 16 * t + 16), pq("CB", 0, 256), col(27), A.add, -1025.0, A.max)
+        if not last and CVT:
+            group(r3("CB", 0, 1), [(I_, ref("MK"))] + [(ref("B2", 16 - i, 144 - i), r3("M2", 16 * t, 16 * t + 16, i, i + 2)) for i in range(0, 16, 2)])
+            act(ref("cw"), r3("CB", 0, 1, 0, 32, 2), F.Copy)
+            tt(ref("cw"), r3("CB", 0, 1, 1, 32, 2), ref("cw"), A.max)
+            ts(ref("COV", B // 16, B // 16 + 16), ref("cw"), 16399.0 + X0, A.add)
+        elif not last:
+            group(r3("CB", 0, 1, 0, 16), [(ref("BK", 16 - i, 144 - i), r3("M2", 16 * t, 16 * t + 16, i, i + 1)) for i in range(16)])
             ts(ref("COV", B // 16, B // 16 + 16), r3("CB", 0, 1, 0, 16), 16399.0 + X0, A.add)
         else:
-            mms([(yc, ref("GT", 3 - t, 35 - t), ref("M2", S * t, S * t + S), False, True)])
+            mms([(yc, ref("GT", 3 - t, 35 - t), r3("M2", 16 * t, 16 * t + 16), False, True)])
             act(ref("YC", parts=(0, 32)), yc, F.Identity, bias=16399.0)
     dma(T.yx[:, 0:W - S], ref("X", X0, X0 + W - S), 720896)
     dma(T.yx[:, W - S:W], ref("X", X0 + W - S, X0 + W), 65536)
@@ -656,7 +660,7 @@ def schedule(ops):
         per = {"cy": m["cy"], "ga": m["cy"] * m["ga"], "sc": m["cy"] * m["sc"], "pe": m["pe"]}
         dur = [o["nb"] / m["xr" if o.get("remote") else "rate"] + 60 if "nb" in o else o["c"][0] + o["c"][1] * per[o["c"][2]] for o in ops]
         tail = [m["lat"] + (600 if o.get("remote") else 0) if "nb" in o else 0 for o in ops]
-        pred = [[(j, tail[j] + m["hop"] if w else tail[j] if o["e"] != "g" else -dur[j]) for j, w in o["d"].items()] for o in ops]
+        pred = [[(j, tail[j] + m["hop"] if w else tail[j] if o["e"] != "g" else -1e6) for j, w in o["d"].items()] for o in ops]
         sets.append((dur, tail, pred))
     dur, tail, pred = sets[0]
     post = [[] for _ in ops]
@@ -686,6 +690,7 @@ def schedule(ops):
 
     que = ["vspgyx".index(o["e"]) for o in ops]
     issue = [o["c"][0] if "nb" in o else -1 for o in ops]
+    pre = [o.get("pre", 0.0) for o in ops]
     ends = [i for i in range(n) if not post[i]]
 
     def replay(seq, s, start=0, base=None):
@@ -704,6 +709,7 @@ def schedule(ops):
                 if issue[i] >= 0:
                     free[e] = t + issue[i]
                     e = 6
+                    t += pre[i]
                     if free[6] > t:
                         t = free[6]
                 end[i] = free[e] = t + du[i]
@@ -806,7 +812,7 @@ def schedule(ops):
                 st[i] = t
                 if issue[i] >= 0:
                     fr[i] = t + issue[i]
-                    end[i] = max(t, end[bd[i]]) + du[i]
+                    end[i] = max(t + pre[i], end[bd[i]]) + du[i]
                 else:
                     end[i] = fr[i] = t + du[i]
             for i in reversed(seq[r0:hi + 1]):
@@ -817,7 +823,7 @@ def schedule(ops):
                         t = x
                 if issue[i] >= 0:
                     dn[i] = max(t, dn[ad[i]]) + du[i]
-                    up[i] = max(dn[i], issue[i] + up[aq[i]])
+                    up[i] = max(pre[i] + dn[i], issue[i] + up[aq[i]])
                 else:
                     x = up[aq[i]]
                     up[i] = (x if x > t else t) + du[i]
@@ -849,7 +855,7 @@ def schedule(ops):
             if j < n and st[i] + up[i] >= bar and fr[j] >= st[i] - 1e-6 and pos[j] >= r0:
                 out.append((j, i))
             j = bd[i]
-            if j < n and end[i] - du[i] + dn[i] >= bar and end[j] > st[i] and pos[j] >= r0:
+            if j < n and end[i] - du[i] + dn[i] >= bar and end[j] > st[i] + pre[i] and pos[j] >= r0:
                 out.append((j, i))
         return out
 
@@ -868,7 +874,7 @@ def schedule(ops):
             (ad if e == 6 else aq)[last[e]] = k
             (bd if e == 6 else bq)[k] = last[e]
 
-    def price(old, mid, tot):
+    def price(old, mid, tot, room):
         free, nxt, low = {}, {}, 0.0
         for i in old:
             free.setdefault(que[i], bq[i])
@@ -889,7 +895,7 @@ def schedule(ops):
                 if issue[i] >= 0:
                     f[e] = t + issue[i]
                     e = 6
-                    t = max(t, f[6])
+                    t = max(t + pre[i], f[6])
                 new[i] = f[e] = t + du[i]
                 x = st[i] + up[i]
                 if x > through:
@@ -903,8 +909,10 @@ def schedule(ops):
                     top = new[i] + t
             for e, k in nxt.items():
                 top = max(top, f[e] + (dn if e == 6 else up)[k])
-            low += top if through > was - 1e-6 or top > was else was
-        return low / len(sets), free, nxt
+            low += (top if through > was - 1e-6 or top > was else was) - was
+            if low > room + 100.0:
+                break
+        return low, free, nxt
 
     best = (1e18, seq[:])
     starts = list(range(0, n - SPAN // 2, SPAN // 2))
@@ -956,8 +964,9 @@ def schedule(ops):
                 if mid == old:
                     continue
                 bar = now - heat * math.log(1.0 - rnd())
-                low, free, nxt = price(old, mid, tot)
-                if low > bar:
+                room = (bar - now) * len(sets)
+                low, free, nxt = price(old, mid, tot, room)
+                if low > room:
                     continue
                 pu, pv = pos[u], pos[v]
                 relink(pu, mid, free, nxt)

@@ -13,68 +13,76 @@ NOT = 32
 NONE = 1024.0 + X0 - NOT
 BIG = 12582912.0
 LOFF = 16 * LIVE - 1024
-NH = 4
-RUN = [256 // NH * h * (h + 1) // 2 for h in range(NH + 1)]
+KM, KN = 524288.0, 16384.0
 bf, f32, i32, u16, f16 = "bfloat16", "float32", "int32", "uint16", "float16"
 SB = {
-    "X": ([X0 + W], bf), "XA": ([W - S], bf), "XB": ([W - S], bf), "xr0": ([2048], bf), "xr1": ([2304], bf), "xr2": ([2560], bf), "xr3": ([2816], bf),
-    "TT": ([2816], f32), "pt": ([2048], i32), "ac": ([1024], bf), "cv": ([128], i32), "wt": ([16], i32), "lf": ([16], i32),
-    "O": ([4096], bf), "OG": ([4096], f32), "XK": ([4096], bf), "SG": ([4096], bf), "C": ([2816], bf), "YP": ([1024], f32), "YC": ([256], f32),
+    "X": ([X0 + W], bf), "XA": ([X0 + W - S], bf), "XB": ([X0 + W - S], bf), "xr0": ([2048], bf), "xr1": ([2304], bf), "xr2": ([2560], bf), "xr3": ([2816], bf),
+    "pt": ([2048], i32), "ac": ([1024], bf), "cv": ([128], i32), "wt": ([16], i32), "lf": ([16], i32),
+    "O": ([4096], bf), "SG": ([4096], bf), "C": ([2816], bf), "YP": ([1024], f32), "YC": ([256], f32),
     "COV": ([192], u16), "PL": ([256], u16), "LU": ([16], u16), "LV": ([16], f32), "PV": ([256], f16),
-    "xv": ([256], bf), "av": ([256], bf), "z0": ([256], bf), "z1": ([256], bf), "E": ([512], bf), "EM": ([256], bf),
+    "xv": ([256], bf), "av": ([256], bf), "z0": ([256], bf), "z1": ([256], bf), "EB": ([256], bf), "EM": ([256], bf),
     "tx": ([128], f32), "hi": ([32], i32), "ha": ([32], i32), "LA": ([16], u16), "LQ": ([16], u16), "hp": ([2], u16),
-    "cq": ([256], f16), "NH": ([128], bf), "HF": ([256], bf), "k4": ([128], bf), "LO": ([16], f32), "I16": ([64], f16), "py": ([4], bf), "CL": ([256], u16), "cs0": ([256], f16), "cs1": ([256], f16),
+    "cq": ([256], f16), "NH": ([128], bf), "HF": ([256], bf), "k4": ([128], bf), "LO": ([16], f32), "I16": ([64], f16), "py": ([4], bf),
+    "rm": ([256], f16), "CU": ([256], u16), "CL": ([256], u16), "tq": ([256], f32), "p3": ([16], u16), "cs0": ([256], f16), "cs1": ([256], f16),
     "F1": ([256], bf), "F2": ([256], bf), "lv0": ([16, 16], bf), "lv1": ([16, 16], bf), "MT": ([16, 16], f16),
-    "LR": ([16, 16], f32), "NE": ([RUN[NH]], bf), "KP": ([RUN[NH]], bf), "RS": ([RUN[NH]], bf), "vt": ([32], f32), "GL": ([16], u16),
+    "LR": ([16, 16], f32), "NE": ([8, 50], bf), "KP": ([8, 50], f32), "RS": ([8, 50], f32), "GL": ([16], u16),
     "TL": ([16], u16), "NV": ([256], bf), "Y": ([256], bf), "yq": ([256], f32), "tp": ([256], f32),
-    "BA": ([160], f16), "EL": ([4], u16), "GF": ([24], f32), "EE": ([1024], bf), "RS2": ([192], bf), "io2": ([16], f32), "B2": ([160], bf), "I32": ([128], f16), "cn": ([4], f32), "pb": ([4], f32), "FS": ([256], bf), "M2": ([64, 16], f16), "MK": ([32], bf), "cw": ([16], f32),
-    "KEY": ([160], bf), "k1": ([128], bf), "k2": ([160], bf), "k3": ([128], bf), "SI": ([128], bf),
-    "pc": ([4], i32), "GI": ([160], bf), "k5": ([256], bf), "pd": ([12], i32), "col": ([64], f32), "XC": ([1536], bf), "SB2": ([128], bf), "IL": ([64], f32), "io16": ([16], f32), "IOT": ([256], bf),
-    "SM": ([256], bf), "I": ([160], bf), "NI": ([128], bf), "BD": ([160], bf), "SBD": ([128], bf),
+    "EC": ([1536], f32), "ZC": ([2048], f32), "L0": ([160], bf), "LM": ([160], bf), "BAR": ([160], bf), "XC": ([2560], bf), "OG": ([4096], bf),
+    "BM": ([160], bf), "BN": ([128], bf),
+    "io2": ([16], f32), "B2": ([160], bf), "I32": ([128], f16), "cn": ([4], f32), "pb": ([4], f32), "FS": ([256], bf), "M2": ([64, 16], f16),
+    "KEY": ([160], bf), "k1": ([128], bf), "k2": ([160], bf), "k3": ([128], bf),
+    "pc": ([4], i32), "GI": ([160], bf), "pd": ([12], i32), "col": ([64], f32), "IL": ([64], f32), "io16": ([16], f32), "IOT": ([256], bf),
+    "SM": ([256], bf), "I": ([160], bf), "NI": ([128], bf), "BD": ([160], bf),
     "BK": ([160], bf), "PK": ([160], bf), "U0": ([128], bf), "U1": ([128], bf), "U2": ([128], bf), "HB": ([128], bf),
     "SH": ([128], bf), "TOP": ([128], bf), "BS": ([320], bf), "IS": ([320], bf), "ZW": ([320], f16),
     "WB": ([128], f16), "GT": ([36], bf), "CM": ([256], bf), "wa": ([16], f32), "wf": ([16], f32),
     "wl": ([8], u16), "p1": ([16], u16), "p2": ([8], u16), "c16": ([128], f16), "tc": ([128], f32),
 }
-PS = {"A0": [16, 32], "A1": [16, 32], "CB": [16, 32], "P1": [16, 32], "P2": [16, 32], "M0": [32, 16], "M1": [32, 16], "M2b": [32, 16]}
+PS = {"A0": [32, 16], "A1": [32, 16], "CB": [32, 16], "P1": [32, 16], "P2": [32, 16], "M0": [32, 16], "M1": [32, 16], "M2b": [32, 16]}
 SCRATCH = {k: ("sbuf", [128] + v[0], v[1]) for k, v in SB.items()}
 SCRATCH.update({k: ("psum", [128] + v, f32) for k, v in PS.items()})
-NDMA = 40
+NDMA = 100
 SEMAPHORES = ["v", "s", "p", "g"] + ["d%d" % i for i in range(NDMA)] + ["arr%d" % t for t in range(2 * RO)] + ["snt%d" % t for t in range(2 * RO)]
-SETS = [dict(cy=0.86, ga=1.25, sc=3.0, pe=0.48, hop=260.0, rate=470.0, xr=400.0, lat=550.0),
-        dict(cy=0.92, ga=1.85, sc=4.5, pe=0.46, hop=210.0, rate=400.0, xr=300.0, lat=750.0),
-        dict(cy=0.85, ga=1.4, sc=3.8, pe=0.62, hop=200.0, rate=440.0, xr=350.0, lat=620.0)]
-PASSES, MOVES, HEAT, REACH, SPAN, SWEEPS, NEAR = 10, 1350000, 85.0, 10, 150, 60, 150.0
-COPY = ["vvgg", "vsggg", "vsggg", "vsgggg"]
-CAND = [[("c", 128), ("c", 64), ("a", 64)]] * 4
-AL, FK = 16.0, 1025.0
-OS = [3, 3, 3, 3]
-HS = [0, 0, 0, 0]
-HB = ["P1", "P2", "P1"]
-SMALL = "vvvs"
-LATE = ("U0", "RS2", "k5", "CM", "SM", "IOT", "GT", "B2", "IL", "PK", "io2")
+SETS = [dict(cy=0.84, ga=1.3, sc=3.2, pe=0.47, hop=240.0, rate=450.0, xr=400.0, lat=650.0),
+        dict(cy=0.95, ga=1.65, sc=4.2, pe=0.56, hop=210.0, rate=400.0, xr=330.0, lat=700.0)]
+PLACE, ROWS, AHEAD = True, "chp", 600.0
+STAGES = ((0, 0.3, 0.27, 50, 200.0), (0.3, 0.6, 0.27, 40, 200.0), (0, 1, 0.12, 10, 50.0), (0.55, 0.8, 0.14, 20, 80.0), (0.74, 1, 0.2, 30, 120.0))
+NVG = (True, True)
+PASSES, MOVES, HEAT, REACH, SPAN, SWEEPS, NEAR = 0, 1800000, 130.0, 10, 150, 70, 150.0
+COPY = ["vvgg", "vvggg", "vvggg", "vvggg"]
+CAND = [[("d", 4), ("d", 4), ("d", 4), ("v", 4)]] * 3 + [[("d", 4), ("d", 4), ("v", 8)]]
+CM = 2
+AL, FK = 16.0, -1025.0 / 256
+SMALL = "vvvss"
+SAME = False
+OVER = False
+LATE = ("U0", "NE", "CM", "SM", "IOT", "GT", "B2", "IL", "PK", "io2", "c184", "BM")
 SEED = 12345
-ACL = True
-HEAD, FIRST, BEHIND = 0, 1000.0, False
-LOT = True
-HALF = True
+FIRST = 1000.0
+GI, ACC, GP, GL = 1300.0, 2.0, 1100.0, 300.0
 NHQ = (2, 2)
-OQ = [(3, 0)] * 3 + [(2, 0)]
-EW = (256, 512)
-EC = "gv"
+OQ = [("ssvv", "svvv")] * 4
+EB = ("A1", "A1")
+KC = ((4, 3, 0), (4, 3, 0))
+JOIN = True
+EC = ("ggg", "vg")
+ZC = "dd"
 
 
 def runs_of(nh):
     return [128 // nh * h * (h + 1) // 2 for h in range(nh + 1)]
 
 
-HC = 512
+PLAN = {"first": 3.0, "round": 14.3, "start": 0.0, "hold": 0.3, "label": 2.3, "repeat": 3.3, "answer": 3.5, "paths": 4.6, "piece": 0.75,
+        "newest": 5.6, "number": 12.0, "upper": 7.6, "lower": 9.0, "live": 9.8, "candd": 7.5, "candv": 10.0, "per": 0.4, "count": 11.5, "cover": 16.5}
 ORDER = []
-BN = {"pl": "M1", "xn": "M1", "pv": "P1", "hn": "M1"}
-NVT, E1, CVT = True, True, False
-TAIL = "M2b"
-NEWP = False
-CG = {"a": [256, 256, 128], "b": [512], "c": [512]}
+BN = {"pl": "M1", "xn": "M1", "pv": "P1", "cl": "M1", "mk": "A0"}
+SC = (0, 2, 6, 10, 16)
+HC = (("v", 0, 2), ("s", 10, 12), ("v", 2, 4), ("s", 12, 14), ("v", 4, 6), ("v", 6, 8), ("s", 14, 16), ("v", 8, 10))
+HS, HB, OB = 2, ("P1", "P2", "A1"), ("A1", "M0", "A0")
+E1 = (4, 1)
+TAIL = "A0"
+CG = {"v": 256, "d": 512}
 WIN = 8192
 
 
@@ -99,7 +107,8 @@ def build(g, T, rank, core, topo):
         b1 = sh[1] if b1 is None else b1
         p = slice(0, 128) if parts is None else slice(parts[0], parts[1])
         ap = T[name][p, a0:a1:step0, b0:b1:step]
-        return {"ap": ap, "rg": [(name, a0 * sh[1] + b0, (a1 - 1) * sh[1] + b1, (1, 0))], "n": len(range(a0, a1, step0)) * len(range(b0, b1, step)),
+        rows = [(a0, a1 - 1)] if ps or b1 - b0 == sh[1] else [(a, a) for a in range(a0, a1, step0)]
+        return {"ap": ap, "rg": [(name, a * sh[1] + b0, b * sh[1] + b1, (1, 0)) for a, b in rows], "n": len(range(a0, a1, step0)) * len(range(b0, b1, step)),
                 "two": (not ps) and SB[name][1] in (bf, u16, f16), "ps": ps, "ind": False}
 
     def pq(name, lo, hi, parts=None):
@@ -119,11 +128,24 @@ def build(g, T, rank, core, topo):
         for x in outs:
             Wr += x["rg"]
             R += x.get("off", [])
-        o = {"e": eng, "fn": fn, "R": R, "W": Wr, "c": cost, "id": len(ops)}
+        o = {"e": eng, "fn": fn, "R": R, "W": Wr, "c": cost, "id": len(ops), "at": now[0], "t": now[3]}
+        now[0] += now[1]
         o.update(kw)
         if eng == "g" and early[0] and outs and outs[0]["rg"][0][0] in LATE:
             o["after"] = first[0]
         ops.append(o)
+
+    now = [0.0, 0.03, 0.0, -1]
+
+    def at(name, more=0.0, step=0.4):
+        now[0], now[1] = now[2] + PLAN[name] + more, step
+
+    rows = {}
+
+    def row(name):
+        if name in rows and name[0] in ROWS:
+            ops[-1].setdefault("behind", []).append(rows[name])
+        rows[name] = len(ops) - 1
 
     first = []
 
@@ -200,10 +222,20 @@ def build(g, T, rank, core, topo):
 
     nd = [0]
 
-    def dma(out, a, nbytes, behind=None):
+    def dma(out, a, nbytes):
         sem = "d%d" % nd[0]
         nd[0] += 1
-        add("y", lambda: g.sync.dma_start(ap(out), ap(a)), [out] if isinstance(out, dict) else [], [a, behind], (60, 0, "cy"), sem=sem, nb=nbytes)
+        add("y", lambda: g.sync.dma_start(ap(out), ap(a)), [out] if isinstance(out, dict) else [], [a], (60, 0, "cy"), sem=sem, nb=nbytes)
+
+    def added(out, a):
+        sem = "d%d" % nd[0]
+        nd[0] += 1
+        add("g", lambda: g.dma_start(out["ap"], a["ap"], accum_op=A.add), [out], [out, a], (GI, 0, "cy"), sem=sem, nb=256 * ACC * out["n"], pre=GP, late=GL)
+
+    def lane0(lo, hi):
+        r = ref("X", X0 + lo, X0 + hi)
+        r["ap"] = T["X"][0:128:16, X0 + lo:X0 + hi]
+        return r
 
     def copy(eng, out, a):
         if eng == "s":
@@ -213,7 +245,7 @@ def build(g, T, rank, core, topo):
         elif eng == "g":
             sel(out, a, [[1, a["n"]]], A.is_ge, 0.0, 0, 0)
         else:
-            dma(out, a, 256 * out["n"])
+            dma(out, a, (256 if out["two"] else 512) * out["n"])
 
     def push(t, lo, hi, k):
         dst = T.cores[(rank - JUMPS[t]) % len(T.cores)]
@@ -222,7 +254,7 @@ def build(g, T, rank, core, topo):
         o = ref("xr%d" % t, lo, hi)
         add("g", lambda: g.remote_dma(o["ap"], src["ap"], T.sem["arr%d" % k], T.sem["snt%d" % k], pid, rid, topo.mask(core, dst)),
             [], [src], (600, 0, "cy"), sem="snt%d" % k, nb=(hi - lo) * 256, cnt=len(topo.engines(core, dst)), remote=True,
-            pre=FIRST if t == lo == 0 else 0.0, **({"after": len(ops) - 2} if lo and not t else {}))
+            pre=0.0 if t else FIRST, late=600.0)
         frm = T.cores[(rank + JUMPS[t]) % len(T.cores)]
         add("x", None, [o], [], (0, 0, "cy"), sem="arr%d" % k, cnt=len(topo.engines(frm, core)), after=len(ops) - 1)
 
@@ -232,39 +264,31 @@ def build(g, T, rank, core, topo):
 
     halves = lambda c, h: 16 + 16 * (c - h)
 
-    if HEAD:
-        dma(ref("X", X0, X0 + HEAD), T.lab[:, 0:HEAD], 256 * HEAD)
     dma(ref("lf"), T.leaf[:], 8192)
     dma(ref("wt"), T.wts[:], 8192)
     dma(ref("cv"), T.cov[:], 65536)
-    dma(ref("X", X0 + HEAD, X0 + B0), T.lab[:, HEAD:B0], 256 * (B0 - HEAD))
-    if not ACL:
-        dma(ref("ac"), T.act[:], 262144)
+    dma(ref("X", X0, X0 + B0), T.lab[:], 256 * B0)
     dma(ref("pt"), T.pth[:], 1048576)
-    if HEAD:
-        push(0, 0, HEAD, RO)
     first.append(len(ops))
-    push(0, HEAD, B0, 0)
-    if ACL:
-        iota(ref("IOT"), [[1, 256]], 0, 0)
-        dma(ref("ac"), T.act[:], 262144, ref("IOT") if BEHIND else None)
+    push(0, 0, B0, 0)
+    iota(ref("IOT"), [[1, 256]], 0, 0)
+    dma(ref("ac"), T.act[:], 262144)
     iota(ref("pc", 0, 1), [[0, 1]], 0, 1)
     iota(ref("KEY"), [[1, 160]], -16, -1)
     iota(ref("GI"), [[1, 10], [0, 16]], -1, 0)
     iota(ref("io16"), [[1, 16]], 0, 0)
     iota(ref("IL"), [[16, 64]], B0, 1)
     iota(ref("SM"), [[0, 16], [1, 16]], 0, 0)
-    if not ACL:
-        iota(ref("IOT"), [[1, 256]], 0, 0)
-    iota(ref("X", 0, X0), [[0, X0]], 300, 0)
+    for nm in ("X", "XA", "XB"):
+        iota(ref(nm, 0, X0), [[0, X0]], 300, 0)
     p = ref("pc", 0, 1)
-    fields = [(4, 7), (4, 1), (5, 3), (3, 1), (0, 3), (2, 1), (0, 15), (1, 6), (0, 7), (0, 1), (1, 3)]
+    fields = [(4, 7), (4, 1), (5, 3), (3, 1), (0, 3), (2, 1), (0, 15), (1, 6), (0, 7), (0, 1)]
     for i, (sh, mk) in enumerate(fields):
         ts(ref("pd", i, i + 1), p, sh, A.arith_shift_right, mk, A.bitwise_and)
     cp(ref("col", 0, 6), ref("pd", 0, 6))
-    cp(ref("col", 41, 46), ref("pd", 6, 11))
+    cp(ref("col", 41, 45), ref("pd", 6, 10))
     cg, hf, pr, up, lo4, b2 = [col(i) for i in range(6)]
-    pm, h6, lo8, odd, j4 = [col(41 + i) for i in range(5)]
+    pm, h6, lo8, odd = [col(41 + i) for i in range(4)]
     ts(ref("BD"), ref("GI"), cg, A.is_equal)
     K = ref("KEY", 16, 144)
     ts(ref("I"), ref("KEY"), 0.0, A.is_equal)
@@ -300,25 +324,24 @@ def build(g, T, rank, core, topo):
     ts(col(17), b2, 16.0, A.mult, col(16), A.add)
     ts(ref("p2"), ref("io16", 0, 8), 2.0, A.mult, col(17), A.add)
     ts(ref("COV", 0, 128), ind(ref("tc"), ref("p2")), 1024.0, A.add)
-    sg = col(20)
-    ts(sg, up, 2.0, A.mult, -1.0, A.add)
-    ts(col(22), up, 2.0 / 1024, A.mult, -1.0 / 1024, A.add)
-    ts(col(23), up, 2048.0, A.mult, -1024.0, A.add)
-    ts(ref("SI"), K, 0.0, A.is_equal, col(22), A.mult)
-    if any(HS):
-        ts(col(21), sg, 8192.0, A.mult, C0, A.add)
-        ts(ref("SB2"), BDm, 512.0, A.mult)
-    for nm in ("BK", "PK", "GT"):
+    for nm in ("BK", "PK", "GT", "BM"):
         iota(ref(nm), [[0, SB[nm][0][0]]], 0, 0)
     ts(ref("BK", 16, 144, 16), ref("io16", 0, 8), cg, A.is_equal)
-    ts(ref("BA"), ref("BK"), 2.0 / 3, A.mult)
+    ts(ref("BM", 16, 144, 16), ref("BK", 16, 144, 16), KM, A.mult)
+    ts(ref("BN"), ref("BK", 8, 136), KN, A.mult)
+    ts(col(22), pm, min([16] + [a for kind, a, b in HC if kind == "s"]) - 0.5, A.is_ge, 4.5 * KM, A.mult)
+    ts(col(23), col(22), -11.5 * KM, A.add)
+    ts(ref("BAR"), ref("GI"), 0.0, A.mult, col(23), A.add)
     ts(ref("PK", 16, 144, 16), ref("BK", 16, 144, 16), -1.0, A.mult)
-    ts(ref("PK", 24, 152, 16), ref("BK", 16, 144, 16), sg, A.mult)
+    ts(ref("PK", 24, 152, 16), ref("BK", 16, 144, 16), 1.0, A.mult)
     ts(ref("GT", 3, 35, 4), ref("BK", 16, 144, 16), 1.0, A.mult)
     ts(col(24), lo8, 32.0, A.mult, up, A.add)
     iota(ref("io2"), [[16, 2], [2, 8]], 0, 0)
     ts(ref("p1"), ref("io2"), col(24), A.add)
-    ts(col(25), up, -188416.0 - 1577216.0, A.mult, 1577216.0, A.add)
+    ts(col(20), up, 15.0, A.mult, col(24), A.add)
+    ts(ref("p3"), ref("io16"), col(20), A.add)
+    ts(col(21), up, -385.0 * 512, A.mult, C0 - 1, A.add)
+    ts(col(25), up, -3448.0 * 512 - 1577216.0, A.mult, 1577216.0, A.add)
     ts(col(26), pm, -K2, A.mult, -17 * K2, A.add)
     ts(col(27), pm, -K2, A.mult, -K2 - LIVE, A.add)
     ts(ref("k1"), BDm, -K2, A.mult)
@@ -338,50 +361,25 @@ def build(g, T, rank, core, topo):
     for t in range(RO):
         ts(col(36 + t), col(34), B0 + S * t - 1024.0, A.mult, 1024.0 - LIVE, A.add)
     ts(ref("CM"), ref("SM"), pm, A.is_ge, 65536.0, A.mult)
-    ms(ref("GF"), 0.0)
-    run = runs_of(2)
-    iota(ref("k5"), [[16, 2], [0, 128]], 0, 0)
-    ts(ref("RS2"), ref("k5", 64, 256), pm, A.add)
-    for h in range(2):
-        iota(ref("RS2", run[h] + 16 * h + 15, run[h + 1], 16 * h + 16), [[0, 4]], WIN, 0)
-    ts(col(52), odd, 2.0, A.mult, j4, A.add)
-    ts(col(53), odd, 16.0, A.mult, 16.0, A.add)
-    ts(col(54), col(52), col(53), A.mult, col(53), A.add)
-    ts(ref("EL", 0, 1), col(54), -2.0, A.add)
+    iota(r3("NE"), [[0, 400]], 0, 0)
+    for lo, hi, h in ((0, 17, 0.0), (17, 50, 16.0)):
+        ts(r3("RS", 0, 8, lo, hi), r3("NE", 0, 8, lo, hi), h, A.add, pm, A.add)
     ts(col(40), cg, -16.0, A.mult, -1024.0, A.add)
     ts(ref("I16"), ref("IL"), col(40), A.add)
-    if LOT:
-        iota(ref("B2"), [[0, 160]], 0, 0)
-        for u in range(2):
-            ts(ref("B2", 16 + u, 144, 16), ref("BK", 16, 144, 16), 1.0, A.mult)
-            ts(col(57 + u), odd, 1.0 - u, A.is_equal, -32768.0, A.mult)
-            ts(ref("I32", u, 128, 2), ref("I16"), col(57 + u), A.add)
-            if CVT:
-                ts(ref("MK", u, 32, 2), ref("io16"), 0.0, A.mult, col(57 + u), A.add)
+    iota(ref("B2"), [[0, 160]], 0, 0)
+    for u in range(2):
+        ts(ref("B2", 16 + u, 144, 16), ref("BK", 16, 144, 16), 1.0, A.mult)
+        ts(col(57 + u), odd, 1.0 - u, A.is_equal, -32768.0, A.mult)
+        ts(ref("I32", u, 128, 2), ref("I16"), col(57 + u), A.add)
     early[0] = False
 
+    def as_list(out, src, bank, mid, perm, *how):
+        swapped(bank, 8, [("IS", lambda h: ref(src, 128 * h, 128 * h + 128))], 2, halves)
+        tr(ref(mid), pq(bank, 0, 256))
+        ts(ref(out), ind(ref(mid), ref(perm)), *how)
+
     def path_list():
-        swapped(BN["pl"], 8, [("IS", lambda h: ref("PV", 128 * h, 128 * h + 128))], 2, halves)
-        tr(ref("tp"), pq(BN["pl"], 0, 256))
-        ts(ref("PL"), ind(ref("tp"), ref("p1")), 1024.0, A.add)
-
-    def hold(t, lo, hi, banks):
-        B = B0 + S * t
-        tt(ref("C", lo, hi), ind(ref("X", 0, X0 + B), ref("COV", lo // 16, hi // 16)), ref("X" + "AB"[t & 1], lo, hi), A.is_le)
-        for i, a in enumerate(range(lo, hi, 512)):
-            b = min(hi, a + 512)
-            bank = pq(banks[i % len(banks)], 0, b - a)
-            group(bank, [(ref("SI"), ref("X", X0 + a, X0 + b)), (BDm, ref("C", a, b))], 1)
-            act(ref("TT", a, b), bank, F.Identity, bias=C0, scale=col(23))
-
-    def hold_s(t, a, b, bank):
-        bank = pq(bank, 0, b - a)
-        xs = ref("X", X0 + a, X0 + b)
-        act(ref("XC", a, b), ind(ref("X", 0, X0 + B0 + S * t), ref("COV", a // 16, b // 16)), F.Copy)
-        group(bank, [(I_, xs), (NI, ref("XC", a, b))], 1)
-        act(ref("C", a, b), bank, F.Sign, bias=0.5)
-        group(bank, [(ref("SI"), xs), (ref("SB2"), ref("C", a, b))])
-        act(ref("TT", a, b), bank, F.Identity, bias=col(21), scale=sg)
+        as_list("PL", "PV", BN["pl"], "tp", "p1", 1024.0, A.add)
 
     for t in range(RO):
         B = B0 + S * t
@@ -392,15 +390,19 @@ def build(g, T, rank, core, topo):
         Xw = ref("X", X0, X0 + B)
         fr = (8 + t) / 16.0
         old = B if t == 0 else B - S
+        wd = old // 16
+        now[2:] = [PLAN["first"] + PLAN["round"] * t, t]
+        at("start", 0.0, 0.0)
         if t:
-            if NEWP:
-                push(t, old, B, RO + t)
-            push(t, 0, old if NEWP else B, t)
-        cuts = list(range(0, old, 512)) + [old] + ([B] if t else [])
+            push(t, 0, B, t)
+        cuts = [wd * i for i in SC] + ([B] if t else [])
         for i in range(len(cuts) - 1):
+            at("start", 0.3 * i)
             a, b = cuts[i], cuts[i + 1]
             e = COPY[t][min(i, len(COPY[t]) - 1)]
-            copy(e, ref(snap, a, b), T.lab[:, a:b] if t == 0 and e == "d" else ref("X", X0 + a, X0 + b))
+            copy(e, ref(snap, X0 + a, X0 + b), T.lab[:, a:b] if t == 0 and e == "d" else ref("X", X0 + a, X0 + b))
+        dma(ref("L0", 0, wd), lane0(0, old), 256 * wd)
+        at("start")
         copy(SMALL[3], ref("xv"), ind(Xw, ref("LU")))
         swapped("M1", 4, [("ZW", lambda h: ref("xv", 64 * h, 64 * h + 64))], 4, lambda c, h: 32 - 2 * h)
         tr(ref("tx"), pq("M1", 0, 128))
@@ -408,148 +410,173 @@ def build(g, T, rank, core, topo):
         ts(ref("ha"), ref("hi"), 4095, A.bitwise_and)
         ts(ref("LA"), ref("ha", 0, 16), 0.25, A.mult)
         ts(ref("LQ"), ref("ha", 16, 32), fr, A.mult, -15.0 / 32, A.add)
-        act(ref("av"), ind(ref("ac"), ref("LA")), F.Copy)
-        group(pq("M0", 0, 256), [(I_, ref("xv")), (NI, ref("av"))])
-        act(z, pq("M0", 0, 256), F.Abs)
+        if t == 0:
+            ts(ref("PV"), ind(ref("pt"), ref("LU")), -1024.0, A.add)
+            path_list()
+        at("label")
+        if SMALL[0] == "v":
+            tt(ref("av"), ind(ref("ac"), ref("LA")), ref("xv"), A.subtract)
+            act(z, ref("av"), F.Abs)
+        else:
+            act(ref("av"), ind(ref("ac"), ref("LA")), F.Copy)
+            group(pq("M0", 0, 256), [(I_, ref("xv")), (NI, ref("av"))])
+            act(z, pq("M0", 0, 256), F.Abs)
         hs = [(ref("NH"), ref("HF")), (ref("WB"), z)]
         group(pq("M2b", 0, 256), hs, 1)
         ts(ref("cq"), pq("M2b", 0, 256), BIG, A.add, BIG, A.subtract)
         group(pq("M2b", 0, 256), [hs[1], (NI, ref("cq"))])
-        ts(ref("CL"), pq("M2b", 0, 256), float(B), A.mult, -15.0 / 32, A.add)
-        ts(cs, ref("CL"), -1024.0, A.add)
-        runs, s0 = [], 0
+        ts(ref("rm"), pq("M2b", 0, 256), 4096.0, A.mult, -2048.0, A.add)
+        as_list("CL", "rm", BN["cl"], "tq", "p3", fr, A.mult, 2048 * fr - 15.0 / 32, A.add)
+        at("number")
+        ts(ref("CU"), ref("rm"), fr, A.mult, 2048 * fr - 15.0 / 32, A.add)
+        ts(cs, ref("CU"), -1024.0, A.add)
+        at("repeat")
+        act(ref("ZC", 0, 256), z, F.Identity, bias=col(21), scale=-1.0)
+        for i, e in enumerate(ZC):
+            copy(e, ref("ZC", 256 << i, 512 << i), ref("ZC", 0, 256 << i))
+        m0 = 0
         for kind, n in CAND[t]:
-            runs.append((kind, s0, s0 + n))
-            s0 += n
-        for kind, s0, s1 in runs:
-            if kind == "a":
-                for m in range(16):
-                    copy("g", ref("XK", 16 * s0 + m, 16 * s1, 16), ref("z%d" % (t & 1), s0, s1))
-            cuts = [s0]
-            while cuts[-1] < s1:
-                cuts.append(min(s1, cuts[-1] + CG[kind][min(len(cuts), len(CG[kind])) - 1] // 16))
-            for a, b in zip(cuts, cuts[1:]):
-                src = ind(ref(snap, 0, B), ref("CL", a, b))
-                if kind == "a":
-                    tt(ref("SG", 16 * a, 16 * b), src, ref("XK", 16 * a, 16 * b), A.is_le)
+            at("cand" + kind, PLAN["per"] * m0 if kind == "d" else 0.0, PLAN["per"] * CG[kind] / 256)
+            for a in range(256 * m0, 256 * (m0 + n), CG[kind]):
+                b = min(a + CG[kind], 256 * (m0 + n))
+                src = ind(ref(snap, X0, X0 + B), ref("CL", a // 16, b // 16))
+                if kind == "v":
+                    tt(ref("SG", a, b), src, ref("ZC", 0, b - a), A.add)
                 else:
-                    copy("s", ref("XK", 16 * a, 16 * b), src)
-        e1 = ref("EE", 384, 640) if HALF else ref("E", 0, 256)
-        act(e1, ind(ref("xr%d" % t), ref("LQ")), F.Copy)
-        if HALF:
-            for q in (1, 0):
-                for w in (128, 256)[:EW[q] // 256]:
-                    copy(EC[q], ref("EE", 512 + w, 512 + 2 * w) if q else ref("EE", 512 - 2 * w, 512 - w), ref("EE", 512, 512 + w) if q else ref("EE", 512 - w, 512))
+                    copy("s", ref("SG", a, b), src)
+                row("c" + kind)
+            if kind == "d":
+                added(ref("SG", 256 * m0, 256 * (m0 + n)), ref("ZC", 0, 256 * n))
+            m0 += n
+        e1 = ref("EC", 896, 1152)
+        at("answer", 0.0, 0.1)
+        act(e1, ind(ref("xr%d" % t), ref("LQ")), F.Identity, bias=C0, scale=-1.0)
+        for q in (1, 0):
+            nv = OQ[t][q].count("v")
+            for i, w in enumerate((128, 256, 512)[:3 if JOIN and "dd" in OQ[t][q] else 2 if nv > E1[q] or "d" in OQ[t][q] else min(nv, 1)]):
+                if EC[q][i] == "D":
+                    for c in (512, 256, 0):
+                        copy("d", ref("EC", c, c + 256), ref("EC", 768, 1024))
+                    break
+                copy(EC[q][i], ref("EC", 1024 + w, 1024 + 2 * w) if q else ref("EC", 1024 - 2 * w, 1024 - w), ref("EC", 1024, 1024 + w) if q else ref("EC", 1024 - w, 1024))
+        if SMALL[4] == "s":
+            act(ref("EB"), e1, F.Identity, bias=C0, scale=-1.0)
         else:
-            copy(SMALL[0], ref("E", 256, 512), ref("E", 0, 256))
+            ts(ref("EB"), e1, -1.0, A.mult, C0, A.add)
         if SMALL[1] == "s":
-            act(ref("EM"), e1, F.Relu, bias=-255 * LIVE, scale=LIVE)
+            act(ref("EM"), ref("EB"), F.Relu, bias=-255 * LIVE, scale=LIVE)
         else:
-            ts(ref("EM"), e1, 255.5, A.is_gt, LIVE, A.mult)
-        if t == 0:
-            ts(ref("PV"), ind(ref("pt"), ref("LU")), -1024.0, A.add)
-            path_list()
-        for a in range(0, HS[t], 512):
-            hold_s(t, a, min(HS[t], a + 512), HB[a // 512])
-        for a in range(HS[t], old, HC):
-            hold(t, a, min(old, a + HC), ["P1", "P2"] if HC > 512 or ((a - HS[t]) // HC) % 2 else ["P2"])
+            ts(ref("EM"), ref("EB"), 255.5, A.is_gt, LIVE, A.mult)
         Xa = ref("X", 0, X0 + B)
-        if HALF:
-            mms([(pq("M0", 128 * j, 128 * j + 128), I_, ref("EE", 384 + 128 * (j // 2), 512 + 128 * (j // 2)), True, True) for j in range(4) if OQ[t][j // 2]])
-        for q in ((1, 0) if HALF else ()):
-            s0, pb, wb, nh = 128 * q, "P%d" % (q + 1), ("M0", "M2b")[q], NHQ[q]
+        mk = pq(BN["mk"], 0, wd)
+        at("start")
+        mms([(mk, I_, ref("BAR", 0, wd), True, False)])
+        done = nb = 0
+        seen = {"v": 0, "s": 0}
+        for kind, a, b in HC:
+            at("hold", 0.17 * seen[kind])
+            seen[kind] += b - a
+            src = ind(Xa, ref("COV", wd * a // 16, wd * b // 16))
+            if kind == "v":
+                tt(ref("C", wd * a, wd * b), src, ref(snap, X0 + wd * a, X0 + wd * b), A.is_le)
+            else:
+                act(ref("XC", wd * a, wd * b), src, F.Copy)
+            row("h" + kind)
+            step = b - a if kind == "v" else HS
+            for c in range(a, b, step):
+                d = min(b, c + step)
+                if kind == "s":
+                    bank = pq(HB[nb % len(HB)], 0, wd * (d - c))
+                    nb += 1
+                    group(bank, [(I_, ref("X", X0 + wd * c, X0 + wd * d)), (NI, ref("XC", wd * c, wd * d))], 1)
+                    act(ref("C", wd * c, wd * d), bank, F.Sign, bias=0.5)
+                done += d - c
+                mms([(mk, ref("BM", 16 - i, 144 - i), ref("C", wd * i, wd * i + wd), False, done == 16 and i == d - 1) for i in range(c, d)])
+        tt(ref("LM", 0, wd), mk, ref("L0", 0, wd), A.max)
+        dma(lane0(0, old), ref("LM", 0, wd), 256 * wd)
+        if t:
+            at("newest")
+            tt(ref("C", old, B), ind(ref(snap, 0, X0 + B), ref("COV", old // 16, B // 16)), ref("X", X0 + old, X0 + B), A.is_le)
+        seen = {"v": 0, "s": 0, "d": 0}
+        nb = 0
+        for q in (1, 0):
+            s0, pb = 128 * q, "P%d" % (q + 1)
             for n, k in enumerate((12, 8, 4, 0)):
-                if k == 0 and t and q:
-                    hold(t, old, B, [BN["hn"]])
+                at("paths", PLAN["piece"] * seen[OQ[t][q][n]], 0.3)
+                seen[OQ[t][q][n]] += 1
                 a = 2048 * q + 128 * k
-                win = ref("TT", 0, old if k else B)
-                if n < OQ[t][q]:
-                    act(ref("OG", a, a + 512), ind(win, ref("PL", a // 16, a // 16 + 32)), F.Copy)
-                    for b in (a, a + 256):
-                        tt(ref("O", b, b + 256), ref("OG", b, b + 256), pq("M0", 256 * q, 256 * q + 256), A.subtract)
+                ec = lambda w: ref("EC", 1024, 1024 + w) if q else ref("EC", 1024 - w, 1024)
+                if OQ[t][q][n] == "d":
+                    act(ref("O", a, a + 512), ind(Xw, ref("PL", a // 16, a // 16 + 32)), F.Copy)
+                    row("ps")
+                    nd2 = OQ[t][q].count("d") if JOIN else 1
+                    if n % nd2 == nd2 - 1:
+                        added(ref("O", a, a + 512 * nd2), ec(512 * nd2))
+                elif OQ[t][q][n] == "s":
+                    act(ref("OG", a, a + 512), ind(Xw, ref("PL", a // 16, a // 16 + 32)), F.Copy)
+                    row("ps")
+                    bank = OB[nb % len(OB)]
+                    nb += 1
+                    mms([(pq(bank, 128 * j, 128 * j + 128), NI, ref("EB", s0, s0 + 128), j == 0, False) for j in range(4)])
+                    mms([(pq(bank, 0, 512), I_, ref("OG", a, a + 512), False, True)])
+                    act(ref("O", a, a + 512), pq(bank, 0, 512), F.Identity, bias=C0)
                 else:
-                    w = 256 if q and n == OQ[t][q] and E1 else EW[q]
+                    w = 256 if OQ[t][q][:n].count("v") < E1[q] else 512
                     for b in range(a, a + 512, w):
-                        tt(ref("O", b, b + w), ind(win, ref("PL", b // 16, (b + w) // 16)), ref("EE", 512, 512 + w) if q else ref("EE", 512 - w, 512), A.subtract)
+                        tt(ref("O", b, b + w), ind(Xw, ref("PL", b // 16, (b + w) // 16)), ec(w), A.add)
+                        row("pv")
+            for n, k in enumerate((12, 8, 4, 0)):
+                at("paths", PLAN["piece"] * (n + 1 + (0 if q else 1.5)), 0.1)
                 for j0 in (k + 2, k):
                     mms([(pq(pb, 128 * (n // 2), 128 * (n // 2) + 128), ref("PK", 16 - j % 8, 144 - j % 8), ref("O", 2048 * q + 128 * j, 2048 * q + 128 * j + 128),
-                          j % 8 == 7, j % 8 == 0) for j in (j0 + 1, j0)])
+                          j % 8 == 7, j == 8 or (j == 0 and not t)) for j in (j0 + 1, j0)])
+            if t:
+                mms([(pq(pb, 128, 256), ref("BN"), ref("C", old + s0, old + s0 + 128), False, True)])
+        dma(lane0(0, old), ref("L0", 0, wd), 256 * wd)
+        for q in (1, 0):
+            s0, pb, wb, nh = 128 * q, "P%d" % (q + 1), ("M0", "M2b")[q], NHQ[q]
             fq = "F%d" % (q + 1)
+            at("upper" if q else "lower", 0.0, 0.25)
             act(ref(fq), pq(pb, 0, 256), F.Sign, bias=col(25))
             group(pq(wb, 0, 128), [(I_, ref("PV", s0, s0 + 128)), (NI, ref("EM", s0, s0 + 128)), (ref("U2"), ref(fq, 0, 128)), (ref("U1"), ref(fq, 128, 256))], 2)
             group(pq("M1", s0, s0 + 128), [(ref("HB"), ref(fq, 0, 128)), (ref("HB"), ref(fq, 128, 256))])
             mt = r3("MT", 8 * q, 8 * q + 8)
             ts(mt, pq(wb, 0, 128), col(26), A.add, -NONE, A.max)
             swapped(wb, 4, [("BS", lambda h: r3("MT", 8 * q + h, 8 * q + 8, step0=2))], 2, halves)
-            group(pq(wb, 128, 256), [(I_, ref("CM", 0, 128)), (BDm, mt)])
-            group(r3(wb, 16, 24, step0=2), [(BDm, r3("MT", 8 * q, 8 * q + 8, step0=2))]) if nh == 2 else group(pq(wb, 256, 384), [(BDm, mt)])
+            eb = EB[q] or wb
+            if EB[q]:
+                mms([(pq(eb, 128, 256), I_, ref("CM", 0, 128), True, False)])
+                mms([(pq(eb, 128, 256), BDm, mt, False, False), (r3(eb, 16, 24, step0=2), BDm, r3("MT", 8 * q, 8 * q + 8, step0=2), False, True)])
+            else:
+                group(pq(wb, 128, 256), [(I_, ref("CM", 0, 128)), (BDm, mt)])
+                group(r3(wb, 16, 24, step0=2), [(BDm, r3("MT", 8 * q, 8 * q + 8, step0=2))])
             tr(r3("LR", 8 * q, 8 * q + 8), pq(wb, 0, 128))
             top = r3("LR", 8 * q, 8 * q + 8, 0, 1)
-            if not (q and NVT):
-                ts(ref("GL", 8 * q, 8 * q + 8), top, 16 * NONE + NOT - X0, A.add)
-            act(ref("GF", 8 * q, 8 * q + 8), top, F.Identity, bias=16 * NONE + NOT)
-            run = [320 * q + x for x in runs_of(nh)]
-            for h in range(nh):
-                for d in range(h + 1):
-                    tt(ref("NE", run[h] + d, run[h + 1], h + 1), r3("LR", 8 * q + h, 8 * q + 8, step0=nh),
-                       r3(wb, 8 + h, 16, step0=nh) if d == h else r3(wb, 16 + d, 24, step0=nh), A.not_equal)
-            kp, rs, ne = ref("KP", run[0], run[nh]), ref("RS%d" % nh), ref("NE", run[0], run[nh])
-            add("v", lambda kp=kp, rs=rs, ne=ne: g.vector.tensor_tensor_scan(kp["ap"], ne["ap"], rs["ap"], float(WIN), A.mult, A.max), [kp], [rs, ne], (0, max(64, kp["n"] // 2), "cy"))
-            tt(ref("vt", 16 * q, 16 * q + 16), ind(kp, ref("EL", nh - 2, nh - 1)), ref("GF", 8 * q, 8 * q + 16), A.min)
-            cp(ref("TL", 8 * q, 8 * q + 8), ref("vt", 16 * q, 16 * q + 8))
-            tt(ref("NV", s0, s0 + 128), ind(Xa, ref("TL", 8, 16)) if q and NVT else ind(ref(snap, 0, B), ref("GL", 8 * q, 8 * q + 8)), ref("EE", 384 + s0, 512 + s0), A.max)
+            if NVG[q]:
+                ts(ref("GL", 8 * q, 8 * q + 8), top, 16 * NONE + NOT, A.add)
+            act(r3("RS", 4 * q, 4 * q + 4, 0, 18, 17), top, F.Identity, bias=16 * NONE + NOT)
+            for h, d, c in ((0, 0, 1), (1, 0, 18), (1, 1, 34)):
+                tt(r3("NE", 4 * q, 4 * q + 4, c, c + 16), r3("LR", 8 * q + h, 8 * q + 8, step0=2),
+                   r3(eb, 8 + h, 16, step0=2) if d == h else r3(eb, 16 + d, 24, step0=2), A.not_equal)
+            for j1, j0 in zip(KC[q], KC[q][1:]):
+                j0, j1 = 4 * q + j0, 4 * q + j1
+                kp, rs, ne = [r3(nm, j0, j1) for nm in ("KP", "RS", "NE")]
+                add("v", lambda j0=j0, j1=j1: [g.vector.tensor_tensor_scan(T.KP[:, j], T.NE[:, j], T.RS[:, j], 0.0, A.mult, A.max) for j in range(j0, j1)][-1],
+                    [kp], [rs, ne], (0, 64 * (j1 - j0), "cy"))
+                cp(ref("TL", 2 * j0, 2 * j1), r3("KP", j0, j1, 16, 50, 33))
+            tt(ref("NV", s0, s0 + 128), ind(ref(snap, 0, X0 + B), ref("GL" if NVG[q] else "TL", 8 * q, 8 * q + 8)), ref("EB", s0, s0 + 128), A.max)
             for b in range(8 * q + 8 - nh, 8 * q - 1, -nh):
                 cp(ind(Xa, ref("TL", b, b + nh)), ref("NV", 16 * b, 16 * (b + nh)))
-        if HALF:
-            act(lv, pq("M1", 0, 256), F.Relu, bias=-7 * LIVE, scale=-LIVE / 2, acc=ref("cn", t, t + 1))
-        if OS[t] and not HALF:
-            mms([(pq("M0", a, a + 256), I_, ref("E", 0, 256), True, True) for a in (0, 256)])
-        for n, k in enumerate([] if HALF else [8, 10, 12, 14, 6, 4, 2, 0]):
-            if k == 0 and t:
-                hold(t, old, B, ["M1"])
-            o, src = ref("O", 256 * k, 256 * k + 512), ind(ref("TT", 0, old if k else B), ref("PL", 16 * k, 16 * k + 32))
-            if k >= 16 - 2 * OS[t]:
-                act(ref("OG", 256 * k, 256 * k + 512), src, F.Copy)
-                tt(o, ref("OG", 256 * k, 256 * k + 512), pq("M0", 0, 512), A.subtract)
-            else:
-                tt(o, src, ref("E"), A.subtract)
-            bank = pq("P2" if k >= 8 else "P1", 0, 256)
-            mms([(bank, ref("PK", 16 - j % 8, 144 - j % 8), ref("O", 256 * j, 256 * j + 256), n % 4 == 0 and j > k, n % 4 == 3 and j == k) for j in (k + 1, k)])
-            if n % 4 == 3:
-                act(ref("F2" if k else "F1"), bank, F.Sign, bias=col(25))
-        if not HALF:
-            group(pq("M2b", 0, 256), [(I_, ref("PV")), (NI, ref("EM")), (ref("U2"), ref("F2")), (ref("U1"), ref("F1"))], 3)
-            group(pq("M1", 0, 256), [(ref("HB"), ref("F2")), (ref("HB"), ref("F1"))], 1)
-            ts(r3("MT"), pq("M2b", 0, 256), col(26), A.add, -NONE, A.max)
-            act(lv, pq("M1", 0, 256), F.Relu, bias=-7 * LIVE, scale=-LIVE / 2, acc=ref("cn", t, t + 1))
-            swapped("M2b", 8, [("BS", lambda h: r3("MT", h, 16, step0=2))], 2, halves)
-            group(r3("M0", 0, 16), [(I_, ref("CM")), (BDm, r3("MT"))], 1)
-            group(r3("M0", 16, 32), [(BDm, r3("MT"))])
-            tr(r3("LR"), pq("M2b", 0, 256))
-            ts(ref("GL"), r3("LR", 0, 16, 0, 1), 16 * NONE + NOT, A.add)
-            act(ref("GF", 0, 16), r3("LR", 0, 16, 0, 1), F.Identity, bias=16 * NONE + NOT)
-            for h in range(NH):
-                for d in range(h + 1):
-                    tt(ref("NE", RUN[h] + d, RUN[h + 1], h + 1), r3("LR", h, 16, step0=NH), r3("M0", h, 16, step0=NH) if d == h else r3("M0", 16 + d, 32, step0=NH), A.not_equal)
-            kp, rs, ne = ref("KP"), ref("RS"), ref("NE")
-            add("v", lambda kp=kp, rs=rs, ne=ne: g.vector.tensor_tensor_scan(kp["ap"], ne["ap"], rs["ap"], float(WIN), A.mult, A.max), [kp], [rs, ne], (0, RUN[NH] // 2, "cy"))
-            nb = 16 // NH
-            tt(ref("vt", 0, 16), ind(kp, ref("EL", 0, 1)), ref("GF", 0, 16), A.min)
-            cp(ref("TL"), ref("vt", 0, 16))
-            tt(ref("NV"), ind(Xa, ref("GL")), ref("E", 0, 256), A.max)
-            for b in range(nb - 1, -1, -1):
-                cp(ind(Xa, ref("TL", NH * b, NH * b + NH)), ref("NV", 16 * NH * b, 16 * NH * (b + 1)))
-        if LOT:
-            group(r3("P1", 0, 1), [(I_, ref("I32", 32 * t, 32 * t + 32))] + [(ref("B2", 16 - i, 144 - i), r3(lvn, 0, 16, i, i + 2)) for i in range(0, 16, 2)])
-            for u in range(2):
-                tt(ref("LO"), r3("P1", 0, 1, u, 32, 2), ref("LO"), A.max)
-        else:
-            group(r3("P1", 0, 1, 0, 16), [(I_, ref("I16", 16 * t, 16 * t + 16))] + [(ref("BK", 16 - i, 144 - i), r3(lvn, 0, 16, i, i + 1)) for i in range(16)])
-            tt(ref("LO"), r3("P1", 0, 1, 0, 16), ref("LO"), A.max)
+        at("live", 0.0, 0.25)
+        act(lv, pq("M1", 0, 256), F.Relu, bias=-7 * LIVE, scale=-LIVE / 2, acc=ref("cn", t, t + 1))
+        group(r3("P1", 0, 2), [(I_, ref("I32", 32 * t, 32 * t + 32))] + [(ref("B2", 16 - i, 144 - i), r3(lvn, 0, 16, i, i + 2)) for i in range(0, 16, 2)])
+        for u in range(2):
+            tt(ref("LO"), r3("P1", 0, 2, u, 16, 2), ref("LO"), A.max)
         if not last:
             ts(ref("LU"), ref("LO"), -LOFF, A.add)
         else:
             act(ref("LV"), ref("LO"), F.Identity, bias=-LOFF)
+        at("live", 0.4, 0.3)
         group(pq(BN["xn"], 0, 256), [(I_, z), (NI, lv)])
         if SMALL[2] == "s":
             act(ref("Y"), pq("M1", 0, 256), F.Relu, scale=-1.0, bias=256.0 - LIVE)
@@ -560,39 +587,19 @@ def build(g, T, rank, core, topo):
         yp = ref("YP", S * t, S * t + S)
         act(yp, pq("P2", 0, 256), F.Relu, bias=col(36 + t))
         dma(T.yp[:, S * t:S * t + S], yp, 131072)
-        yc = pq("P1", 0, 256, (0, 32))
         if not last:
             act(ref("yq"), yp, F.Identity, bias=-1024.0)
             group(pq(BN["pv"], 0, 256), [(I_, ref("PV")), (NI, lv)])
             tt(ref("PV"), pq(BN["pv"], 0, 256), ref("yq"), A.max)
             path_list()
-        elif not TAIL:
-            mms([(yc, ref("GT", 3 - r, 35 - r), r3("M2", 16 * r, 16 * r + 16), r == 0, False) for r in range(t)])
-        n = 0
-        two = all(kind != "b" for kind, s0, s1 in runs)
-        for kind, s0, s1 in runs:
-            w = s1 - s0
-            zs = ref("z%d" % (t & 1), s0, s1)
-            if kind == "c":
-                per = 512 // w
-                for m0 in range(0, 16, per):
-                    bank = "A%d" % (n & 1) if two else "A0"
-                    n += 1
-                    m1 = min(16, m0 + per)
-                    mms([x for m in range(m0, m1) for x in chain(pq(bank, w * (m - m0), w * (m - m0 + 1)), [
-                        (I_, zs), (NI, ref("XK", 16 * s0 + m, 16 * s1, 16))])])
-                    act(ref("SG", 16 * s0 + w * m0, 16 * s0 + w * m1), pq(bank, 0, w * (m1 - m0)), F.Sign, bias=0.5)
-            if kind == "b":
-                group(pq("A1", 0, w), [(I_, zs)])
-                for m in range(16):
-                    tt(ref("SG", 16 * s0 + w * m, 16 * s0 + w * m + w), ref("XK", 16 * s0 + m, 16 * s1, 16), pq("A1", 0, w), A.is_le)
-            for m0 in range(0, 16, 4):
-                mms([(pq(TAIL if last and TAIL and s0 >= 128 else "CB", s0, s1), ref("BK" if kind == "c" else "BA", 16 - m, 144 - m),
-                      ref("SG", 16 * s0 + m, 16 * s1, 16) if kind == "a" else ref("SG", 16 * s0 + w * m, 16 * s0 + w * m + w), m == 0, m == 15)
-                     for m in range(m0, m0 + 4)])
+        at("count", 0.0, PLAN["per"] * CM / (2 if last else 1))
+        for m0 in range(0, 16, CM):
+            for s0, s1, cb in ((0, 128, "CB"), (128, 256, TAIL)) if last else ((0, 256, "CB"),):
+                mms([(pq(cb, s0, s1), ref("BK", 16 - m, 144 - m), ref("SG", 256 * m + s0, 256 * m + s1), m == 0, m == 15) for m in range(m0, m0 + CM)])
+        at("cover")
         act(ref("py", t, t + 1), ref("cn", t, t + 1), F.Identity, bias=-512.5 * AL, scale=AL / LIVE)
         act(ref("pb", t, t + 1), ref("cn", t, t + 1), F.Identity, bias=ref("py", t, t + 1), scale=-AL / LIVE)
-        if last and TAIL:
+        if last:
             for a, cb, yb in ((0, "CB", "P1"), (128, TAIL, "P2")):
                 yc = pq(yb, 0, 128, (0, 32))
                 m2 = lambda r: r3("M2", 16 * r + a // 16, 16 * r + a // 16 + 8)
@@ -606,17 +613,8 @@ def build(g, T, rank, core, topo):
         act(ref("FS"), pq("CB", 0, 256), F.Sign, bias=ref("pb", t, t + 1), scale=FK)
         group(pq("CB", 0, 256), [(ref("U0"), ref("FS")), (I_, lv), (I_, cs)])
         ts(r3("M2", 16 * t, 16 * t + 16), pq("CB", 0, 256), col(27), A.add, -1025.0, A.max)
-        if not last and CVT:
-            group(r3("CB", 0, 1), [(I_, ref("MK"))] + [(ref("B2", 16 - i, 144 - i), r3("M2", 16 * t, 16 * t + 16, i, i + 2)) for i in range(0, 16, 2)])
-            act(ref("cw"), r3("CB", 0, 1, 0, 32, 2), F.Copy)
-            tt(ref("cw"), r3("CB", 0, 1, 1, 32, 2), ref("cw"), A.max)
-            ts(ref("COV", B // 16, B // 16 + 16), ref("cw"), 16399.0 + X0, A.add)
-        elif not last:
-            group(r3("CB", 0, 1, 0, 16), [(ref("BK", 16 - i, 144 - i), r3("M2", 16 * t, 16 * t + 16, i, i + 1)) for i in range(16)])
-            ts(ref("COV", B // 16, B // 16 + 16), r3("CB", 0, 1, 0, 16), 16399.0 + X0, A.add)
-        else:
-            mms([(yc, ref("GT", 3 - t, 35 - t), r3("M2", 16 * t, 16 * t + 16), False, True)])
-            act(ref("YC", parts=(0, 32)), yc, F.Identity, bias=16399.0)
+        group(r3("CB", 0, 1, 0, 16), [(ref("BK", 16 - i, 144 - i), r3("M2", 16 * t, 16 * t + 16, i, i + 1)) for i in range(16)])
+        ts(ref("COV", B // 16, B // 16 + 16), r3("CB", 0, 1, 0, 16), 16399.0 + X0, A.add)
     dma(T.yx[:, 0:W - S], ref("X", X0, X0 + W - S), 720896)
     dma(T.yx[:, W - S:W], ref("X", X0 + W - S, X0 + W), 65536)
     dma(T.yv[:], ref("LV"), 8192)
@@ -630,6 +628,8 @@ def depend(ops):
         d = {}
         if "after" in o:
             d[o["after"]] = False
+        for j in o.get("behind", []):
+            d[j] = False
         for kind in ("R", "W"):
             for (nm, lo, hi, par) in o[kind]:
                 ps = nm in PS
@@ -640,7 +640,7 @@ def depend(ops):
                     if ps:
                         d[j] = d.get(j, False) or not same
                     elif (kind == "W" or k2 == "W") and lo < h2 and l2 < hi and (par[0] != p2[0] or par == p2):
-                        d[j] = True
+                        d[j] = d.get(j, False) or not (SAME and same and kind == "W" and "nb" not in o and "nb" not in ops[j])
         o["d"] = d
         for kind in ("R", "W"):
             for (nm, lo, hi, par) in o[kind]:
@@ -659,7 +659,7 @@ def schedule(ops):
     for m in SETS:
         per = {"cy": m["cy"], "ga": m["cy"] * m["ga"], "sc": m["cy"] * m["sc"], "pe": m["pe"]}
         dur = [o["nb"] / m["xr" if o.get("remote") else "rate"] + 60 if "nb" in o else o["c"][0] + o["c"][1] * per[o["c"][2]] for o in ops]
-        tail = [m["lat"] + (600 if o.get("remote") else 0) if "nb" in o else 0 for o in ops]
+        tail = [m["lat"] + o.get("late", 0) if "nb" in o else 0 for o in ops]
         pred = [[(j, tail[j] + m["hop"] if w else tail[j] if o["e"] != "g" else -1e6) for j, w in o["d"].items()] for o in ops]
         sets.append((dur, tail, pred))
     dur, tail, pred = sets[0]
@@ -748,7 +748,13 @@ def schedule(ops):
         seq = topo_by(st, pred, post)
         return sum(replay(seq, s)[0] for s in sets) / len(sets), st, seq
 
-    best = both([-float(i) for i in range(n)])
+    def planned():
+        seq = topo_by([o["at"] for o in ops], pred, post)
+        if PLACE:
+            seq = topo_by(place(seq, pred), pred, post)
+        return sum(replay(seq, s)[0] for s in sets) / len(sets), [], seq
+
+    best = planned() if PASSES == 0 else both([-float(i) for i in range(n)])
     cur = best
     for it in range(PASSES):
         st = cur[1]
@@ -914,18 +920,39 @@ def schedule(ops):
                 break
         return low, free, nxt
 
-    best = (1e18, seq[:])
-    starts = list(range(0, n - SPAN // 2, SPAN // 2))
-    each = MOVES // (SWEEPS * len(starts))
-    for sweep in range(SWEEPS):
-        heat = HEAT * (1.0 - sweep / (SWEEPS - 1.0)) ** 1.5
+    def repeat():
         links()
         times(0, n - 1, 0, n)
-        old = seq[:]
-        seq.sort(key=lambda i: tm[0][0][i])
-        if [i for i in old if issue[i] >= 0] != [i for i in seq if issue[i] >= 0]:
-            seq[:] = old
+        st = tm[0][0]
+        tags, count = {}, {}
+        for o in ops:
+            k = (o["t"], o["e"], o["W"][0][0].rstrip("01").replace("XB", "XA")[:2] if o["W"] else "")
+            count[k] = count.get(k, 0) + 1
+            tags[o["id"]] = k[1:] + (count[k],)
+        was = [min(st[o["id"]] for o in ops if o["t"] == t and o["W"] and o["W"][0][0] == "xv") for t in range(RO)]
+        period = was[2] - was[1]
+        rel = {tags[o["id"]]: st[o["id"]] - was[1] for o in ops if o["t"] == 1}
+        rel.update({tags[o["id"]]: st[o["id"]] - was[1] + period for o in ops if o["t"] == 0 and st[o["id"]] >= was[1]})
+        new = [was[1] + period * (t - 1) for t in range(RO)]
+        key = [st[i] if st[i] < was[2] and o["t"] < 2 else new[max(1, o["t"])] + rel.get(tags[i], st[i] - was[max(1, o["t"])]) for i, o in enumerate(ops)]
+        seq[:] = topo_by(key, pred, succ[0])
+
+    best = (1e18, seq[:])
+    plan = [(sweep, part) for part in STAGES for sweep in range(part[3])]
+    for sweep, (lo, hi, share, sweeps, hot) in plan:
+        if sweep == 0:
+            seq[:] = best[1]
+            if (lo, hi) == (0, 1) and len(STAGES) > 1:
+                repeat()
+                best = (1e18, seq[:])
+        starts = [x for x in range(0, n - SPAN // 2, SPAN // 2) if lo * n <= x <= hi * n]
+        each = int(MOVES * share) // (sweeps * len(starts))
+        heat = hot * (1.0 - sweep / (sweeps - 1.0)) ** 1.5
         links()
+        times(0, n - 1, 0, n)
+        seq.sort(key=lambda i: tm[0][0][i] + max(0.0, min(pre[i], issue[i])))
+        links()
+        times(0, n - 1, 0, n)
         for r0 in starts:
             r1 = min(n, r0 + SPAN)
             times(max(0, r0 - SPAN), r1 - 1, r0, min(n, r1 + SPAN))

import math
from concourse.mybir import AluOpType, ActivationFunctionType

A = AluOpType
F = ActivationFunctionType
B0, S, RO, W = 2048, 256, 4, 3072
JUMPS = [1, 2, 3, 1]
X0 = 48
C0 = 98560.5
K2 = 2048.0
LIVE = 4096.0
NOT = 32
NONE = 1024.0 + X0 - NOT
BIG = 12582912.0
LOFF = 16 * LIVE - 1024
KM, KN = 524288.0, 16384.0
bf, f32, i32, u16, f16 = "bfloat16", "float32", "int32", "uint16", "float16"
SB = {
    "X": ([X0 + W], bf), "XA": ([X0 + W - S], bf), "XB": ([X0 + W - S], bf), "xr0": ([2048], bf), "xr1": ([2304], bf), "xr2": ([2560], bf), "xr3": ([2816], bf),
    "pt": ([2048], i32), "ac": ([1024], bf), "cv": ([128], i32), "wt": ([16], i32), "lf": ([16], i32),
    "O": ([4096], bf), "SG": ([4096], bf), "C": ([2816], bf), "YP": ([1024], f32), "YC": ([256], f32),
    "COV": ([192], u16), "PL": ([256], u16), "LU": ([16], u16), "LV": ([16], f32), "PV": ([256], f16),
    "xv": ([256], bf), "av": ([256], bf), "z0": ([256], bf), "z1": ([256], bf), "EB": ([256], bf), "EM": ([256], bf),
    "tx": ([128], f32), "hi": ([32], i32), "ha": ([32], i32), "LA": ([16], u16), "LQ": ([16], u16), "hp": ([2], u16),
    "cq": ([256], f16), "NH": ([128], bf), "HF": ([256], bf), "k4": ([128], bf), "LO": ([16], f32), "I16": ([64], f16), "py": ([4], bf),
    "rm": ([256], f16), "CU": ([256], u16), "CL": ([256], u16), "tq": ([256], f32), "p3": ([16], u16), "cs0": ([256], f16), "cs1": ([256], f16),
    "F1": ([256], bf), "F2": ([256], bf), "lv0": ([16, 16], bf), "lv1": ([16, 16], bf), "MT": ([16, 16], f16),
    "LR": ([16, 16], f32), "NE": ([8, 50], bf), "KP": ([8, 50], f32), "RS": ([8, 50], f32), "GL": ([16], u16),
    "TL": ([16], u16), "NV": ([256], bf), "Y": ([256], bf), "yq": ([256], f32), "tp": ([256], f32),
    "EC": ([1536], f32), "ZC": ([2048], f32), "L0": ([160], bf), "LM": ([160], bf), "BAR": ([160], bf), "XC": ([2560], bf), "OG": ([4096], bf),
    "BM": ([160], bf), "BN": ([128], bf),
    "io2": ([16], f32), "B2": ([160], bf), "I32": ([128], f16), "cn": ([4], f32), "pb": ([4], f32), "FS": ([256], bf), "M2": ([64, 16], f16),
    "KEY": ([160], bf), "k1": ([128], bf), "k2": ([160], bf), "k3": ([128], bf),
    "pc": ([4], i32), "GI": ([160], bf), "pd": ([12], i32), "col": ([64], f32), "IL": ([64], f32), "io16": ([16], f32), "IOT": ([256], bf),
    "SM": ([256], bf), "I": ([160], bf), "NI": ([128], bf), "BD": ([160], bf),
    "BK": ([160], bf), "PK": ([160], bf), "U0": ([128], bf), "U1": ([128], bf), "U2": ([128], bf), "HB": ([128], bf),
    "SH": ([128], bf), "TOP": ([128], bf), "BS": ([320], bf), "IS": ([320], bf), "ZW": ([320], f16),
    "WB": ([128], f16), "GT": ([36], bf), "CM": ([256], bf), "wa": ([16], f32), "wf": ([16], f32),
    "wl": ([8], u16), "p1": ([16], u16), "p2": ([8], u16), "c16": ([128], f16), "tc": ([128], f32),
}
PS = {"A0": [32, 16], "A1": [32, 16], "CB": [32, 16], "P1": [32, 16], "P2": [32, 16], "M0": [32, 16], "M1": [32, 16], "M2b": [32, 16]}
SCRATCH = {k: ("sbuf", [128] + v[0], v[1]) for k, v in SB.items()}
SCRATCH.update({k: ("psum", [128] + v, f32) for k, v in PS.items()})
NDMA = 100
SEMAPHORES = ["v", "s", "p", "g"] + ["d%d" % i for i in range(NDMA)] + ["arr%d" % t for t in range(2 * RO)] + ["snt%d" % t for t in range(2 * RO)]
SETS = [dict(cy=0.84, ga=1.3, sc=3.2, pe=0.47, hop=240.0, rate=450.0, xr=400.0, lat=650.0),
        dict(cy=0.95, ga=1.65, sc=4.2, pe=0.56, hop=210.0, rate=400.0, xr=330.0, lat=700.0)]
PLACE, ROWS, AHEAD = True, "chp", 600.0
STAGES = ((0, 0.3, 0.27, 50, 200.0), (0.3, 0.6, 0.27, 40, 200.0), (0, 1, 0.12, 10, 50.0), (0.55, 0.8, 0.14, 20, 80.0), (0.74, 1, 0.2, 30, 120.0))
NVG = (True, True)
PASSES, MOVES, HEAT, REACH, SPAN, SWEEPS, NEAR = 0, 1800000, 130.0, 10, 150, 70, 150.0
COPY = ["vvgg", "vvggg", "vvggg", "vvggg"]
CAND = [[("d", 4), ("d", 4), ("d", 4), ("v", 4)]] * 3 + [[("d", 4), ("d", 4), ("v", 8)]]
CM = 2
AL, FK = 16.0, -1025.0 / 256
SMALL = "vvvss"
SAME = False
OVER = False
LATE = ("U0", "NE", "CM", "SM", "IOT", "GT", "B2", "IL", "PK", "io2", "c184", "BM")
SEED = 12345
FIRST = 1000.0
GI, ACC, GP, GL = 1300.0, 2.0, 1100.0, 300.0
NHQ = (2, 2)
OQ = [("ssvv", "svvv")] * 4
EB = ("A1", "A1")
KC = ((4, 3, 0), (4, 3, 0))
JOIN = True
EC = ("ggg", "vg")
ZC = "dd"


def runs_of(nh):
    return [128 // nh * h * (h + 1) // 2 for h in range(nh + 1)]


PLAN = {"first": 3.0, "round": 14.3, "start": 0.0, "hold": 0.3, "label": 2.3, "repeat": 3.3, "answer": 3.5, "paths": 4.6, "piece": 0.75,
        "newest": 5.6, "number": 12.0, "upper": 7.6, "lower": 9.0, "live": 9.8, "candd": 7.5, "candv": 10.0, "per": 0.4, "count": 11.5, "cover": 16.5}
ORDER = []
BN = {"pl": "M1", "xn": "M1", "pv": "P1", "cl": "M1", "mk": "A0"}
SC = (0, 2, 6, 10, 16)
HC = (("v", 0, 2), ("s", 10, 12), ("v", 2, 4), ("s", 12, 14), ("v", 4, 6), ("v", 6, 8), ("s", 14, 16), ("v", 8, 10))
HS, HB, OB = 2, ("P1", "P2", "A1"), ("A1", "M0", "A0")
E1 = (4, 1)
TAIL = "A0"
CG = {"v": 256, "d": 512}
WIN = 8192


def build(g, T, rank, core, topo):
    ops = []

    def ref(name, lo=None, hi=None, step=1, parts=None):
        sh = SB[name][0]
        n = sh[0]
        lo = 0 if lo is None else lo
        hi = n if hi is None else hi
        p = slice(0, 128) if parts is None else slice(parts[0], parts[1])
        return {"ap": T[name][p, lo:hi:step] if step != 1 else T[name][p, lo:hi], "rg": [(name, lo, hi, (step, lo % step))],
                "n": len(range(lo, hi, step)), "two": SB[name][1] in (bf, u16, f16), "ps": False, "ind": False}

    def r3(name, a0=None, a1=None, b0=None, b1=None, step=1, parts=None, step0=1):
        ps = name in PS
        sh = PS[name] if ps else SB[name][0]
        a0 = 0 if a0 is None else a0
        a1 = sh[0] if a1 is None else a1
        b0 = 0 if b0 is None else b0
        b1 = sh[1] if b1 is None else b1
        p = slice(0, 128) if parts is None else slice(parts[0], parts[1])
        ap = T[name][p, a0:a1:step0, b0:b1:step]
        rows = [(a0, a1 - 1)] if ps or b1 - b0 == sh[1] else [(a, a) for a in range(a0, a1, step0)]
        return {"ap": ap, "rg": [(name, a * sh[1] + b0, b * sh[1] + b1, (1, 0)) for a, b in rows], "n": len(range(a0, a1, step0)) * len(range(b0, b1, step)),
                "two": (not ps) and SB[name][1] in (bf, u16, f16), "ps": ps, "ind": False}

    def pq(name, lo, hi, parts=None):
        return r3(name, lo // PS[name][1], hi // PS[name][1], parts=parts)

    def ind(win, off):
        return {"ap": win["ap"].indirect(off["ap"]), "rg": win["rg"], "off": off["rg"], "n": 16 * off["n"], "two": False, "ps": False, "ind": True}

    def col(k):
        return ref("col", k, k + 1)

    def add(eng, fn, outs, ins, cost, **kw):
        R, Wr = [], []
        for x in ins:
            if isinstance(x, dict):
                R += x["rg"] + x.get("off", [])
        for x in outs:
            Wr += x["rg"]
            R += x.get("off", [])
        o = {"e": eng, "fn": fn, "R": R, "W": Wr, "c": cost, "id": len(ops), "at": now[0], "t": now[3]}
        now[0] += now[1]
        o.update(kw)
        if eng == "g" and early[0] and outs and outs[0]["rg"][0][0] in LATE:
            o["after"] = first[0]
        ops.append(o)

    now = [0.0, 0.03, 0.0, -1]

    def at(name, more=0.0, step=0.4):
        now[0], now[1] = now[2] + PLAN[name] + more, step

    rows = {}

    def row(name):
        if name in rows and name[0] in ROWS:
            ops[-1].setdefault("behind", []).append(rows[name])
        rows[name] = len(ops) - 1

    first = []

    def ap(x):
        return x["ap"] if isinstance(x, dict) else x

    def vc(out, ins, per):
        if out["ind"]:
            return (50, out["n"], "sc")
        if ins[0]["ind"]:
            return (50, out["n"], "ga")
        return (0, max(64, per * ins[0]["n"]), "cy")

    def cp(out, a):
        add("v", lambda: g.vector.tensor_copy(out["ap"], a["ap"]), [out], [a], vc(out, [a], 0.5 if out["two"] and a["two"] else 1))

    def tt(out, a, b, op):
        add("v", lambda: g.vector.tensor_tensor(out["ap"], a["ap"], b["ap"], op), [out], [a, b], vc(out, [a], 1 if a["ps"] or b["ps"] else 2))

    early = [True]

    def ts(out, a, s1, op0, s2=None, op1=None):
        if early[0] and not a["ind"] and all(SB[x["rg"][0][0]][1] in (bf, f32) for x in (out, a)):
            if op0 == A.mult and op1 in (None, A.add):
                return act(out, a, F.Identity, bias=0.0 if op1 is None else s2, scale=s1)
            if op0 == A.add and op1 is None:
                return act(out, a, F.Identity, bias=s1)
        if op1 is None:
            fn = lambda: g.vector.tensor_scalar(out["ap"], a["ap"], ap(s1), None, op0)
        else:
            fn = lambda: g.vector.tensor_scalar(out["ap"], a["ap"], ap(s1), ap(s2), op0, op1)
        add("v", fn, [out], [a, s1, s2], vc(out, [a], 0.5 if out["two"] and a["two"] else 1))

    def ms(out, v):
        add("v", lambda: g.vector.memset(out["ap"], v), [out], [], (0, max(64, out["n"] * 0.5), "cy"))

    def tr(out, a):
        add("v", lambda: g.vector.transpose(out["ap"], a["ap"]), [out], [a], (0, a["n"], "cy"))

    def act(out, a, fn, bias=0.0, scale=1.0, acc=None):
        kw = {}
        if fn != F.Copy:
            kw["bias"] = ap(bias)
        if scale != 1.0:
            kw["scale"] = ap(scale)
        if acc is not None:
            kw["accum_out"] = acc["ap"]
        c = (65, out["n"], "ga") if a["ind"] else (20, max(64, out["n"]), "cy")
        add("s", lambda: g.scalar.activation(out["ap"], a["ap"], fn, **kw), [out] + ([acc] if acc else []), [a, bias, scale], c)

    def mms(lst):
        fn = lambda: [g.tensor.matmul(o["ap"], l["ap"], r["ap"], a, b) for o, l, r, a, b in lst][-1]
        add("p", fn, [x[0] for x in lst], [x[1] for x in lst] + [x[2] for x in lst], (0, sum(max(min(64, x[1]["n"]), x[2]["n"]) for x in lst), "pe"))

    def chain(out, pairs):
        return [(out, l, r, i == 0, i == len(pairs) - 1) for i, (l, r) in enumerate(pairs)]

    def group(out, pairs, cut=0):
        lst = chain(out, pairs)
        if cut:
            mms(lst[:cut])
        mms(lst[cut:])

    def sel(out, a, pat, cmp, fill, base, cm):
        add("g", lambda: g.affine_select(out["ap"], a["ap"], pat, cmp, fill, base, cm), [out], [a], (170, 2 * a["n"], "cy"))

    def iota(out, pat, base, cm):
        small = SB[out["rg"][0][0]][1] != i32
        if small:
            fn = lambda: g.iota(out["ap"], pat, base, cm, allow_small_or_imprecise_dtypes=True)
        else:
            fn = lambda: g.iota(out["ap"], pat, base, cm)
        add("g", fn, [out], [], (130, 2 * out["n"], "cy"))

    nd = [0]

    def dma(out, a, nbytes):
        sem = "d%d" % nd[0]
        nd[0] += 1
        add("y", lambda: g.sync.dma_start(ap(out), ap(a)), [out] if isinstance(out, dict) else [], [a], (60, 0, "cy"), sem=sem, nb=nbytes)

    def added(out, a):
        sem = "d%d" % nd[0]
        nd[0] += 1
        add("g", lambda: g.dma_start(out["ap"], a["ap"], accum_op=A.add), [out], [out, a], (GI, 0, "cy"), sem=sem, nb=256 * ACC * out["n"], pre=GP, late=GL)

    def lane0(lo, hi):
        r = ref("X", X0 + lo, X0 + hi)
        r["ap"] = T["X"][0:128:16, X0 + lo:X0 + hi]
        return r

    def copy(eng, out, a):
        if eng == "s":
            act(out, a, F.Copy)
        elif eng == "v":
            cp(out, a)
        elif eng == "g":
            sel(out, a, [[1, a["n"]]], A.is_ge, 0.0, 0, 0)
        else:
            dma(out, a, (256 if out["two"] else 512) * out["n"])

    def push(t, lo, hi, k):
        dst = T.cores[(rank - JUMPS[t]) % len(T.cores)]
        rid, pid, se = topo.addr(dst)
        src = ref("X", X0 + lo, X0 + hi)
        o = ref("xr%d" % t, lo, hi)
        add("g", lambda: g.remote_dma(o["ap"], src["ap"], T.sem["arr%d" % k], T.sem["snt%d" % k], pid, rid, topo.mask(core, dst)),
            [], [src], (600, 0, "cy"), sem="snt%d" % k, nb=(hi - lo) * 256, cnt=len(topo.engines(core, dst)), remote=True,
            pre=0.0 if t else FIRST, late=600.0)
        frm = T.cores[(rank + JUMPS[t]) % len(T.cores)]
        add("x", None, [o], [], (0, 0, "cy"), sem="arr%d" % k, cnt=len(topo.engines(frm, core)), after=len(ops) - 1)

    def swapped(bank, rows, mats, nh, start, *more):
        mms([x for c in range(2) for x in chain(r3(bank, c, 2 * rows, step0=2), list(more) + [
            (ref(mat, 160 * c + start(c, h), 160 * c + start(c, h) + 128), src(h)) for mat, src in mats for h in range(nh)])])

    halves = lambda c, h: 16 + 16 * (c - h)

    dma(ref("lf"), T.leaf[:], 8192)
    dma(ref("wt"), T.wts[:], 8192)
    dma(ref("cv"), T.cov[:], 65536)
    dma(ref("X", X0, X0 + B0), T.lab[:], 256 * B0)
    dma(ref("pt"), T.pth[:], 1048576)
    first.append(len(ops))
    push(0, 0, B0, 0)
    iota(ref("IOT"), [[1, 256]], 0, 0)
    dma(ref("ac"), T.act[:], 262144)
    iota(ref("pc", 0, 1), [[0, 1]], 0, 1)
    iota(ref("KEY"), [[1, 160]], -16, -1)
    iota(ref("GI"), [[1, 10], [0, 16]], -1, 0)
    iota(ref("io16"), [[1, 16]], 0, 0)
    iota(ref("IL"), [[16, 64]], B0, 1)
    iota(ref("SM"), [[0, 16], [1, 16]], 0, 0)
    for nm in ("X", "XA", "XB"):
        iota(ref(nm, 0, X0), [[0, X0]], 300, 0)
    p = ref("pc", 0, 1)
    fields = [(4, 7), (4, 1), (5, 3), (3, 1), (0, 3), (2, 1), (0, 15), (1, 6), (0, 7), (0, 1)]
    for i, (sh, mk) in enumerate(fields):
        ts(ref("pd", i, i + 1), p, sh, A.arith_shift_right, mk, A.bitwise_and)
    cp(ref("col", 0, 6), ref("pd", 0, 6))
    cp(ref("col", 41, 45), ref("pd", 6, 10))
    cg, hf, pr, up, lo4, b2 = [col(i) for i in range(6)]
    pm, h6, lo8, odd = [col(41 + i) for i in range(4)]
    ts(ref("BD"), ref("GI"), cg, A.is_equal)
    K = ref("KEY", 16, 144)
    ts(ref("I"), ref("KEY"), 0.0, A.is_equal)
    I_, NI, BDm = ref("I", 16, 144), ref("NI"), ref("BD", 16, 144)
    ts(NI, I_, -1.0, A.mult)
    ts(col(10), hf, -1.0, A.mult, 1.0, A.add)
    half = [col(10), hf]
    for c in range(2):
        ts(ref("IS", 160 * c, 160 * c + 160), ref("I"), half[c], A.mult)
        ts(ref("BS", 160 * c, 160 * c + 160), ref("BD"), half[c], A.mult)
    ts(ref("wa"), ref("wt"), 2047.5, A.is_ge, -4096.0, A.mult)
    tt(ref("wf"), ref("wt"), ref("wa"), A.add)
    ts(ref("pd", 11, 12), ref("wt", 0, 1), 1023, A.bitwise_and)
    ts(col(11), ref("pd", 11, 12), 4.0, A.mult)
    ts(ref("wl"), ref("io16", 0, 8), 0.0, A.mult, pm, A.add)
    ts(ref("k4"), BDm, 1.0 / 4096, A.mult)
    tt(ref("WB"), ind(ref("wf"), ref("wl")), ref("k4"), A.mult)
    ts(ref("NH"), I_, -63.0 / 8192, A.mult)
    iota(ref("HF"), [[0, 256]], 65, 0)
    ms(ref("ZW"), 0.0)
    for c in range(2):
        ts(col(12 + c), half[1 - c], 100.0, A.mult, pr, A.add)
        for m, wc in enumerate((col(11), ref("wf", 1, 2))):
            ts(ref("ZW", 160 * c + 32 + m, 160 * c + 160, 32), ref("io16", 0, 4), col(12 + c), A.is_equal, wc, A.mult)
    ts(col(15), lo4, 32.0, A.mult, h6, A.add)
    ts(ref("hp"), ref("io16", 0, 2), col(15), A.add)
    cp(ref("LU"), ref("lf"))
    ts(ref("LO"), ref("lf"), LOFF, A.add)
    ts(ref("c16"), ref("cv"), X0 - 1024.0, A.add)
    swapped("M1", 4, [("IS", lambda h: ref("c16", 64 * h, 64 * h + 64))], 2, halves)
    tr(ref("tc"), pq("M1", 0, 128))
    ts(col(16), lo4, 32.0, A.mult, up, A.add)
    ts(col(17), b2, 16.0, A.mult, col(16), A.add)
    ts(ref("p2"), ref("io16", 0, 8), 2.0, A.mult, col(17), A.add)
    ts(ref("COV", 0, 128), ind(ref("tc"), ref("p2")), 1024.0, A.add)
    for nm in ("BK", "PK", "GT", "BM"):
        iota(ref(nm), [[0, SB[nm][0][0]]], 0, 0)
    ts(ref("BK", 16, 144, 16), ref("io16", 0, 8), cg, A.is_equal)
    ts(ref("BM", 16, 144, 16), ref("BK", 16, 144, 16), KM, A.mult)
    ts(ref("BN"), ref("BK", 8, 136), KN, A.mult)
    ts(col(22), pm, min([16] + [a for kind, a, b in HC if kind == "s"]) - 0.5, A.is_ge, 4.5 * KM, A.mult)
    ts(col(23), col(22), -11.5 * KM, A.add)
    ts(ref("BAR"), ref("GI"), 0.0, A.mult, col(23), A.add)
    ts(ref("PK", 16, 144, 16), ref("BK", 16, 144, 16), -1.0, A.mult)
    ts(ref("PK", 24, 152, 16), ref("BK", 16, 144, 16), 1.0, A.mult)
    ts(ref("GT", 3, 35, 4), ref("BK", 16, 144, 16), 1.0, A.mult)
    ts(col(24), lo8, 32.0, A.mult, up, A.add)
    iota(ref("io2"), [[16, 2], [2, 8]], 0, 0)
    ts(ref("p1"), ref("io2"), col(24), A.add)
    ts(col(20), up, 15.0, A.mult, col(24), A.add)
    ts(ref("p3"), ref("io16"), col(20), A.add)
    ts(col(21), up, -385.0 * 512, A.mult, C0 - 1, A.add)
    ts(col(25), up, -3448.0 * 512 - 1577216.0, A.mult, 1577216.0, A.add)
    ts(col(26), pm, -K2, A.mult, -17 * K2, A.add)
    ts(col(27), pm, -K2, A.mult, -K2 - LIVE, A.add)
    ts(ref("k1"), BDm, -K2, A.mult)
    sel(ref("U0"), ref("k1"), [[1, 128]], A.is_gt, 0.0, 0, -1)
    sel(ref("U0"), ref("U0"), [[1, 128]], A.not_equal, K2, 0, -1)
    ts(ref("k2"), ref("I"), up, A.mult)
    ts(col(29), up, -1.0, A.mult, 1.0, A.add)
    ts(ref("k3"), I_, col(29), A.mult)
    for j, (nm, low) in enumerate((("U1", ref("k3")), ("U2", ref("k2", 24, 152)))):
        group(pq("A%d" % j, 0, 128), [(low, ref("U0")), (ref("k2", 16, 144), ref("k1"))])
        act(ref(nm), pq("A%d" % j, 0, 128), F.Copy)
    ts(ref("HB"), BDm, up, A.mult)
    ts(col(33), pm, 14.5, A.is_lt)
    ts(ref("SH"), K, 1.0, A.is_equal, col(33), A.mult)
    ts(col(34), pm, 0.0, A.is_equal)
    ts(ref("TOP"), I_, col(34), A.mult)
    for t in range(RO):
        ts(col(36 + t), col(34), B0 + S * t - 1024.0, A.mult, 1024.0 - LIVE, A.add)
    ts(ref("CM"), ref("SM"), pm, A.is_ge, 65536.0, A.mult)
    iota(r3("NE"), [[0, 400]], 0, 0)
    for lo, hi, h in ((0, 17, 0.0), (17, 50, 16.0)):
        ts(r3("RS", 0, 8, lo, hi), r3("NE", 0, 8, lo, hi), h, A.add, pm, A.add)
    ts(col(40), cg, -16.0, A.mult, -1024.0, A.add)
    ts(ref("I16"), ref("IL"), col(40), A.add)
    iota(ref("B2"), [[0, 160]], 0, 0)
    for u in range(2):
        ts(ref("B2", 16 + u, 144, 16), ref("BK", 16, 144, 16), 1.0, A.mult)
        ts(col(57 + u), odd, 1.0 - u, A.is_equal, -32768.0, A.mult)
        ts(ref("I32", u, 128, 2), ref("I16"), col(57 + u), A.add)
    early[0] = False

    def as_list(out, src, bank, mid, perm, *how):
        swapped(bank, 8, [("IS", lambda h: ref(src, 128 * h, 128 * h + 128))], 2, halves)
        tr(ref(mid), pq(bank, 0, 256))
        ts(ref(out), ind(ref(mid), ref(perm)), *how)

    def path_list():
        as_list("PL", "PV", BN["pl"], "tp", "p1", 1024.0, A.add)

    for t in range(RO):
        B = B0 + S * t
        last = t == RO - 1
        z, cs, lvn = ref("z%d" % (t & 1)), ref("cs%d" % (t & 1)), "lv%d" % (t & 1)
        lv = r3(lvn)
        snap = "X" + "AB"[t & 1]
        Xw = ref("X", X0, X0 + B)
        fr = (8 + t) / 16.0
        old = B if t == 0 else B - S
        wd = old // 16
        now[2:] = [PLAN["first"] + PLAN["round"] * t, t]
        at("start", 0.0, 0.0)
        if t:
            push(t, 0, B, t)
        cuts = [wd * i for i in SC] + ([B] if t else [])
        for i in range(len(cuts) - 1):
            at("start", 0.3 * i)
            a, b = cuts[i], cuts[i + 1]
            e = COPY[t][min(i, len(COPY[t]) - 1)]
            copy(e, ref(snap, X0 + a, X0 + b), T.lab[:, a:b] if t == 0 and e == "d" else ref("X", X0 + a, X0 + b))
        dma(ref("L0", 0, wd), lane0(0, old), 256 * wd)
        at("start")
        copy(SMALL[3], ref("xv"), ind(Xw, ref("LU")))
        swapped("M1", 4, [("ZW", lambda h: ref("xv", 64 * h, 64 * h + 64))], 4, lambda c, h: 32 - 2 * h)
        tr(ref("tx"), pq("M1", 0, 128))
        cp(ref("hi"), ind(ref("tx"), ref("hp")))
        ts(ref("ha"), ref("hi"), 4095, A.bitwise_and)
        ts(ref("LA"), ref("ha", 0, 16), 0.25, A.mult)
        ts(ref("LQ"), ref("ha", 16, 32), fr, A.mult, -15.0 / 32, A.add)
        if t == 0:
            ts(ref("PV"), ind(ref("pt"), ref("LU")), -1024.0, A.add)
            path_list()
        at("label")
        if SMALL[0] == "v":
            tt(ref("av"), ind(ref("ac"), ref("LA")), ref("xv"), A.subtract)
            act(z, ref("av"), F.Abs)
        else:
            act(ref("av"), ind(ref("ac"), ref("LA")), F.Copy)
            group(pq("M0", 0, 256), [(I_, ref("xv")), (NI, ref("av"))])
            act(z, pq("M0", 0, 256), F.Abs)
        hs = [(ref("NH"), ref("HF")), (ref("WB"), z)]
        group(pq("M2b", 0, 256), hs, 1)
        ts(ref("cq"), pq("M2b", 0, 256), BIG, A.add, BIG, A.subtract)
        group(pq("M2b", 0, 256), [hs[1], (NI, ref("cq"))])
        ts(ref("rm"), pq("M2b", 0, 256), 4096.0, A.mult, -2048.0, A.add)
        as_list("CL", "rm", BN["cl"], "tq", "p3", fr, A.mult, 2048 * fr - 15.0 / 32, A.add)
        at("number")
        ts(ref("CU"), ref("rm"), fr, A.mult, 2048 * fr - 15.0 / 32, A.add)
        ts(cs, ref("CU"), -1024.0, A.add)
        at("repeat")
        act(ref("ZC", 0, 256), z, F.Identity, bias=col(21), scale=-1.0)
        for i, e in enumerate(ZC):
            copy(e, ref("ZC", 256 << i, 512 << i), ref("ZC", 0, 256 << i))
        m0 = 0
        for kind, n in CAND[t]:
            at("cand" + kind, PLAN["per"] * m0 if kind == "d" else 0.0, PLAN["per"] * CG[kind] / 256)
            for a in range(256 * m0, 256 * (m0 + n), CG[kind]):
                b = min(a + CG[kind], 256 * (m0 + n))
                src = ind(ref(snap, X0, X0 + B), ref("CL", a // 16, b // 16))
                if kind == "v":
                    tt(ref("SG", a, b), src, ref("ZC", 0, b - a), A.add)
                else:
                    copy("s", ref("SG", a, b), src)
                row("c" + kind)
            if kind == "d":
                added(ref("SG", 256 * m0, 256 * (m0 + n)), ref("ZC", 0, 256 * n))
            m0 += n
        e1 = ref("EC", 896, 1152)
        at("answer", 0.0, 0.1)
        act(e1, ind(ref("xr%d" % t), ref("LQ")), F.Identity, bias=C0, scale=-1.0)
        for q in (1, 0):
            nv = OQ[t][q].count("v")
            for i, w in enumerate((128, 256, 512)[:3 if JOIN and "dd" in OQ[t][q] else 2 if nv > E1[q] or "d" in OQ[t][q] else min(nv, 1)]):
                if EC[q][i] == "D":
                    for c in (512, 256, 0):
                        copy("d", ref("EC", c, c + 256), ref("EC", 768, 1024))
                    break
                copy(EC[q][i], ref("EC", 1024 + w, 1024 + 2 * w) if q else ref("EC", 1024 - 2 * w, 1024 - w), ref("EC", 1024, 1024 + w) if q else ref("EC", 1024 - w, 1024))
        if SMALL[4] == "s":
            act(ref("EB"), e1, F.Identity, bias=C0, scale=-1.0)
        else:
            ts(ref("EB"), e1, -1.0, A.mult, C0, A.add)
        if SMALL[1] == "s":
            act(ref("EM"), ref("EB"), F.Relu, bias=-255 * LIVE, scale=LIVE)
        else:
            ts(ref("EM"), ref("EB"), 255.5, A.is_gt, LIVE, A.mult)
        Xa = ref("X", 0, X0 + B)
        mk = pq(BN["mk"], 0, wd)
        at("start")
        mms([(mk, I_, ref("BAR", 0, wd), True, False)])
        done = nb = 0
        seen = {"v": 0, "s": 0}
        for kind, a, b in HC:
            at("hold", 0.17 * seen[kind])
            seen[kind] += b - a
            src = ind(Xa, ref("COV", wd * a // 16, wd * b // 16))
            if kind == "v":
                tt(ref("C", wd * a, wd * b), src, ref(snap, X0 + wd * a, X0 + wd * b), A.is_le)
            else:
                act(ref("XC", wd * a, wd * b), src, F.Copy)
            row("h" + kind)
            step = b - a if kind == "v" else HS
            for c in range(a, b, step):
                d = min(b, c + step)
                if kind == "s":
                    bank = pq(HB[nb % len(HB)], 0, wd * (d - c))
                    nb += 1
                    group(bank, [(I_, ref("X", X0 + wd * c, X0 + wd * d)), (NI, ref("XC", wd * c, wd * d))], 1)
                    act(ref("C", wd * c, wd * d), bank, F.Sign, bias=0.5)
                done += d - c
                mms([(mk, ref("BM", 16 - i, 144 - i), ref("C", wd * i, wd * i + wd), False, done == 16 and i == d - 1) for i in range(c, d)])
        tt(ref("LM", 0, wd), mk, ref("L0", 0, wd), A.max)
        dma(lane0(0, old), ref("LM", 0, wd), 256 * wd)
        if t:
            at("newest")
            tt(ref("C", old, B), ind(ref(snap, 0, X0 + B), ref("COV", old // 16, B // 16)), ref("X", X0 + old, X0 + B), A.is_le)
        seen = {"v": 0, "s": 0, "d": 0}
        nb = 0
        for q in (1, 0):
            s0, pb = 128 * q, "P%d" % (q + 1)
            for n, k in enumerate((12, 8, 4, 0)):
                at("paths", PLAN["piece"] * seen[OQ[t][q][n]], 0.3)
                seen[OQ[t][q][n]] += 1
                a = 2048 * q + 128 * k
                ec = lambda w: ref("EC", 1024, 1024 + w) if q else ref("EC", 1024 - w, 1024)
                if OQ[t][q][n] == "d":
                    act(ref("O", a, a + 512), ind(Xw, ref("PL", a // 16, a // 16 + 32)), F.Copy)
                    row("ps")
                    nd2 = OQ[t][q].count("d") if JOIN else 1
                    if n % nd2 == nd2 - 1:
                        added(ref("O", a, a + 512 * nd2), ec(512 * nd2))
                elif OQ[t][q][n] == "s":
                    act(ref("OG", a, a + 512), ind(Xw, ref("PL", a // 16, a // 16 + 32)), F.Copy)
                    row("ps")
                    bank = OB[nb % len(OB)]
                    nb += 1
                    mms([(pq(bank, 128 * j, 128 * j + 128), NI, ref("EB", s0, s0 + 128), j == 0, False) for j in range(4)])
                    mms([(pq(bank, 0, 512), I_, ref("OG", a, a + 512), False, True)])
                    act(ref("O", a, a + 512), pq(bank, 0, 512), F.Identity, bias=C0)
                else:
                    w = 256 if OQ[t][q][:n].count("v") < E1[q] else 512
                    for b in range(a, a + 512, w):
                        tt(ref("O", b, b + w), ind(Xw, ref("PL", b // 16, (b + w) // 16)), ec(w), A.add)
                        row("pv")
            for n, k in enumerate((12, 8, 4, 0)):
                at("paths", PLAN["piece"] * (n + 1 + (0 if q else 1.5)), 0.1)
                for j0 in (k + 2, k):
                    mms([(pq(pb, 128 * (n // 2), 128 * (n // 2) + 128), ref("PK", 16 - j % 8, 144 - j % 8), ref("O", 2048 * q + 128 * j, 2048 * q + 128 * j + 128),
                          j % 8 == 7, j == 8 or (j == 0 and not t)) for j in (j0 + 1, j0)])
            if t:
                mms([(pq(pb, 128, 256), ref("BN"), ref("C", old + s0, old + s0 + 128), False, True)])
        dma(lane0(0, old), ref("L0", 0, wd), 256 * wd)
        for q in (1, 0):
            s0, pb, wb, nh = 128 * q, "P%d" % (q + 1), ("M0", "M2b")[q], NHQ[q]
            fq = "F%d" % (q + 1)
            at("upper" if q else "lower", 0.0, 0.25)
            act(ref(fq), pq(pb, 0, 256), F.Sign, bias=col(25))
            group(pq(wb, 0, 128), [(I_, ref("PV", s0, s0 + 128)), (NI, ref("EM", s0, s0 + 128)), (ref("U2"), ref(fq, 0, 128)), (ref("U1"), ref(fq, 128, 256))], 2)
            group(pq("M1", s0, s0 + 128), [(ref("HB"), ref(fq, 0, 128)), (ref("HB"), ref(fq, 128, 256))])
            mt = r3("MT", 8 * q, 8 * q + 8)
            ts(mt, pq(wb, 0, 128), col(26), A.add, -NONE, A.max)
            swapped(wb, 4, [("BS", lambda h: r3("MT", 8 * q + h, 8 * q + 8, step0=2))], 2, halves)
            eb = EB[q] or wb
            if EB[q]:
                mms([(pq(eb, 128, 256), I_, ref("CM", 0, 128), True, False)])
                mms([(pq(eb, 128, 256), BDm, mt, False, False), (r3(eb, 16, 24, step0=2), BDm, r3("MT", 8 * q, 8 * q + 8, step0=2), False, True)])
            else:
                group(pq(wb, 128, 256), [(I_, ref("CM", 0, 128)), (BDm, mt)])
                group(r3(wb, 16, 24, step0=2), [(BDm, r3("MT", 8 * q, 8 * q + 8, step0=2))])
            tr(r3("LR", 8 * q, 8 * q + 8), pq(wb, 0, 128))
            top = r3("LR", 8 * q, 8 * q + 8, 0, 1)
            if NVG[q]:
                ts(ref("GL", 8 * q, 8 * q + 8), top, 16 * NONE + NOT, A.add)
            act(r3("RS", 4 * q, 4 * q + 4, 0, 18, 17), top, F.Identity, bias=16 * NONE + NOT)
            for h, d, c in ((0, 0, 1), (1, 0, 18), (1, 1, 34)):
                tt(r3("NE", 4 * q, 4 * q + 4, c, c + 16), r3("LR", 8 * q + h, 8 * q + 8, step0=2),
                   r3(eb, 8 + h, 16, step0=2) if d == h else r3(eb, 16 + d, 24, step0=2), A.not_equal)
            for j1, j0 in zip(KC[q], KC[q][1:]):
                j0, j1 = 4 * q + j0, 4 * q + j1
                kp, rs, ne = [r3(nm, j0, j1) for nm in ("KP", "RS", "NE")]
                add("v", lambda j0=j0, j1=j1: [g.vector.tensor_tensor_scan(T.KP[:, j], T.NE[:, j], T.RS[:, j], 0.0, A.mult, A.max) for j in range(j0, j1)][-1],
                    [kp], [rs, ne], (0, 64 * (j1 - j0), "cy"))
                cp(ref("TL", 2 * j0, 2 * j1), r3("KP", j0, j1, 16, 50, 33))
            tt(ref("NV", s0, s0 + 128), ind(ref(snap, 0, X0 + B), ref("GL" if NVG[q] else "TL", 8 * q, 8 * q + 8)), ref("EB", s0, s0 + 128), A.max)
            for b in range(8 * q + 8 - nh, 8 * q - 1, -nh):
                cp(ind(Xa, ref("TL", b, b + nh)), ref("NV", 16 * b, 16 * (b + nh)))
        at("live", 0.0, 0.25)
        act(lv, pq("M1", 0, 256), F.Relu, bias=-7 * LIVE, scale=-LIVE / 2, acc=ref("cn", t, t + 1))
        group(r3("P1", 0, 2), [(I_, ref("I32", 32 * t, 32 * t + 32))] + [(ref("B2", 16 - i, 144 - i), r3(lvn, 0, 16, i, i + 2)) for i in range(0, 16, 2)])
        for u in range(2):
            tt(ref("LO"), r3("P1", 0, 2, u, 16, 2), ref("LO"), A.max)
        if not last:
            ts(ref("LU"), ref("LO"), -LOFF, A.add)
        else:
            act(ref("LV"), ref("LO"), F.Identity, bias=-LOFF)
        at("live", 0.4, 0.3)
        group(pq(BN["xn"], 0, 256), [(I_, z), (NI, lv)])
        if SMALL[2] == "s":
            act(ref("Y"), pq("M1", 0, 256), F.Relu, scale=-1.0, bias=256.0 - LIVE)
            act(ref("X", X0 + B, X0 + B + S), ref("Y"), F.Identity, bias=256.0, scale=-1.0)
        else:
            ts(ref("X", X0 + B, X0 + B + S), pq(BN["xn"], 0, 256), LIVE, A.add, 256.0, A.min)
        group(pq("P2", 0, 256), [(ref("SH"), ref("PV")), (ref("TOP"), ref("IOT")), (I_, lv)])
        yp = ref("YP", S * t, S * t + S)
        act(yp, pq("P2", 0, 256), F.Relu, bias=col(36 + t))
        dma(T.yp[:, S * t:S * t + S], yp, 131072)
        if not last:
            act(ref("yq"), yp, F.Identity, bias=-1024.0)
            group(pq(BN["pv"], 0, 256), [(I_, ref("PV")), (NI, lv)])
            tt(ref("PV"), pq(BN["pv"], 0, 256), ref("yq"), A.max)
            path_list()
        at("count", 0.0, PLAN["per"] * CM / (2 if last else 1))
        for m0 in range(0, 16, CM):
            for s0, s1, cb in ((0, 128, "CB"), (128, 256, TAIL)) if last else ((0, 256, "CB"),):
                mms([(pq(cb, s0, s1), ref("BK", 16 - m, 144 - m), ref("SG", 256 * m + s0, 256 * m + s1), m == 0, m == 15) for m in range(m0, m0 + CM)])
        at("cover")
        act(ref("py", t, t + 1), ref("cn", t, t + 1), F.Identity, bias=-512.5 * AL, scale=AL / LIVE)
        act(ref("pb", t, t + 1), ref("cn", t, t + 1), F.Identity, bias=ref("py", t, t + 1), scale=-AL / LIVE)
        if last:
            for a, cb, yb in ((0, "CB", "P1"), (128, TAIL, "P2")):
                yc = pq(yb, 0, 128, (0, 32))
                m2 = lambda r: r3("M2", 16 * r + a // 16, 16 * r + a // 16 + 8)
                mms([(yc, ref("GT", 3 - r, 35 - r), m2(r), r == 0, False) for r in range(t)])
                act(ref("FS", a, a + 128), pq(cb, a, a + 128), F.Sign, bias=ref("pb", t, t + 1), scale=FK)
                group(pq(cb, a, a + 128), [(ref("U0"), ref("FS", a, a + 128)), (I_, r3(lvn, a // 16, a // 16 + 8)), (I_, ref("cs%d" % (t & 1), a, a + 128))])
                ts(m2(t), pq(cb, a, a + 128), col(27), A.add, -1025.0, A.max)
                mms([(yc, ref("GT", 3 - t, 35 - t), m2(t), False, True)])
                act(ref("YC", a, a + 128, parts=(0, 32)), yc, F.Identity, bias=16399.0)
            continue
        act(ref("FS"), pq("CB", 0, 256), F.Sign, bias=ref("pb", t, t + 1), scale=FK)
        group(pq("CB", 0, 256), [(ref("U0"), ref("FS")), (I_, lv), (I_, cs)])
        ts(r3("M2", 16 * t, 16 * t + 16), pq("CB", 0, 256), col(27), A.add, -1025.0, A.max)
        group(r3("CB", 0, 1, 0, 16), [(ref("BK", 16 - i, 144 - i), r3("M2", 16 * t, 16 * t + 16, i, i + 1)) for i in range(16)])
        ts(ref("COV", B // 16, B // 16 + 16), r3("CB", 0, 1, 0, 16), 16399.0 + X0, A.add)
    dma(T.yx[:, 0:W - S], ref("X", X0, X0 + W - S), 720896)
    dma(T.yx[:, W - S:W], ref("X", X0 + W - S, X0 + W), 65536)
    dma(T.yv[:], ref("LV"), 8192)
    dma(T.yc[:], ref("YC", parts=(0, 32)), 32768)
    return ops


def depend(ops):
    seen = {}
    for o in ops:
        d = {}
        if "after" in o:
            d[o["after"]] = False
        for j in o.get("behind", []):
            d[j] = False
        for kind in ("R", "W"):
            for (nm, lo, hi, par) in o[kind]:
                ps = nm in PS
                for (j, k2, l2, h2, p2) in seen.get(nm, []):
                    if j == o["id"]:
                        continue
                    same = ops[j]["e"] == o["e"]
                    if ps:
                        d[j] = d.get(j, False) or not same
                    elif (kind == "W" or k2 == "W") and lo < h2 and l2 < hi and (par[0] != p2[0] or par == p2):
                        d[j] = d.get(j, False) or not (SAME and same and kind == "W" and "nb" not in o and "nb" not in ops[j])
        o["d"] = d
        for kind in ("R", "W"):
            for (nm, lo, hi, par) in o[kind]:
                lst = seen.setdefault(nm, [])
                if nm in PS:
                    lst[:] = [x for x in lst if ops[x[0]]["e"] != o["e"]][-3:]
                elif kind == "W":
                    lst[:] = [x for x in lst if not (lo <= x[2] and x[3] <= hi and par in ((1, 0), x[4]))]
                lst.append((o["id"], kind, lo, hi, par))


def schedule(ops):
    n = len(ops)
    res = ["dma" if "nb" in o else o["e"] for o in ops]
    sets = []
    for m in SETS:
        per = {"cy": m["cy"], "ga": m["cy"] * m["ga"], "sc": m["cy"] * m["sc"], "pe": m["pe"]}
        dur = [o["nb"] / m["xr" if o.get("remote") else "rate"] + 60 if "nb" in o else o["c"][0] + o["c"][1] * per[o["c"][2]] for o in ops]
        tail = [m["lat"] + o.get("late", 0) if "nb" in o else 0 for o in ops]
        pred = [[(j, tail[j] + m["hop"] if w else tail[j] if o["e"] != "g" else -1e6) for j, w in o["d"].items()] for o in ops]
        sets.append((dur, tail, pred))
    dur, tail, pred = sets[0]
    post = [[] for _ in ops]
    for i in range(n):
        for j, lag in pred[i]:
            post[j].append((i, lag))

    def place(seq, before):
        st = [0.0] * n
        busy = {}
        for i in seq:
            t = max([st[j] + dur[j] + lag for j, lag in before[i]] + [0.0])
            b = busy.setdefault(res[i], [])
            lo, hi = 0, len(b)
            while lo < hi:
                mid = (lo + hi) // 2
                if b[mid][1] <= t:
                    lo = mid + 1
                else:
                    hi = mid
            while lo < len(b) and b[lo][0] < t + dur[i]:
                t = max(t, b[lo][1])
                lo += 1
            b.insert(lo, (t, t + dur[i]))
            st[i] = t
        return st

    que = ["vspgyx".index(o["e"]) for o in ops]
    issue = [o["c"][0] if "nb" in o else -1 for o in ops]
    pre = [o.get("pre", 0.0) for o in ops]
    ends = [i for i in range(n) if not post[i]]

    def replay(seq, s, start=0, base=None):
        du, ta, pr = s
        k = start // 32
        end, snaps = (base[1][:], base[2][:k + 1]) if base else ([0.0] * n, [[0.0] * 7])
        free = snaps[k][:]
        for a in range(32 * k, n, 32):
            for i in seq[a:a + 32]:
                e = que[i]
                t = free[e]
                for j, lag in pr[i]:
                    x = end[j] + lag
                    if x > t:
                        t = x
                if issue[i] >= 0:
                    free[e] = t + issue[i]
                    e = 6
                    t += pre[i]
                    if free[6] > t:
                        t = free[6]
                end[i] = free[e] = t + du[i]
            snaps.append(free[:])
        return max(end[i] + ta[i] for i in ends), end, snaps

    seed = [SEED]

    def rnd():
        seed[0] = (seed[0] * 1103515245 + 12345) % 2147483648
        return seed[0] / 2147483648.0

    def topo_by(key, before, after):
        left = [len(before[i]) for i in range(n)]
        rank = sorted(range(n), key=lambda i: key[i])
        pos = [0] * n
        for k, i in enumerate(rank):
            pos[i] = k
        pool = sorted(pos[i] for i in range(n) if not left[i])
        out = []
        while pool:
            i = rank[pool.pop(0)]
            out.append(i)
            new = []
            for j, lag in after[i]:
                left[j] -= 1
                if not left[j]:
                    new.append(pos[j])
            if new:
                pool = sorted(pool + new)
        return out

    def both(key):
        back = place(topo_by(key, post, pred), post)
        st = place(topo_by([-(back[i] + dur[i]) for i in range(n)], pred, post), pred)
        seq = topo_by(st, pred, post)
        return sum(replay(seq, s)[0] for s in sets) / len(sets), st, seq

    def planned():
        seq = topo_by([o["at"] for o in ops], pred, post)
        if PLACE:
            seq = topo_by(place(seq, pred), pred, post)
        return sum(replay(seq, s)[0] for s in sets) / len(sets), [], seq

    best = planned() if PASSES == 0 else both([-float(i) for i in range(n)])
    cur = best
    for it in range(PASSES):
        st = cur[1]
        a = best[0] * rnd()
        b = a + 1000.0 + 5000.0 * rnd()
        amp = 2500.0 * rnd() ** 2
        eng = "vsp*"[int(4 * rnd())]
        new = both([-(st[i] + dur[i]) + (amp * (rnd() - 0.5) if a <= st[i] <= b and eng in ("*", res[i]) else 0.0) for i in range(n)])
        if new[0] <= cur[0] + 150.0 * (1.0 - it / PASSES):
            cur = new
        if new[0] < best[0]:
            best = new

    anc = []
    for i in range(n):
        far = set()
        for j, w in ops[i]["d"].items():
            if w:
                far |= anc[j]
        for du, ta, pr in sets:
            pr[i] = [(j, lag) for j, lag in pr[i] if j not in far or issue[j] >= 0]
        anc.append(set(ops[i]["d"]).union(*[anc[j] for j in ops[i]["d"]]))
    succ = []
    for du, ta, pr in sets:
        sc = [[] for _ in ops]
        for i in range(n):
            for j, lag in pr[i]:
                sc[j].append((i, lag))
        succ.append(sc)
    before = [[j for j, lag in x] for x in pred]
    after = [[j for j, lag in x] for x in succ[0]]
    seq = best[2][:]
    pos, bq, aq, bd, ad = [0] * n, [n] * (n + 1), [n] * (n + 1), [n] * (n + 1), [n] * (n + 1)
    tm = [[[0.0] * (n + 1) for _ in range(5)] for _ in sets]

    def links():
        last = [n] * 7
        for p, i in enumerate(seq):
            pos[i] = p
            e = que[i]
            bq[i] = k = last[e]
            aq[i] = n
            if k < n:
                aq[k] = i
            last[e] = i
            if issue[i] >= 0:
                bd[i] = k = last[6]
                ad[i] = n
                if k < n:
                    ad[k] = i
                last[6] = i

    def times(lo, hi, r0, r1):
        for (du, ta, pr), sc, (st, end, fr, up, dn) in zip(sets, succ, tm):
            for i in seq[lo:r1]:
                t = fr[bq[i]]
                for j, lag in pr[i]:
                    x = end[j] + lag
                    if x > t:
                        t = x
                st[i] = t
                if issue[i] >= 0:
                    fr[i] = t + issue[i]
                    end[i] = max(t + pre[i], end[bd[i]]) + du[i]
                else:
                    end[i] = fr[i] = t + du[i]
            for i in reversed(seq[r0:hi + 1]):
                t = ta[i]
                for j, lag in sc[i]:
                    x = up[j] + lag
                    if x > t:
                        t = x
                if issue[i] >= 0:
                    dn[i] = max(t, dn[ad[i]]) + du[i]
                    up[i] = max(pre[i] + dn[i], issue[i] + up[aq[i]])
                else:
                    x = up[aq[i]]
                    up[i] = (x if x > t else t) + du[i]

    def total(r0, r1, rest):
        return [max([top] + [st[i] + up[i] if issue[i] < 0 else max(st[i] + up[i], end[i] - du[i] + dn[i]) for i in seq[r0:r1]])
                for (du, ta, pr), (st, end, fr, up, dn), top in zip(sets, tm, rest)]

    def passing(r0, r1):
        out = []
        for (du, ta, pr), (st, end, fr, up, dn) in zip(sets, tm):
            top = max([end[i] + ta[i] for i in seq[:r0]] + [0.0])
            for i in seq[r1:]:
                t = fr[bq[i]] if bq[i] == n or pos[bq[i]] < r0 else 0.0
                for j, lag in pr[i]:
                    if pos[j] < r0 and end[j] + lag > t:
                        t = end[j] + lag
                top = max(top, t + up[i])
                if issue[i] >= 0 and bd[i] < n and pos[bd[i]] < r0:
                    top = max(top, end[bd[i]] + dn[i])
            out.append(top)
        return out

    def critical(k, r0, r1, bar):
        (du, ta, pr), (st, end, fr, up, dn) = sets[k], tm[k]
        out = []
        for i in seq[r0:r1]:
            j = bq[i]
            if j < n and st[i] + up[i] >= bar and fr[j] >= st[i] - 1e-6 and pos[j] >= r0:
                out.append((j, i))
            j = bd[i]
            if j < n and end[i] - du[i] + dn[i] >= bar and end[j] > st[i] + pre[i] and pos[j] >= r0:
                out.append((j, i))
        return out

    def relink(p, mid, free, nxt):
        seq[p:p + len(mid)] = mid
        last = dict(free)
        for i in mid:
            pos[i] = p
            p += 1
            bq[i] = k = last[que[i]]
            aq[k] = last[que[i]] = i
            if issue[i] >= 0:
                bd[i] = k = last[6]
                ad[k] = last[6] = i
        for e, k in nxt.items():
            (ad if e == 6 else aq)[last[e]] = k
            (bd if e == 6 else bq)[k] = last[e]

    def price(old, mid, tot, room):
        free, nxt, low = {}, {}, 0.0
        for i in old:
            free.setdefault(que[i], bq[i])
            nxt[que[i]] = aq[i]
            if issue[i] >= 0:
                free.setdefault(6, bd[i])
                nxt[6] = ad[i]
        for (du, ta, pr), sc, (st, end, fr, up, dn), was in zip(sets, succ, tm, tot):
            f = {e: (end if e == 6 else fr)[k] for e, k in free.items()}
            new, top, through = {}, 0.0, 0.0
            for i in mid:
                e = que[i]
                t = f[e]
                for j, lag in pr[i]:
                    x = new.get(j, end[j]) + lag
                    if x > t:
                        t = x
                if issue[i] >= 0:
                    f[e] = t + issue[i]
                    e = 6
                    t = max(t + pre[i], f[6])
                new[i] = f[e] = t + du[i]
                x = st[i] + up[i]
                if x > through:
                    through = x
            for i in mid:
                t = ta[i]
                for j, lag in sc[i]:
                    if j not in new and up[j] + lag > t:
                        t = up[j] + lag
                if new[i] + t > top:
                    top = new[i] + t
            for e, k in nxt.items():
                top = max(top, f[e] + (dn if e == 6 else up)[k])
            low += (top if through > was - 1e-6 or top > was else was) - was
            if low > room + 100.0:
                break
        return low, free, nxt

    def repeat():
        links()
        times(0, n - 1, 0, n)
        st = tm[0][0]
        tags, count = {}, {}
        for o in ops:
            k = (o["t"], o["e"], o["W"][0][0].rstrip("01").replace("XB", "XA")[:2] if o["W"] else "")
            count[k] = count.get(k, 0) + 1
            tags[o["id"]] = k[1:] + (count[k],)
        was = [min(st[o["id"]] for o in ops if o["t"] == t and o["W"] and o["W"][0][0] == "xv") for t in range(RO)]
        period = was[2] - was[1]
        rel = {tags[o["id"]]: st[o["id"]] - was[1] for o in ops if o["t"] == 1}
        rel.update({tags[o["id"]]: st[o["id"]] - was[1] + period for o in ops if o["t"] == 0 and st[o["id"]] >= was[1]})
        new = [was[1] + period * (t - 1) for t in range(RO)]
        key = [st[i] if st[i] < was[2] and o["t"] < 2 else new[max(1, o["t"])] + rel.get(tags[i], st[i] - was[max(1, o["t"])]) for i, o in enumerate(ops)]
        seq[:] = topo_by(key, pred, succ[0])

    best = (1e18, seq[:])
    plan = [(sweep, part) for part in STAGES for sweep in range(part[3])]
    for sweep, (lo, hi, share, sweeps, hot) in plan:
        if sweep == 0:
            seq[:] = best[1]
            if (lo, hi) == (0, 1) and len(STAGES) > 1:
                repeat()
                best = (1e18, seq[:])
        starts = [x for x in range(0, n - SPAN // 2, SPAN // 2) if lo * n <= x <= hi * n]
        each = int(MOVES * share) // (sweeps * len(starts))
        heat = hot * (1.0 - sweep / (sweeps - 1.0)) ** 1.5
        links()
        times(0, n - 1, 0, n)
        seq.sort(key=lambda i: tm[0][0][i] + max(0.0, min(pre[i], issue[i])))
        links()
        times(0, n - 1, 0, n)
        for r0 in starts:
            r1 = min(n, r0 + SPAN)
            times(max(0, r0 - SPAN), r1 - 1, r0, min(n, r1 + SPAN))
            rest = passing(r0, r1)
            tot = total(r0, r1, rest)
            now = sum(tot) / len(sets)
            crit = []
            for it in range(each):
                if not crit:
                    k = int(len(sets) * rnd())
                    crit = critical(k, r0, r1, tot[k] - NEAR * rnd() - 1e-6)
                    if not crit:
                        break
                u, v = crit[int(len(crit) * rnd())]
                back, step = (bd, ad) if bq[v] != u else (bq, aq)
                if rnd() < 0.5:
                    for _ in range(int(REACH * rnd() ** 2)):
                        if back[u] < n and pos[back[u]] >= r0:
                            u = back[u]
                    old = seq[pos[u]:pos[v] + 1]
                    need = {v}
                    for i in reversed(old):
                        if i in need:
                            need.update(before[i])
                    mid = [i for i in old if i in need] + [i for i in old if i not in need]
                else:
                    for _ in range(int(REACH * rnd() ** 2)):
                        if step[v] < n and pos[step[v]] < r1:
                            v = step[v]
                    old = seq[pos[u]:pos[v] + 1]
                    need = {u}
                    for i in old:
                        if i in need:
                            need.update(after[i])
                    mid = [i for i in old if i not in need] + [i for i in old if i in need]
                if mid == old:
                    continue
                bar = now - heat * math.log(1.0 - rnd())
                room = (bar - now) * len(sets)
                low, free, nxt = price(old, mid, tot, room)
                if low > room:
                    continue
                pu, pv = pos[u], pos[v]
                relink(pu, mid, free, nxt)
                times(pu, pv, r0, r1)
                got = total(r0, r1, rest)
                c = sum(got) / len(sets)
                if c <= bar:
                    now, tot, crit = c, got, []
                    if c < best[0]:
                        best = (c, seq[:])
                else:
                    relink(pu, old, free, nxt)
                    times(pu, pv, r0, r1)
    return [ops[i] for i in best[1]]


def rank_program(g, core, T, topo):
    rank = T.rank_of(core)
    if rank is None:
        return
    ops = build(g, T, rank, core, topo)
    depend(ops)
    if not ORDER:
        ORDER.extend(o["id"] for o in schedule(ops))
    order = [ops[i] for i in ORDER]
    Q = {"v": g.vector, "s": g.scalar, "p": g.tensor, "g": g, "y": g.sync}
    cnt = {"v": 0, "s": 0, "p": 0, "g": 0}
    need = set(j for o in ops for j, w in o["d"].items() if w)
    had = {e: {} for e in Q}
    top = {}
    for o in order:
        e = o["e"]
        if e == "x":
            o["sig"] = (o["sem"], o["cnt"])
            top[o["sem"]] = o["cnt"]
            continue
        want = {}
        for j, w in o["d"].items():
            if w:
                s, c = ops[j]["sig"]
                want[s] = max(want.get(s, 0), c)
        for s, c in want.items():
            if had[e].get(s, 0) < c:
                Q[e].wait_ge(T.sem[s], c)
                had[e][s] = c
        ins = o["fn"]()
        if o.get("remote"):
            o["sig"] = (o["sem"], o["cnt"])
        elif "sem" in o:
            ins.then_inc(T.sem[o["sem"]], 16)
            o["sig"] = (o["sem"], 16)
        elif o["id"] in need:
            cnt[e] += 1
            ins.then_inc(T.sem[e], 1)
            o["sig"] = (e, cnt[e])
        else:
            continue
        top[o["sig"][0]] = o["sig"][1]
    for s, c in top.items():
        if had["y"].get(s, 0) < c:
            g.sync.wait_ge(T.sem[s], c)
